import numpy as np
import ml_dtypes


def mxq(x, axis, fmt="e4m3"):
    dtype, down = {"e4m3": (ml_dtypes.float8_e4m3fn, 7), "e5m2": (ml_dtypes.float8_e5m2, 14)}[fmt]
    v = np.moveaxis(np.asarray(x, np.float32).astype(ml_dtypes.bfloat16).astype(np.float64), axis, -1)
    blocks = v.reshape(v.shape[:-1] + (-1, 32))
    amax = np.abs(blocks).max(-1, keepdims=True)
    byte = np.maximum(np.where(amax > 0, np.frexp(amax)[1] - 1 + 127, 0) - down, 1)
    scale = np.exp2(byte - 127.0)
    codes = (blocks / scale).astype(np.float32).astype(dtype).astype(np.float64)
    return np.moveaxis((codes * scale).reshape(v.shape), -1, axis)


WIDE = False


def mx_kscale(k):
    if not WIDE:
        return np.ones(k)
    levels = np.array([10, -10, 5, -5, 0])
    if k % 512:
        return np.exp2(np.random.permutation(np.resize(levels, k // 32))).repeat(32)
    a = np.empty((k // 512, 16))
    for p in range(k // 512):
        a[p, :8] = np.random.permutation(np.resize(levels, 8))
        for g in range(8):
            far = levels[np.abs(levels - a[p, g]) >= 10]
            a[p, g + 8] = far[np.random.randint(len(far))]
    return np.exp2(a.ravel()).repeat(32)


def f64(x):
    return np.asarray(x).astype(np.float64)


def striped(idx):
    return np.tile(np.asarray(idx).reshape(-1, 16).T, (8, 1)).astype(np.uint16)


def unstriped(offs):
    return offs[:16].T.reshape(-1).astype(np.int64)


G, K, T, D, M = 512, 4, 2048, 512, 256


def setup_inputs():
    n = np.random.standard_normal
    s = mx_kscale(D)[:, None]
    grid = lambda x: np.round(x * 32) / 32
    x = grid(n((D, T))) * s
    idx = np.random.randint(0, T, (G, K))
    return {
        "xT": x.astype(np.float32),
        "w": (n((D, M)) / np.sqrt(D * K) / s).astype(np.float32),
        "offs": striped(idx.reshape(-1)),
    }


def reference(xT, w, offs):
    x = f64(xT)[:, unstriped(offs)]
    y = mxq(f64(w), 0, "e4m3").T @ mxq(x.reshape(D, G, K).sum(-1), 0, "e4m3")
    return y

@@ -1,0 +1,150 @@
+from contextlib import ExitStack
+
+import concourse.mybir as mybir
+
+D, T, G, K, M = 512, 2048, 512, 4, 256
+P = 128
+FLOPS = 2 * D * G * M
+
+F32 = mybir.dt.float32
+BF16 = mybir.dt.bfloat16
+U32 = mybir.dt.uint32
+U16 = mybir.dt.uint16
+U8 = mybir.dt.uint8
+FP8X4 = mybir.dt.float8_e4m3fn_x4
+ADD = mybir.AluOpType.add
+COPY = mybir.ActivationFunctionType.Copy
+
+FIRST_LOADS = (1024, 512, 512)
+FIRST_CASTS = (("scalar", 0, 512), ("vector", 512, 1024), ("vector", 1024, 1536), ("scalar", 1536, 1696), ("vector", 1696, 2048))
+SECOND_LOADS = (512, 512, 384, 384, 256)
+
+
+def tile_attend_bag_kernel(tc, xT, w, offs, out):
+    nc = tc.nc
+    x_rows = xT.rearrange("(p t) c -> p t c", t=4)
+    w_rows = w.rearrange("(p t) m -> p t m", t=4)
+    out_rows = out.rearrange("(m p) g -> p m g", m=2)
+    with ExitStack() as ctx:
+        keep = ctx.enter_context(tc.tile_pool(name="keep", bufs=1))
+        psum = ctx.enter_context(tc.psum_pool(name="psum", bufs=1))
+
+        offsets = keep.tile([P, G * K // 16], U16, name="offsets")
+        pairs = [keep.tile([P, 2 * T], BF16, name=f"pair{h}") for h in range(2)]
+
+        first = keep.tile([P, 2, T], F32, name="first")
+        nc.sync.dma_start(first[:, 0, :], x_rows[:, 0, :])
+        c = 0
+        for cols in FIRST_LOADS:
+            nc.sync.dma_start(first[:, 1, c : c + cols], x_rows[:, 1, c : c + cols])
+            c += cols
+        nc.sync.dma_start(offsets[:], offs)
+        second = []
+        c = 0
+        for cols in SECOND_LOADS:
+            raw = keep.tile([P, 2, cols], F32, name=f"second{c}")
+            nc.sync.dma_start(raw[:], x_rows[:, 2:4, c : c + cols])
+            second.append((raw, c, cols))
+            c += cols
+        w_raw = keep.tile([P, 4, M], F32, name="w_raw")
+        nc.sync.dma_start(w_raw[:], w_rows)
+
+        warm = keep.tile([P, 1], F32, name="warm")
+        warmed = keep.tile([P, 1], F32, name="warmed")
+        nc.vector.memset(warm[:], 0.0)
+        nc.scalar.activation(warmed[:], warm[:], COPY)
+
+        sums = keep.tile([P, 2, G, 4], F32, name="sums")
+        e_bf = keep.tile([P, G * 4], BF16, name="e_bf", align_bytes=64)
+        codes = keep.tile([P, G], U32, name="codes", align_bytes=64)
+        scales = keep.tile([P, G], U8, name="scales", align_bytes=64)
+        got = {}
+
+        def gather(h, g0, bags):
+            a = g0 * K // 16
+            b = a + bags * K // 16
+            g = keep.tile([P, bags * K], U32, name=f"got{h}_{g0}")
+            nc.vector.tensor_copy(g[:], pairs[h][:].bitcast(U32).indirect(offsets[:, a:b]))
+            got[h, g0] = g
+
+        def level1(engine, h, g0, bags):
+            v = got[h, g0][:].bitcast(BF16).rearrange("p (g e) -> p g e", e=8)
+            engine.tensor_tensor(sums[:, h, g0 : g0 + bags, :], v[:, :, 0:4], v[:, :, 4:8], ADD)
+
+        def level2(g0, bags):
+            s = sums[:, :, g0 : g0 + bags, :].rearrange("p h g e -> p g h e")
+            nc.vector.tensor_tensor(
+                e_bf[:, 4 * g0 : 4 * (g0 + bags)].rearrange("p (g h t) -> p g h t", h=2, t=2),
+                s[:, :, :, 0:2],
+                s[:, :, :, 2:4],
+                ADD,
+            )
+
+        w_bf = keep.tile([P, M * 4], BF16, name="w_bf", align_bytes=64)
+        w_codes = keep.tile([P, M], U32, name="w_codes", align_bytes=64)
+        w_scales = keep.tile([P, M], U8, name="w_scales", align_bytes=64)
+
+        def quantise_w():
+            nc.vector.quantize_mx(w_codes[:].bitcast(FP8X4), w_scales[:], w_bf[:])
+
+        def product(g0, bags, last=False):
+            g = slice(g0, g0 + bags)
+            nc.vector.quantize_mx(codes[:, g].bitcast(FP8X4), scales[:, g], e_bf[:, 4 * g0 : 4 * (g0 + bags)])
+            res = keep.tile([P, 2, bags], F32, name=f"res{g0}")
+            if last:
+                accs = []
+                for m in range(2):
+                    acc = psum.tile([P, bags], F32, name=f"acc{g0}_{m}")
+                    accs.append(acc[:])
+            else:
+                both = psum.tile([P, 2, bags], F32, name=f"acc{g0}")
+                accs = [both[:, 0, :], both[:, 1, :]]
+            for m in range(2):
+                cols = slice(m * P, (m + 1) * P)
+                nc.tensor.matmul_mx(
+                    accs[m],
+                    lhsT=w_codes[:, cols].bitcast(FP8X4),
+                    lhsT_scale=w_scales[:, cols],
+                    rhs=codes[:, g].bitcast(FP8X4),
+                    rhs_scale=scales[:, g],
+                    start=True,
+                    stop=True,
+                )
+            if last:
+                res1 = keep.tile([P, bags], F32, name=f"res1_{g0}")
+                nc.scalar.activation(res[:, 0, :], accs[0], COPY)
+                nc.vector.tensor_copy(res1[:], accs[1])
+                nc.scalar.dma_start(out[0:P, g], res[:, 0, :])
+                nc.sync.dma_start(out[P : 2 * P, g], res1[:])
+            else:
+                nc.scalar.activation(res[:], both[:], COPY)
+                nc.sync.dma_start(out_rows[:, :, g], res[:])
+
+        wide = [pair[:].rearrange("p (c t) -> p c t", t=2) for pair in pairs]
+        for engine, c0, c1 in FIRST_CASTS:
+            source = first[:, :, c0:c1].rearrange("p t c -> p c t")
+            if engine == "scalar":
+                nc.scalar.activation(wide[0][:, c0:c1, :], source, COPY)
+            else:
+                nc.vector.tensor_copy(wide[0][:, c0:c1, :], source)
+        for raw, c, cols in second:
+            nc.scalar.activation(wide[1][:, c : c + cols, :], raw[:].rearrange("p t c -> p c t"), COPY)
+        nc.scalar.activation(w_bf[:].rearrange("p (m t) -> p m t", t=4), w_raw[:].rearrange("p t m -> p m t"), COPY)
+        for g0, bags in ((0, 128), (128, 128), (256, 256)):
+            gather(0, g0, bags)
+            level1(nc.gpsimd, 0, g0, bags)
+        for g0 in range(0, G, 128):
+            gather(1, g0, 128)
+            if g0 < 256:
+                level1(nc.gpsimd, 1, g0, 128)
+        quantise_w()
+        level1(nc.vector, 1, 256, 128)
+        level2(0, 128)
+        level1(nc.vector, 1, 384, 128)
+        product(0, 128)
+        level2(128, 128)
+        level2(256, 128)
+        product(128, 128)
+        level2(384, 128)
+        product(256, 128)
+        product(384, 128, last=True)

@@ -1,6 +1,7 @@
 from contextlib import ExitStack
 
 import concourse.mybir as mybir
+from concourse.masks import make_identity
 
 D, T, G, K, M = 512, 2048, 512, 4, 256
 P = 128
@@ -16,8 +17,9 @@ ADD = mybir.AluOpType.add
 COPY = mybir.ActivationFunctionType.Copy
 
 FIRST_LOADS = (1024, 512, 512)
-FIRST_CASTS = (("scalar", 0, 512), ("vector", 512, 1024), ("vector", 1024, 1536), ("scalar", 1536, 1696), ("vector", 1696, 2048))
-SECOND_LOADS = (512, 512, 384, 384, 256)
+SECOND_LOADS = (1024, 512, 256, 256)
+B = 128
+SPLIT = 256
 
 
 def tile_attend_bag_kernel(tc, xT, w, offs, out):
@@ -30,22 +32,18 @@ def tile_attend_bag_kernel(tc, xT, w, offs, out):
         psum = ctx.enter_context(tc.psum_pool(name="psum", bufs=1))
 
         offsets = keep.tile([P, G * K // 16], U16, name="offsets")
-        pairs = [keep.tile([P, 2 * T], BF16, name=f"pair{h}") for h in range(2)]
-
-        first = keep.tile([P, 2, T], F32, name="first")
-        nc.sync.dma_start(first[:, 0, :], x_rows[:, 0, :])
-        c = 0
-        for cols in FIRST_LOADS:
-            nc.sync.dma_start(first[:, 1, c : c + cols], x_rows[:, 1, c : c + cols])
-            c += cols
-        nc.sync.dma_start(offsets[:], offs)
-        second = []
-        c = 0
-        for cols in SECOND_LOADS:
-            raw = keep.tile([P, 2, cols], F32, name=f"second{c}")
-            nc.sync.dma_start(raw[:], x_rows[:, 2:4, c : c + cols])
-            second.append((raw, c, cols))
-            c += cols
+        pairs = [keep.tile([P, T], F32, name=f"pair{h}") for h in range(2)]
+        pieces = [[], []]
+        for h, loads in enumerate((FIRST_LOADS, SECOND_LOADS)):
+            c = 0
+            for cols in loads:
+                low = keep.tile([P, cols], F32, name=f"low{h}_{c}", tag=f"low{h}_{c}")
+                nc.sync.dma_start(low[:], x_rows[:, 2 * h, c : c + cols])
+                nc.sync.dma_start(pairs[h][:, c : c + cols], x_rows[:, 2 * h + 1, c : c + cols])
+                pieces[h].append((low, c, cols))
+                c += cols
+            if h == 0:
+                nc.sync.dma_start(offsets[:], offs)
         w_raw = keep.tile([P, 4, M], F32, name="w_raw")
         nc.sync.dma_start(w_raw[:], w_rows)
 
@@ -53,28 +51,61 @@ def tile_attend_bag_kernel(tc, xT, w, offs, out):
         warmed = keep.tile([P, 1], F32, name="warmed")
         nc.vector.memset(warm[:], 0.0)
         nc.scalar.activation(warmed[:], warm[:], COPY)
+        ident = keep.tile([P, P], F32, name="ident")
+        make_identity(nc, ident[:])
 
-        sums = keep.tile([P, 2, G, 4], F32, name="sums")
         e_bf = keep.tile([P, G * 4], BF16, name="e_bf", align_bytes=64)
         codes = keep.tile([P, G], U32, name="codes", align_bytes=64)
         scales = keep.tile([P, G], U8, name="scales", align_bytes=64)
+        last_sums = keep.tile([P, 2, G, 4], F32, name="last_sums")
         got = {}
+        halves = {}
+        turned = {}
 
-        def gather(h, g0, bags):
+        def gather(h, g0):
             a = g0 * K // 16
-            b = a + bags * K // 16
-            g = keep.tile([P, bags * K], U32, name=f"got{h}_{g0}")
-            nc.vector.tensor_copy(g[:], pairs[h][:].bitcast(U32).indirect(offsets[:, a:b]))
+            g = keep.tile([P, B * K], U32, name=f"got{h}_{g0}")
+            nc.vector.tensor_copy(g[:], pairs[h][:].bitcast(U32).indirect(offsets[:, a : a + B * K // 16]))
             got[h, g0] = g
 
-        def level1(engine, h, g0, bags):
-            v = got[h, g0][:].bitcast(BF16).rearrange("p (g e) -> p g e", e=8)
-            engine.tensor_tensor(sums[:, h, g0 : g0 + bags, :], v[:, :, 0:4], v[:, :, 4:8], ADD)
+        def level1_for_tensor(h, g0):
+            v = got[h, g0][:].bitcast(BF16).rearrange("p (g s j t) -> p g s j t", s=2, j=2, t=2)
+            half = keep.tile([P, 2, B, 2], F32, name=f"half{h}_{g0}")
+            nc.gpsimd.tensor_tensor(half[:].rearrange("p j g t -> p g j t"), v[:, :, 0], v[:, :, 1], ADD)
+            halves[h, g0] = lambda j, t: half[:, j, :, t]
 
-        def level2(g0, bags):
-            s = sums[:, :, g0 : g0 + bags, :].rearrange("p h g e -> p g h e")
+        def level2_on_tensor(h, g0):
+            bank = psum.tile([P, 2, P], F32, name="fwd", tag="fwd", bufs=3)
+            for t in range(2):
+                for j in range(2):
+                    nc.tensor.matmul(
+                        bank[:, t, :], lhsT=halves[h, g0](j, t), rhs=ident[:], is_transpose=True, start=j == 0, stop=j == 1
+                    )
+            if h == 0:
+                turned[h, g0] = first_turned[:, g0 : g0 + P]
+            else:
+                turned[h, g0] = keep.tile([P, P], F32, name=f"turned{g0}")[:]
+            nc.scalar.activation(
+                turned[h, g0].bitcast(BF16).rearrange("g (p t) -> g p t", t=2), bank[:].rearrange("g t p -> g p t"), COPY
+            )
+
+        def turn_back(g0):
+            bank = psum.tile([P, 2, B], F32, name="back", tag="back", bufs=2)
+            for h in range(2):
+                nc.tensor.transpose(bank[:, h, :], turned[h, g0], ident[:])
+            nc.scalar.copy(
+                e_bf[:, 4 * g0 : 4 * (g0 + B)].bitcast(F32).rearrange("p (g h) -> p g h", h=2),
+                bank[:].rearrange("p h g -> p g h"),
+            )
+
+        def level1(engine, h, g0):
+            v = got[h, g0][:].bitcast(BF16).rearrange("p (g e) -> p g e", e=8)
+            engine.tensor_tensor(last_sums[:, h, g0 : g0 + B], v[:, :, 0:4], v[:, :, 4:8], ADD)
+
+        def level2(g0):
+            s = last_sums[:, :, g0 : g0 + B].rearrange("p h g e -> p g h e")
             nc.vector.tensor_tensor(
-                e_bf[:, 4 * g0 : 4 * (g0 + bags)].rearrange("p (g h t) -> p g h t", h=2, t=2),
+                e_bf[:, 4 * g0 : 4 * (g0 + B)].rearrange("p (g h t) -> p g h t", h=2, t=2),
                 s[:, :, :, 0:2],
                 s[:, :, :, 2:4],
                 ADD,
@@ -84,20 +115,17 @@ def tile_attend_bag_kernel(tc, xT, w, offs, out):
         w_codes = keep.tile([P, M], U32, name="w_codes", align_bytes=64)
         w_scales = keep.tile([P, M], U8, name="w_scales", align_bytes=64)
 
-        def quantise_w():
-            nc.vector.quantize_mx(w_codes[:].bitcast(FP8X4), w_scales[:], w_bf[:])
-
-        def product(g0, bags, last=False):
-            g = slice(g0, g0 + bags)
-            nc.vector.quantize_mx(codes[:, g].bitcast(FP8X4), scales[:, g], e_bf[:, 4 * g0 : 4 * (g0 + bags)])
-            res = keep.tile([P, 2, bags], F32, name=f"res{g0}")
+        def product(g0, last=False):
+            g = slice(g0, g0 + B)
+            nc.vector.quantize_mx(codes[:, g].bitcast(FP8X4), scales[:, g], e_bf[:, 4 * g0 : 4 * (g0 + B)])
+            res = keep.tile([P, 2, B], F32, name=f"res{g0}")
             if last:
                 accs = []
                 for m in range(2):
-                    acc = psum.tile([P, bags], F32, name=f"acc{g0}_{m}")
+                    acc = psum.tile([P, B], F32, name="acc", tag="acc", bufs=3)
                     accs.append(acc[:])
             else:
-                both = psum.tile([P, 2, bags], F32, name=f"acc{g0}")
+                both = psum.tile([P, 2, B], F32, name="acc", tag="acc", bufs=3)
                 accs = [both[:, 0, :], both[:, 1, :]]
             for m in range(2):
                 cols = slice(m * P, (m + 1) * P)
@@ -111,7 +139,7 @@ def tile_attend_bag_kernel(tc, xT, w, offs, out):
                     stop=True,
                 )
             if last:
-                res1 = keep.tile([P, bags], F32, name=f"res1_{g0}")
+                res1 = keep.tile([P, B], F32, name=f"res1_{g0}")
                 nc.scalar.activation(res[:, 0, :], accs[0], COPY)
                 nc.vector.tensor_copy(res1[:], accs[1])
                 nc.scalar.dma_start(out[0:P, g], res[:, 0, :])
@@ -120,31 +148,32 @@ def tile_attend_bag_kernel(tc, xT, w, offs, out):
                 nc.scalar.activation(res[:], both[:], COPY)
                 nc.sync.dma_start(out_rows[:, :, g], res[:])
 
-        wide = [pair[:].rearrange("p (c t) -> p c t", t=2) for pair in pairs]
-        for engine, c0, c1 in FIRST_CASTS:
-            source = first[:, :, c0:c1].rearrange("p t c -> p c t")
-            if engine == "scalar":
-                nc.scalar.activation(wide[0][:, c0:c1, :], source, COPY)
-            else:
-                nc.vector.tensor_copy(wide[0][:, c0:c1, :], source)
-        for raw, c, cols in second:
-            nc.scalar.activation(wide[1][:, c : c + cols, :], raw[:].rearrange("p t c -> p c t"), COPY)
-        nc.scalar.activation(w_bf[:].rearrange("p (m t) -> p m t", t=4), w_raw[:].rearrange("p t m -> p m t"), COPY)
-        for g0, bags in ((0, 128), (128, 128), (256, 256)):
-            gather(0, g0, bags)
-            level1(nc.gpsimd, 0, g0, bags)
-        for g0 in range(0, G, 128):
-            gather(1, g0, 128)
-            if g0 < 256:
-                level1(nc.gpsimd, 1, g0, 128)
-        quantise_w()
-        level1(nc.vector, 1, 256, 128)
-        level2(0, 128)
-        level1(nc.vector, 1, 384, 128)
-        product(0, 128)
-        level2(128, 128)
-        level2(256, 128)
-        product(128, 128)
-        level2(384, 128)
-        product(256, 128)
-        product(384, 128, last=True)
+        wide = [pair[:].bitcast(BF16).rearrange("p (c t) -> p c t", t=2) for pair in pairs]
+        for low, c, cols in pieces[0]:
+            nc.vector.tensor_copy(wide[0][:, c : c + cols, 0], low[:])
+        for low, c, cols in pieces[1]:
+            nc.scalar.activation(wide[1][:, c : c + cols, 0], low[:], COPY)
+        first_turned = keep.tile([P, SPLIT], F32, name="first_turned", tag=f"low1_{T - SECOND_LOADS[-1]}")
+        for h in range(2):
+            for g0 in range(0, G, B):
+                gather(h, g0)
+                if g0 < SPLIT:
+                    level1_for_tensor(h, g0)
+                    level2_on_tensor(h, g0)
+                    if h == 1:
+                        turn_back(g0)
+                elif h == 0:
+                    level1(nc.gpsimd, 0, g0)
+            if h == 0:
+                nc.scalar.activation(
+                    w_bf[:].rearrange("p (m t) -> p m t", t=4), w_raw[:].rearrange("p t m -> p m t"), COPY
+                )
+        nc.vector.quantize_mx(w_codes[:].bitcast(FP8X4), w_scales[:], w_bf[:])
+        level1(nc.vector, 1, 2 * B)
+        product(0)
+        level1(nc.vector, 1, 3 * B)
+        level2(2 * B)
+        level2(3 * B)
+        product(2 * B)
+        product(B)
+        product(3 * B, last=True)

@@ -16,8 +16,8 @@ FP8X4 = mybir.dt.float8_e4m3fn_x4
 ADD = mybir.AluOpType.add
 COPY = mybir.ActivationFunctionType.Copy
 
-FIRST_LOADS = (1024, 512, 512)
-SECOND_LOADS = (1024, 512, 256, 256)
+FIRST_LOADS = (1024, 512, 256, 256)
+SECOND_LOADS = (512, 512, 512, 256, 256)
 B = 128
 SPLIT = 256
 
@@ -54,9 +54,7 @@ def tile_attend_bag_kernel(tc, xT, w, offs, out):
         ident = keep.tile([P, P], F32, name="ident")
         make_identity(nc, ident[:])
 
-        e_bf = keep.tile([P, G * 4], BF16, name="e_bf", align_bytes=64)
-        codes = keep.tile([P, G], U32, name="codes", align_bytes=64)
-        scales = keep.tile([P, G], U8, name="scales", align_bytes=64)
+        e_bf = {}
         last_sums = keep.tile([P, 2, G, 4], F32, name="last_sums")
         got = {}
         halves = {}
@@ -84,17 +82,18 @@ def tile_attend_bag_kernel(tc, xT, w, offs, out):
             if h == 0:
                 turned[h, g0] = first_turned[:, g0 : g0 + P]
             else:
-                turned[h, g0] = keep.tile([P, P], F32, name=f"turned{g0}")[:]
+                turned[h, g0] = keep.tile([P, P], F32, name=f"turned{g0}", tag=f"turned{g0}")[:]
             nc.scalar.activation(
                 turned[h, g0].bitcast(BF16).rearrange("g (p t) -> g p t", t=2), bank[:].rearrange("g t p -> g p t"), COPY
             )
 
         def turn_back(g0):
-            bank = psum.tile([P, 2, B], F32, name="back", tag="back", bufs=2)
+            bank = psum.tile([P, 2, B], F32, name="back", tag=f"back{g0}")
+            e_bf[g0] = keep.tile([P, 4 * B], BF16, name=f"e{g0}", tag=f"e{g0}", align_bytes=64)
             for h in range(2):
                 nc.tensor.transpose(bank[:, h, :], turned[h, g0], ident[:])
             nc.scalar.copy(
-                e_bf[:, 4 * g0 : 4 * (g0 + B)].bitcast(F32).rearrange("p (g h) -> p g h", h=2),
+                e_bf[g0][:].bitcast(F32).rearrange("p (g h) -> p g h", h=2),
                 bank[:].rearrange("p h g -> p g h"),
             )
 
@@ -102,10 +101,11 @@ def tile_attend_bag_kernel(tc, xT, w, offs, out):
             v = got[h, g0][:].bitcast(BF16).rearrange("p (g e) -> p g e", e=8)
             engine.tensor_tensor(last_sums[:, h, g0 : g0 + B], v[:, :, 0:4], v[:, :, 4:8], ADD)
 
-        def level2(g0):
+        def level2(g0, tag):
+            e_bf[g0] = keep.tile([P, 4 * B], BF16, name=f"e{g0}", tag=tag, align_bytes=64)
             s = last_sums[:, :, g0 : g0 + B].rearrange("p h g e -> p g h e")
             nc.vector.tensor_tensor(
-                e_bf[:, 4 * g0 : 4 * (g0 + B)].rearrange("p (g h t) -> p g h t", h=2, t=2),
+                e_bf[g0][:].rearrange("p (g h t) -> p g h t", h=2, t=2),
                 s[:, :, :, 0:2],
                 s[:, :, :, 2:4],
                 ADD,
@@ -115,17 +115,20 @@ def tile_attend_bag_kernel(tc, xT, w, offs, out):
         w_codes = keep.tile([P, M], U32, name="w_codes", align_bytes=64)
         w_scales = keep.tile([P, M], U8, name="w_scales", align_bytes=64)
 
-        def product(g0, last=False):
+        def product(g0, codes_tag, bank_tags, res_tag):
+            last = len(bank_tags) == 2
             g = slice(g0, g0 + B)
-            nc.vector.quantize_mx(codes[:, g].bitcast(FP8X4), scales[:, g], e_bf[:, 4 * g0 : 4 * (g0 + B)])
-            res = keep.tile([P, 2, B], F32, name=f"res{g0}")
+            codes = keep.tile([P, B], U32, name=f"codes{g0}", tag=codes_tag, align_bytes=64)
+            scales = keep.tile([P, B], U8, name=f"scales{g0}", align_bytes=64)
+            nc.vector.quantize_mx(codes[:].bitcast(FP8X4), scales[:], e_bf[g0][:])
+            res = keep.tile([P, 2, B], F32, name=f"res{g0}", tag=res_tag)
             if last:
                 accs = []
                 for m in range(2):
-                    acc = psum.tile([P, B], F32, name="acc", tag="acc", bufs=3)
+                    acc = psum.tile([P, B], F32, name="acc", tag=bank_tags[m])
                     accs.append(acc[:])
             else:
-                both = psum.tile([P, 2, B], F32, name="acc", tag="acc", bufs=3)
+                both = psum.tile([P, 2, B], F32, name="acc", tag=bank_tags[0])
                 accs = [both[:, 0, :], both[:, 1, :]]
             for m in range(2):
                 cols = slice(m * P, (m + 1) * P)
@@ -133,8 +136,8 @@ def tile_attend_bag_kernel(tc, xT, w, offs, out):
                     accs[m],
                     lhsT=w_codes[:, cols].bitcast(FP8X4),
                     lhsT_scale=w_scales[:, cols],
-                    rhs=codes[:, g].bitcast(FP8X4),
-                    rhs_scale=scales[:, g],
+                    rhs=codes[:].bitcast(FP8X4),
+                    rhs_scale=scales[:],
                     start=True,
                     stop=True,
                 )
@@ -168,12 +171,12 @@ def tile_attend_bag_kernel(tc, xT, w, offs, out):
                 nc.scalar.activation(
                     w_bf[:].rearrange("p (m t) -> p m t", t=4), w_raw[:].rearrange("p t m -> p m t"), COPY
                 )
-        nc.vector.quantize_mx(w_codes[:].bitcast(FP8X4), w_scales[:], w_bf[:])
         level1(nc.vector, 1, 2 * B)
-        product(0)
         level1(nc.vector, 1, 3 * B)
-        level2(2 * B)
-        level2(3 * B)
-        product(2 * B)
-        product(B)
-        product(3 * B, last=True)
+        nc.vector.quantize_mx(w_codes[:].bitcast(FP8X4), w_scales[:], w_bf[:])
+        level2(2 * B, "e256")
+        product(0, "codes0", ["acc0"], "turned128")
+        level2(3 * B, "e0")
+        product(2 * B, "codes256", ["back128"], "res256")
+        product(B, "codes128", ["acc128"], "res128")
+        product(3 * B, "e128", ["back0", "acc384"], "res384")

@@ -16,8 +16,8 @@ FP8X4 = mybir.dt.float8_e4m3fn_x4
 ADD = mybir.AluOpType.add
 COPY = mybir.ActivationFunctionType.Copy
 
-FIRST_LOADS = (1024, 512, 256, 256)
-SECOND_LOADS = (512, 512, 512, 256, 256)
+LOADS = ((0, 0, 2048), (1, 0, 1024), (1, 1024, 1536), (1, 1536, 2048), (2, 0, 512), (3, 0, 512), (2, 512, 1024), (3, 512, 1024), (2, 1024, 1536), (3, 1024, 1536), (2, 1536, 1792), (3, 1536, 1792), (2, 1792, 2048), (3, 1792, 2048))
+MERGES = (("vector", 0, 0, 1024), ("vector", 0, 1024, 1536), ("vector", 0, 1536, 1856), ("scalar", 0, 1856, 2048), ("scalar", 1, 0, 512), ("scalar", 1, 512, 1024), ("scalar", 1, 1024, 1536), ("scalar", 1, 1536, 1792), ("scalar", 1, 1792, 2048))
 B = 128
 SPLIT = 256
 
@@ -33,17 +33,17 @@ def tile_attend_bag_kernel(tc, xT, w, offs, out):
 
         offsets = keep.tile([P, G * K // 16], U16, name="offsets")
         pairs = [keep.tile([P, T], F32, name=f"pair{h}") for h in range(2)]
-        pieces = [[], []]
-        for h, loads in enumerate((FIRST_LOADS, SECOND_LOADS)):
-            c = 0
-            for cols in loads:
-                low = keep.tile([P, cols], F32, name=f"low{h}_{c}", tag=f"low{h}_{c}")
-                nc.sync.dma_start(low[:], x_rows[:, 2 * h, c : c + cols])
-                nc.sync.dma_start(pairs[h][:, c : c + cols], x_rows[:, 2 * h + 1, c : c + cols])
-                pieces[h].append((low, c, cols))
-                c += cols
-            if h == 0:
+        lows = {}
+        for t, c0, c1 in LOADS:
+            if t % 2 == 0:
+                low = keep.tile([P, c1 - c0], F32, name=f"low{t}_{c0}", tag=f"low{t}_{c0}")
+                nc.sync.dma_start(low[:], x_rows[:, t, c0:c1])
+                lows[t // 2, c0, c1] = low
+            else:
+                nc.sync.dma_start(pairs[t // 2][:, c0:c1], x_rows[:, t, c0:c1])
+            if t == 1 and c1 == T:
                 nc.sync.dma_start(offsets[:], offs)
+        last_low = max(c0 for t, c0, c1 in LOADS if t == 2)
         w_raw = keep.tile([P, 4, M], F32, name="w_raw")
         nc.sync.dma_start(w_raw[:], w_rows)
 
@@ -152,11 +152,13 @@ def tile_attend_bag_kernel(tc, xT, w, offs, out):
                 nc.sync.dma_start(out_rows[:, :, g], res[:])
 
         wide = [pair[:].bitcast(BF16).rearrange("p (c t) -> p c t", t=2) for pair in pairs]
-        for low, c, cols in pieces[0]:
-            nc.vector.tensor_copy(wide[0][:, c : c + cols, 0], low[:])
-        for low, c, cols in pieces[1]:
-            nc.scalar.activation(wide[1][:, c : c + cols, 0], low[:], COPY)
-        first_turned = keep.tile([P, SPLIT], F32, name="first_turned", tag=f"low1_{T - SECOND_LOADS[-1]}")
+        for engine, h, c0, c1 in MERGES:
+            low, l0 = [(tile, a) for (k, a, b), tile in lows.items() if k == h and a <= c0 and c1 <= b][0]
+            if engine == "vector":
+                nc.vector.tensor_copy(wide[h][:, c0:c1, 0], low[:, c0 - l0 : c1 - l0])
+            else:
+                nc.scalar.activation(wide[h][:, c0:c1, 0], low[:, c0 - l0 : c1 - l0], COPY)
+        first_turned = keep.tile([P, SPLIT], F32, name="first_turned", tag=f"low2_{last_low}")
         for h in range(2):
             for g0 in range(0, G, B):
                 gather(h, g0)

@@ -19,7 +19,6 @@ COPY = mybir.ActivationFunctionType.Copy
 LOADS = ((0, 0, 2048), (1, 0, 1024), (1, 1024, 1536), (1, 1536, 2048), (2, 0, 512), (3, 0, 512), (2, 512, 1024), (3, 512, 1024), (2, 1024, 1536), (3, 1024, 1536), (2, 1536, 1792), (3, 1536, 1792), (2, 1792, 2048), (3, 1792, 2048))
 MERGES = (("vector", 0, 0, 1024), ("vector", 0, 1024, 1536), ("vector", 0, 1536, 1856), ("scalar", 0, 1856, 2048), ("scalar", 1, 0, 512), ("scalar", 1, 512, 1024), ("scalar", 1, 1024, 1536), ("scalar", 1, 1536, 1792), ("scalar", 1, 1792, 2048))
 B = 128
-SPLIT = 256
 
 
 def tile_attend_bag_kernel(tc, xT, w, offs, out):
@@ -31,12 +30,15 @@ def tile_attend_bag_kernel(tc, xT, w, offs, out):
         keep = ctx.enter_context(tc.tile_pool(name="keep", bufs=1))
         psum = ctx.enter_context(tc.psum_pool(name="psum", bufs=1))
 
+        def sbuf(shape, dtype, name, tag=None):
+            return keep.tile(shape, dtype, name=name, tag=tag or name, align_bytes=64)
+
         offsets = keep.tile([P, G * K // 16], U16, name="offsets")
         pairs = [keep.tile([P, T], F32, name=f"pair{h}") for h in range(2)]
         lows = {}
         for t, c0, c1 in LOADS:
             if t % 2 == 0:
-                low = keep.tile([P, c1 - c0], F32, name=f"low{t}_{c0}", tag=f"low{t}_{c0}")
+                low = sbuf([P, c1 - c0], F32, f"low{t}_{c0}")
                 nc.sync.dma_start(low[:], x_rows[:, t, c0:c1])
                 lows[t // 2, c0, c1] = low
             else:
@@ -44,7 +46,7 @@ def tile_attend_bag_kernel(tc, xT, w, offs, out):
             if t == 1 and c1 == T:
                 nc.sync.dma_start(offsets[:], offs)
         last_low = max(c0 for t, c0, c1 in LOADS if t == 2)
-        w_raw = keep.tile([P, 4, M], F32, name="w_raw")
+        w_raw = sbuf([P, 4, M], F32, "w_raw")
         nc.sync.dma_start(w_raw[:], w_rows)
 
         warm = keep.tile([P, 1], F32, name="warm")
@@ -54,102 +56,86 @@ def tile_attend_bag_kernel(tc, xT, w, offs, out):
         ident = keep.tile([P, P], F32, name="ident")
         make_identity(nc, ident[:])
 
-        e_bf = {}
-        last_sums = keep.tile([P, 2, G, 4], F32, name="last_sums")
+        flat_sums = sbuf([P, 2 * 2 * B * 4], F32, "last_sums")
+        last_sums = flat_sums[:].rearrange("p (h g e) -> p h g e", h=2, e=4)
         got = {}
         halves = {}
         turned = {}
 
-        def gather(h, g0):
+        def gather(h, g0, bags=B, into=None):
             a = g0 * K // 16
-            g = keep.tile([P, B * K], U32, name=f"got{h}_{g0}")
-            nc.vector.tensor_copy(g[:], pairs[h][:].bitcast(U32).indirect(offsets[:, a : a + B * K // 16]))
-            got[h, g0] = g
+            g = sbuf([P, bags * K], U32, f"got{h}_{g0}") if into is None else into
+            nc.vector.tensor_copy(g[:], pairs[h][:].bitcast(U32).indirect(offsets[:, a : a + bags * K // 16]))
+            got[h, g0] = g[:]
 
-        def level1_for_tensor(h, g0):
-            v = got[h, g0][:].bitcast(BF16).rearrange("p (g s j t) -> p g s j t", s=2, j=2, t=2)
-            half = keep.tile([P, 2, B, 2], F32, name=f"half{h}_{g0}")
+        def level1(engine, h, g0, sums):
+            v = got[h, g0].bitcast(BF16).rearrange("p (g e) -> p g e", e=8)
+            engine.tensor_tensor(sums, v[:, :, 0:4], v[:, :, 4:8], ADD)
+
+        def level2_on_tensor(h, g0, into):
+            half = sbuf([P, 2, B, 2], F32, f"half{h}_{g0}")
+            v = got[h, g0].bitcast(BF16).rearrange("p (g s j t) -> p g s j t", s=2, j=2, t=2)
             nc.gpsimd.tensor_tensor(half[:].rearrange("p j g t -> p g j t"), v[:, :, 0], v[:, :, 1], ADD)
-            halves[h, g0] = lambda j, t: half[:, j, :, t]
-
-        def level2_on_tensor(h, g0):
-            bank = psum.tile([P, 2, P], F32, name="fwd", tag="fwd", bufs=3)
+            bank = psum.tile([P, 2, P], F32, name="fwd", tag=f"fwd{g0}")
             for t in range(2):
                 for j in range(2):
                     nc.tensor.matmul(
-                        bank[:, t, :], lhsT=halves[h, g0](j, t), rhs=ident[:], is_transpose=True, start=j == 0, stop=j == 1
+                        bank[:, t, :], lhsT=half[:, j, :, t], rhs=ident[:], is_transpose=True, start=j == 0, stop=j == 1
                     )
-            if h == 0:
-                turned[h, g0] = first_turned[:, g0 : g0 + P]
-            else:
-                turned[h, g0] = keep.tile([P, P], F32, name=f"turned{g0}", tag=f"turned{g0}")[:]
+            turned[h, g0] = into
             nc.scalar.activation(
-                turned[h, g0].bitcast(BF16).rearrange("g (p t) -> g p t", t=2), bank[:].rearrange("g t p -> g p t"), COPY
+                into.bitcast(BF16).rearrange("g (p t) -> g p t", t=2), bank[:].rearrange("g t p -> g p t"), COPY
             )
 
-        def turn_back(g0):
+        def turn_back(g0, e):
             bank = psum.tile([P, 2, B], F32, name="back", tag=f"back{g0}")
-            e_bf[g0] = keep.tile([P, 4 * B], BF16, name=f"e{g0}", tag=f"e{g0}", align_bytes=64)
             for h in range(2):
                 nc.tensor.transpose(bank[:, h, :], turned[h, g0], ident[:])
-            nc.scalar.copy(
-                e_bf[g0][:].bitcast(F32).rearrange("p (g h) -> p g h", h=2),
-                bank[:].rearrange("p h g -> p g h"),
+            nc.scalar.copy(e.bitcast(F32).rearrange("p (g h) -> p g h", h=2), bank[:].rearrange("p h g -> p g h"))
+
+        def level2(e, b0, b1):
+            s = last_sums[:, :, b0:b1].rearrange("p h g e -> p g h e")
+            nc.vector.tensor_tensor(e.rearrange("p (g h t) -> p g h t", h=2, t=2), s[:, :, :, 0:2], s[:, :, :, 2:4], ADD)
+
+        w_bf = sbuf([P, M * 4], BF16, "w_bf")
+        w_codes = sbuf([P, M], U32, "w_codes")
+        w_scales = sbuf([P, M], U8, "w_scales")
+
+        def quantise(g0, bags, e, tag=None):
+            codes = sbuf([P, bags], U32, f"codes{g0}", tag)
+            scales = sbuf([P, bags], U8, f"scales{g0}")
+            nc.vector.quantize_mx(codes[:].bitcast(FP8X4), scales[:], e)
+            return codes, scales
+
+        def multiply(acc, m, codes, scales):
+            cols = slice(m * P, (m + 1) * P)
+            nc.tensor.matmul_mx(
+                acc,
+                lhsT=w_codes[:, cols].bitcast(FP8X4),
+                lhsT_scale=w_scales[:, cols],
+                rhs=codes[:].bitcast(FP8X4),
+                rhs_scale=scales[:],
+                start=True,
+                stop=True,
             )
 
-        def level1(engine, h, g0):
-            v = got[h, g0][:].bitcast(BF16).rearrange("p (g e) -> p g e", e=8)
-            engine.tensor_tensor(last_sums[:, h, g0 : g0 + B], v[:, :, 0:4], v[:, :, 4:8], ADD)
-
-        def level2(g0, tag):
-            e_bf[g0] = keep.tile([P, 4 * B], BF16, name=f"e{g0}", tag=tag, align_bytes=64)
-            s = last_sums[:, :, g0 : g0 + B].rearrange("p h g e -> p g h e")
-            nc.vector.tensor_tensor(
-                e_bf[g0][:].rearrange("p (g h t) -> p g h t", h=2, t=2),
-                s[:, :, :, 0:2],
-                s[:, :, :, 2:4],
-                ADD,
-            )
-
-        w_bf = keep.tile([P, M * 4], BF16, name="w_bf", align_bytes=64)
-        w_codes = keep.tile([P, M], U32, name="w_codes", align_bytes=64)
-        w_scales = keep.tile([P, M], U8, name="w_scales", align_bytes=64)
-
-        def product(g0, codes_tag, bank_tags, res_tag):
-            last = len(bank_tags) == 2
-            g = slice(g0, g0 + B)
-            codes = keep.tile([P, B], U32, name=f"codes{g0}", tag=codes_tag, align_bytes=64)
-            scales = keep.tile([P, B], U8, name=f"scales{g0}", align_bytes=64)
-            nc.vector.quantize_mx(codes[:].bitcast(FP8X4), scales[:], e_bf[g0][:])
-            res = keep.tile([P, 2, B], F32, name=f"res{g0}", tag=res_tag)
-            if last:
-                accs = []
-                for m in range(2):
-                    acc = psum.tile([P, B], F32, name="acc", tag=bank_tags[m])
-                    accs.append(acc[:])
-            else:
-                both = psum.tile([P, 2, B], F32, name="acc", tag=bank_tags[0])
-                accs = [both[:, 0, :], both[:, 1, :]]
+        def product(g0, bags, quantised, bank_tag):
+            acc = psum.tile([P, 2, bags], F32, name="acc", tag=bank_tag)
             for m in range(2):
-                cols = slice(m * P, (m + 1) * P)
-                nc.tensor.matmul_mx(
-                    accs[m],
-                    lhsT=w_codes[:, cols].bitcast(FP8X4),
-                    lhsT_scale=w_scales[:, cols],
-                    rhs=codes[:].bitcast(FP8X4),
-                    rhs_scale=scales[:],
-                    start=True,
-                    stop=True,
-                )
-            if last:
-                res1 = keep.tile([P, B], F32, name=f"res1_{g0}")
-                nc.scalar.activation(res[:, 0, :], accs[0], COPY)
-                nc.vector.tensor_copy(res1[:], accs[1])
-                nc.scalar.dma_start(out[0:P, g], res[:, 0, :])
-                nc.sync.dma_start(out[P : 2 * P, g], res1[:])
-            else:
-                nc.scalar.activation(res[:], both[:], COPY)
-                nc.sync.dma_start(out_rows[:, :, g], res[:])
+                multiply(acc[:, m, :], m, *quantised)
+            res = sbuf([P, 2, bags], F32, f"res{g0}")
+            nc.scalar.activation(res[:], acc[:], COPY)
+            nc.sync.dma_start(out_rows[:, :, g0 : g0 + bags], res[:])
+
+        def last_product(g0, bags, quantised, bank_tags, queues=None):
+            accs = [psum.tile([P, bags], F32, name="acc", tag=tag) for tag in bank_tags]
+            res = [sbuf([P, bags], F32, f"res{g0}_{m}") for m in range(2)]
+            for m in range(2):
+                multiply(accs[m][:], m, *quantised)
+            nc.scalar.activation(res[0][:], accs[0][:], COPY)
+            nc.vector.tensor_copy(res[1][:], accs[1][:])
+            nc.scalar.dma_start(out[0:P, g0 : g0 + bags], res[0][:])
+            nc.sync.dma_start(out[P : 2 * P, g0 : g0 + bags], res[1][:])
 
         wide = [pair[:].bitcast(BF16).rearrange("p (c t) -> p c t", t=2) for pair in pairs]
         for engine, h, c0, c1 in MERGES:
@@ -158,27 +144,27 @@ def tile_attend_bag_kernel(tc, xT, w, offs, out):
                 nc.vector.tensor_copy(wide[h][:, c0:c1, 0], low[:, c0 - l0 : c1 - l0])
             else:
                 nc.scalar.activation(wide[h][:, c0:c1, 0], low[:, c0 - l0 : c1 - l0], COPY)
-        first_turned = keep.tile([P, SPLIT], F32, name="first_turned", tag=f"low2_{last_low}")
-        for h in range(2):
-            for g0 in range(0, G, B):
-                gather(h, g0)
-                if g0 < SPLIT:
-                    level1_for_tensor(h, g0)
-                    level2_on_tensor(h, g0)
-                    if h == 1:
-                        turn_back(g0)
-                elif h == 0:
-                    level1(nc.gpsimd, 0, g0)
-            if h == 0:
-                nc.scalar.activation(
-                    w_bf[:].rearrange("p (m t) -> p m t", t=4), w_raw[:].rearrange("p t m -> p m t"), COPY
-                )
-        level1(nc.vector, 1, 2 * B)
-        level1(nc.vector, 1, 3 * B)
+        first_turned = sbuf([P, 2 * P], F32, "first_turned", f"low2_{last_low}")
+        for g0 in range(0, 2 * B, B):
+            gather(0, g0)
+            level2_on_tensor(0, g0, first_turned[:, g0 : g0 + P])
+        for g0 in range(2 * B, G, B):
+            gather(0, g0)
+            level1(nc.gpsimd, 0, g0, last_sums[:, 0, g0 - 2 * B : g0 - B])
+        nc.scalar.activation(w_bf[:].rearrange("p (m t) -> p m t", t=4), w_raw[:].rearrange("p t m -> p m t"), COPY)
+        e = [sbuf([P, 4 * B], BF16, f"e{i}") for i in range(4)]
+        for i, into in ((0, None), (1, flat_sums[:, 10 * B : 14 * B].bitcast(U32))):
+            gather(1, i * B, into=into)
+            level2_on_tensor(1, i * B, sbuf([P, P], F32, f"turned{i}")[:])
+            turn_back(i * B, e[i][:])
+        gather(1, 2 * B)
+        gather(1, 3 * B)
         nc.vector.quantize_mx(w_codes[:].bitcast(FP8X4), w_scales[:], w_bf[:])
-        level2(2 * B, "e256")
-        product(0, "codes0", ["acc0"], "turned128")
-        level2(3 * B, "e0")
-        product(2 * B, "codes256", ["back128"], "res256")
-        product(B, "codes128", ["acc128"], "res128")
-        product(3 * B, "e128", ["back0", "acc384"], "res384")
+        level1(nc.vector, 1, 2 * B, last_sums[:, 1, :B])
+        level1(nc.vector, 1, 3 * B, last_sums[:, 1, B:])
+        level2(e[2][:], 0, B)
+        product(0, B, quantise(0, B, e[0][:]), "fwd0")
+        level2(e[3][:], B, 2 * B)
+        product(2 * B, B, quantise(2 * B, B, e[2][:]), "fwd128")
+        product(3 * B, B, quantise(3 * B, B, e[3][:]), "back0")
+        last_product(B, B, quantise(B, B, e[1][:]), ["acc0", "acc1"])

@@ -5,6 +5,7 @@ from concourse.masks import make_identity
 
 D, T, G, K, M = 512, 2048, 512, 4, 256
 P = 128
+B = 128
 FLOPS = 2 * D * G * M
 
 F32 = mybir.dt.float32
@@ -15,10 +16,10 @@ U8 = mybir.dt.uint8
 FP8X4 = mybir.dt.float8_e4m3fn_x4
 ADD = mybir.AluOpType.add
 COPY = mybir.ActivationFunctionType.Copy
+ALONG = mybir.AxisListType.X
 
-LOADS = ((0, 0, 2048), (1, 0, 1024), (1, 1024, 1536), (1, 1536, 2048), (2, 0, 512), (3, 0, 512), (2, 512, 1024), (3, 512, 1024), (2, 1024, 1536), (3, 1024, 1536), (2, 1536, 1792), (3, 1536, 1792), (2, 1792, 2048), (3, 1792, 2048))
-MERGES = (("vector", 0, 0, 1024), ("vector", 0, 1024, 1536), ("vector", 0, 1536, 1856), ("scalar", 0, 1856, 2048), ("scalar", 1, 0, 512), ("scalar", 1, 512, 1024), ("scalar", 1, 1024, 1536), ("scalar", 1, 1536, 1792), ("scalar", 1, 1792, 2048))
-B = 128
+PIECES = (512, 512, 512, 256, 256)
+ON_SCALAR = 384
 
 
 def tile_attend_bag_kernel(tc, xT, w, offs, out):
@@ -34,78 +35,102 @@ def tile_attend_bag_kernel(tc, xT, w, offs, out):
             return keep.tile(shape, dtype, name=name, tag=tag or name, align_bytes=64)
 
         offsets = keep.tile([P, G * K // 16], U16, name="offsets")
-        pairs = [keep.tile([P, T], F32, name=f"pair{h}") for h in range(2)]
-        lows = {}
-        for t, c0, c1 in LOADS:
-            if t % 2 == 0:
-                low = sbuf([P, c1 - c0], F32, f"low{t}_{c0}")
-                nc.sync.dma_start(low[:], x_rows[:, t, c0:c1])
-                lows[t // 2, c0, c1] = low
-            else:
-                nc.sync.dma_start(pairs[t // 2][:, c0:c1], x_rows[:, t, c0:c1])
-            if t == 1 and c1 == T:
-                nc.sync.dma_start(offsets[:], offs)
-        last_low = max(c0 for t, c0, c1 in LOADS if t == 2)
+        early = sbuf([P, T], F32, "early")
+        pair = sbuf([P, T], F32, "pair")
+        late = sbuf([P, T], F32, "late")
+        late_bf = sbuf([P, T], BF16, "late_bf")
+        nc.sync.dma_start(offsets[:], offs)
+        nc.scalar.dma_start(early[:, :512], x_rows[:, 2, :512])
+        nc.sync.dma_start(early[:, 1024:], x_rows[:, 2, 1024:])
+        nc.scalar.dma_start(early[:, 512:1024], x_rows[:, 2, 512:1024])
+        lows = []
+        c = 0
+        for cols in PIECES:
+            low = sbuf([P, cols], F32, f"low{c}")
+            nc.sync.dma_start(low[:], x_rows[:, 0, c : c + cols])
+            nc.sync.dma_start(pair[:, c : c + cols], x_rows[:, 1, c : c + cols])
+            lows.append((low, c, cols))
+            c += cols
+        for c in (0, T // 2):
+            nc.sync.dma_start(late[:, c : c + T // 2], x_rows[:, 3, c : c + T // 2])
         w_raw = sbuf([P, 4, M], F32, "w_raw")
         nc.sync.dma_start(w_raw[:], w_rows)
 
-        warm = keep.tile([P, 1], F32, name="warm")
-        warmed = keep.tile([P, 1], F32, name="warmed")
+        warm = sbuf([P, 1], F32, "warm")
+        warmed = sbuf([P, 1], F32, "warmed")
         nc.vector.memset(warm[:], 0.0)
         nc.scalar.activation(warmed[:], warm[:], COPY)
         ident = keep.tile([P, P], F32, name="ident")
         make_identity(nc, ident[:])
 
-        flat_sums = sbuf([P, 2 * 2 * B * 4], F32, "last_sums")
-        last_sums = flat_sums[:].rearrange("p (h g e) -> p h g e", h=2, e=4)
-        got = {}
-        halves = {}
-        turned = {}
+        def listed(g0, bags):
+            return offsets[:, g0 * K // 16 : (g0 + bags) * K // 16]
 
-        def gather(h, g0, bags=B, into=None):
-            a = g0 * K // 16
-            g = sbuf([P, bags * K], U32, f"got{h}_{g0}") if into is None else into
-            nc.vector.tensor_copy(g[:], pairs[h][:].bitcast(U32).indirect(offsets[:, a : a + bags * K // 16]))
-            got[h, g0] = g[:]
+        e = sbuf([P, 4 * G], BF16, "e")
+        lanes = e[:].rearrange("p (g t) -> p g t", t=4)
+        words = e[:].bitcast(F32).rearrange("p (g h) -> p g h", h=2)
 
-        def level1(engine, h, g0, sums):
-            v = got[h, g0].bitcast(BF16).rearrange("p (g e) -> p g e", e=8)
-            engine.tensor_tensor(sums, v[:, :, 0:4], v[:, :, 4:8], ADD)
+        for g0 in range(0, G, B):
+            got = sbuf([P, B, K], F32, f"early{g0}")
+            nc.vector.tensor_copy(got[:].rearrange("p g j -> p (g j)"), early[:].indirect(listed(g0, B)))
+            half = sbuf([P, B, 2], F32, f"early_half{g0}")
+            nc.gpsimd.tensor_tensor(half[:], got[:, :, 0:2], got[:, :, 2:4], ADD)
+            nc.gpsimd.tensor_tensor(lanes[:, g0 : g0 + B, 2], half[:, :, 0], half[:, :, 1], ADD)
 
-        def level2_on_tensor(h, g0, into):
-            half = sbuf([P, 2, B, 2], F32, f"half{h}_{g0}")
-            v = got[h, g0].bitcast(BF16).rearrange("p (g s j t) -> p g s j t", s=2, j=2, t=2)
+        wide = pair[:].bitcast(BF16).rearrange("p (c t) -> p c t", t=2)
+        for low, c, cols in lows:
+            nc.scalar.activation(wide[:, c : c + cols, 0], low[:], COPY)
+        for c in (0, T // 2):
+            nc.scalar.activation(late_bf[:, c : c + T // 2], late[:, c : c + T // 2], COPY)
+
+        banks = []
+        for g0 in range(0, G, B):
+            got = sbuf([P, B * K], U32, f"pairs{g0}")
+            nc.vector.tensor_copy(got[:], pair[:].bitcast(U32).indirect(listed(g0, B)))
+            v = got[:].bitcast(BF16).rearrange("p (g s j t) -> p g s j t", s=2, j=2, t=2)
+            half = sbuf([P, 2, B, 2], F32, f"half{g0}")
             nc.gpsimd.tensor_tensor(half[:].rearrange("p j g t -> p g j t"), v[:, :, 0], v[:, :, 1], ADD)
-            bank = psum.tile([P, 2, P], F32, name="fwd", tag=f"fwd{g0}")
-            for t in range(2):
-                for j in range(2):
-                    nc.tensor.matmul(
-                        bank[:, t, :], lhsT=half[:, j, :, t], rhs=ident[:], is_transpose=True, start=j == 0, stop=j == 1
-                    )
-            turned[h, g0] = into
+            if g0 < 3 * B:
+                bank = psum.tile([P, 2, P], F32, name="fwd", tag=f"bank{g0}")
+                for t in range(2):
+                    for j in range(2):
+                        nc.tensor.matmul(
+                            bank[:, t, :], lhsT=half[:, j, :, t], rhs=ident[:], is_transpose=True, start=j == 0, stop=j == 1
+                        )
+                banks.append(bank)
+            else:
+                last_half = half
+
+        by_scalar = sbuf([P, ON_SCALAR * K], BF16, "by_scalar", f"early_half{G - 2 * B}")
+        for g0 in range(0, ON_SCALAR, B):
+            n = min(B, ON_SCALAR - g0)
+            nc.scalar.activation(by_scalar[:, g0 * K : (g0 + n) * K], late_bf[:].indirect(listed(g0, n)), COPY)
+        by_vector = sbuf([P, (G - ON_SCALAR) * K], F32, "by_vector", f"early_half{G - B}")
+        nc.vector.tensor_copy(by_vector[:], late[:].indirect(listed(ON_SCALAR, G - ON_SCALAR)))
+        with nc.allow_low_precision(reason="the sum is float32 inside the instruction and is rounded once"):
+            for g0 in range(0, ON_SCALAR, B):
+                n = min(B, ON_SCALAR - g0)
+                nc.vector.tensor_reduce(
+                    lanes[:, g0 : g0 + n, 3], by_scalar[:, g0 * K : (g0 + n) * K].rearrange("p (g j) -> p g j", j=K), ALONG, ADD
+                )
+            nc.vector.tensor_reduce(lanes[:, ON_SCALAR:, 3], by_vector[:].rearrange("p (g j) -> p g j", j=K), ALONG, ADD)
+
+        turned = sbuf([P, 3 * P], F32, "turned", "late_bf")
+        w_bf = sbuf([P, M * 4], BF16, "w_bf", "pairs384")
+        for i, bank in enumerate(banks):
             nc.scalar.activation(
-                into.bitcast(BF16).rearrange("g (p t) -> g p t", t=2), bank[:].rearrange("g t p -> g p t"), COPY
+                turned[:, i * P : (i + 1) * P].bitcast(BF16).rearrange("g (p t) -> g p t", t=2),
+                bank[:].rearrange("g t p -> g p t"),
+                COPY,
             )
-
-        def turn_back(g0, e):
-            bank = psum.tile([P, 2, B], F32, name="back", tag=f"back{g0}")
-            for h in range(2):
-                nc.tensor.transpose(bank[:, h, :], turned[h, g0], ident[:])
-            nc.scalar.copy(e.bitcast(F32).rearrange("p (g h) -> p g h", h=2), bank[:].rearrange("p h g -> p g h"))
-
-        def level2(e, b0, b1):
-            s = last_sums[:, :, b0:b1].rearrange("p h g e -> p g h e")
-            nc.vector.tensor_tensor(e.rearrange("p (g h t) -> p g h t", h=2, t=2), s[:, :, :, 0:2], s[:, :, :, 2:4], ADD)
-
-        w_bf = sbuf([P, M * 4], BF16, "w_bf")
+            back = psum.tile([P, B], F32, name="back", tag=f"back{i}")
+            nc.tensor.transpose(back[:], turned[:, i * P : (i + 1) * P], ident[:])
+            nc.scalar.copy(words[:, i * B : (i + 1) * B, 0], back[:])
+        nc.vector.tensor_copy(w_bf[:].rearrange("p (m t) -> p m t", t=4), w_raw[:].rearrange("p t m -> p m t"))
+        nc.vector.tensor_tensor(lanes[:, 3 * B :, 0:2], last_half[:, 0], last_half[:, 1], ADD)
         w_codes = sbuf([P, M], U32, "w_codes")
         w_scales = sbuf([P, M], U8, "w_scales")
-
-        def quantise(g0, bags, e, tag=None):
-            codes = sbuf([P, bags], U32, f"codes{g0}", tag)
-            scales = sbuf([P, bags], U8, f"scales{g0}")
-            nc.vector.quantize_mx(codes[:].bitcast(FP8X4), scales[:], e)
-            return codes, scales
+        nc.vector.quantize_mx(w_codes[:].bitcast(FP8X4), w_scales[:], w_bf[:])
 
         def multiply(acc, m, codes, scales):
             cols = slice(m * P, (m + 1) * P)
@@ -119,52 +144,22 @@ def tile_attend_bag_kernel(tc, xT, w, offs, out):
                 stop=True,
             )
 
-        def product(g0, bags, quantised, bank_tag):
-            acc = psum.tile([P, 2, bags], F32, name="acc", tag=bank_tag)
-            for m in range(2):
-                multiply(acc[:, m, :], m, *quantised)
-            res = sbuf([P, 2, bags], F32, f"res{g0}")
-            nc.scalar.activation(res[:], acc[:], COPY)
-            nc.sync.dma_start(out_rows[:, :, g0 : g0 + bags], res[:])
-
-        def last_product(g0, bags, quantised, bank_tags, queues=None):
-            accs = [psum.tile([P, bags], F32, name="acc", tag=tag) for tag in bank_tags]
-            res = [sbuf([P, bags], F32, f"res{g0}_{m}") for m in range(2)]
-            for m in range(2):
-                multiply(accs[m][:], m, *quantised)
-            nc.scalar.activation(res[0][:], accs[0][:], COPY)
-            nc.vector.tensor_copy(res[1][:], accs[1][:])
-            nc.scalar.dma_start(out[0:P, g0 : g0 + bags], res[0][:])
-            nc.sync.dma_start(out[P : 2 * P, g0 : g0 + bags], res[1][:])
-
-        wide = [pair[:].bitcast(BF16).rearrange("p (c t) -> p c t", t=2) for pair in pairs]
-        for engine, h, c0, c1 in MERGES:
-            low, l0 = [(tile, a) for (k, a, b), tile in lows.items() if k == h and a <= c0 and c1 <= b][0]
-            if engine == "vector":
-                nc.vector.tensor_copy(wide[h][:, c0:c1, 0], low[:, c0 - l0 : c1 - l0])
+        for i, tags in ((3, ("back2",)), (0, ("bank0",)), (1, ("bank128",)), (2, ("acc0", "acc1"))):
+            g = slice(i * B, (i + 1) * B)
+            codes = sbuf([P, B], U32, f"codes{i}")
+            scales = sbuf([P, B], U8, f"scales{i}")
+            nc.vector.quantize_mx(codes[:].bitcast(FP8X4), scales[:], e[:, 4 * i * B : 4 * (i + 1) * B])
+            if len(tags) == 1:
+                acc = psum.tile([P, 2, B], F32, name="acc", tag=tags[0])
+                res = sbuf([P, 2, B], F32, f"res{i}")
+                for m in range(2):
+                    multiply(acc[:, m, :], m, codes, scales)
+                nc.scalar.activation(res[:], acc[:], COPY)
+                nc.sync.dma_start(out_rows[:, :, g], res[:])
             else:
-                nc.scalar.activation(wide[h][:, c0:c1, 0], low[:, c0 - l0 : c1 - l0], COPY)
-        first_turned = sbuf([P, 2 * P], F32, "first_turned", f"low2_{last_low}")
-        for g0 in range(0, 2 * B, B):
-            gather(0, g0)
-            level2_on_tensor(0, g0, first_turned[:, g0 : g0 + P])
-        for g0 in range(2 * B, G, B):
-            gather(0, g0)
-            level1(nc.gpsimd, 0, g0, last_sums[:, 0, g0 - 2 * B : g0 - B])
-        nc.scalar.activation(w_bf[:].rearrange("p (m t) -> p m t", t=4), w_raw[:].rearrange("p t m -> p m t"), COPY)
-        e = [sbuf([P, 4 * B], BF16, f"e{i}") for i in range(4)]
-        for i, into in ((0, None), (1, flat_sums[:, 10 * B : 14 * B].bitcast(U32))):
-            gather(1, i * B, into=into)
-            level2_on_tensor(1, i * B, sbuf([P, P], F32, f"turned{i}")[:])
-            turn_back(i * B, e[i][:])
-        gather(1, 2 * B)
-        gather(1, 3 * B)
-        nc.vector.quantize_mx(w_codes[:].bitcast(FP8X4), w_scales[:], w_bf[:])
-        level1(nc.vector, 1, 2 * B, last_sums[:, 1, :B])
-        level1(nc.vector, 1, 3 * B, last_sums[:, 1, B:])
-        level2(e[2][:], 0, B)
-        product(0, B, quantise(0, B, e[0][:]), "fwd0")
-        level2(e[3][:], B, 2 * B)
-        product(2 * B, B, quantise(2 * B, B, e[2][:]), "fwd128")
-        product(3 * B, B, quantise(3 * B, B, e[3][:]), "back0")
-        last_product(B, B, quantise(B, B, e[1][:]), ["acc0", "acc1"])
+                for m in range(2):
+                    acc = psum.tile([P, B], F32, name="acc", tag=tags[m])
+                    res = sbuf([P, B], F32, f"res{i}_{m}")
+                    multiply(acc[:], m, codes, scales)
+                    nc.vector.tensor_copy(res[:], acc[:])
+                    (nc.sync if m else nc.scalar).dma_start(out[m * P : (m + 1) * P, g], res[:])

@@ -19,7 +19,6 @@ COPY = mybir.ActivationFunctionType.Copy
 ALONG = mybir.AxisListType.X
 
 PIECES = (512, 512, 512, 256, 256)
-ON_SCALAR = 384
 
 
 def tile_attend_bag_kernel(tc, xT, w, offs, out):
@@ -83,15 +82,27 @@ def tile_attend_bag_kernel(tc, xT, w, offs, out):
         for c in (0, T // 2):
             nc.scalar.activation(late_bf[:, c : c + T // 2], late[:, c : c + T // 2], COPY)
 
-        banks = []
+        order = (3, 0, 1, 2)
+        singles = {}
+        for i in order:
+            singles[i] = sbuf([P, B * K], BF16, f"single{i}", f"early_half{i * B}")
+            nc.scalar.activation(singles[i][:], late_bf[:].indirect(listed(i * B, B)), COPY)
+        gots = []
         for g0 in range(0, G, B):
-            got = sbuf([P, B * K], U32, f"pairs{g0}")
-            nc.vector.tensor_copy(got[:], pair[:].bitcast(U32).indirect(listed(g0, B)))
-            v = got[:].bitcast(BF16).rearrange("p (g s j t) -> p g s j t", s=2, j=2, t=2)
-            half = sbuf([P, 2, B, 2], F32, f"half{g0}")
+            gots.append(sbuf([P, B * K], U32, f"pairs{g0}"))
+            nc.vector.tensor_copy(gots[-1][:], pair[:].bitcast(U32).indirect(listed(g0, B)))
+        with nc.allow_low_precision(reason="the sum is float32 inside the instruction and is rounded once"):
+            for i in order:
+                nc.vector.tensor_reduce(
+                    lanes[:, i * B : (i + 1) * B, 3], singles[i][:].rearrange("p (g j) -> p g j", j=K), ALONG, ADD
+                )
+        banks = []
+        for i in range(4):
+            v = gots[i][:].bitcast(BF16).rearrange("p (g s j t) -> p g s j t", s=2, j=2, t=2)
+            half = sbuf([P, 2, B, 2], F32, f"half{i}", f"early_half{3 * B}" if i == 3 else None)
             nc.gpsimd.tensor_tensor(half[:].rearrange("p j g t -> p g j t"), v[:, :, 0], v[:, :, 1], ADD)
-            if g0 < 3 * B:
-                bank = psum.tile([P, 2, P], F32, name="fwd", tag=f"bank{g0}")
+            if i < 3:
+                bank = psum.tile([P, 2, P], F32, name="fwd", tag=f"bank{i * B}")
                 for t in range(2):
                     for j in range(2):
                         nc.tensor.matmul(
@@ -99,24 +110,9 @@ def tile_attend_bag_kernel(tc, xT, w, offs, out):
                         )
                 banks.append(bank)
             else:
-                last_half = half
-
-        by_scalar = sbuf([P, ON_SCALAR * K], BF16, "by_scalar", f"early_half{G - 2 * B}")
-        for g0 in range(0, ON_SCALAR, B):
-            n = min(B, ON_SCALAR - g0)
-            nc.scalar.activation(by_scalar[:, g0 * K : (g0 + n) * K], late_bf[:].indirect(listed(g0, n)), COPY)
-        by_vector = sbuf([P, (G - ON_SCALAR) * K], F32, "by_vector", f"early_half{G - B}")
-        nc.vector.tensor_copy(by_vector[:], late[:].indirect(listed(ON_SCALAR, G - ON_SCALAR)))
-        with nc.allow_low_precision(reason="the sum is float32 inside the instruction and is rounded once"):
-            for g0 in range(0, ON_SCALAR, B):
-                n = min(B, ON_SCALAR - g0)
-                nc.vector.tensor_reduce(
-                    lanes[:, g0 : g0 + n, 3], by_scalar[:, g0 * K : (g0 + n) * K].rearrange("p (g j) -> p g j", j=K), ALONG, ADD
-                )
-            nc.vector.tensor_reduce(lanes[:, ON_SCALAR:, 3], by_vector[:].rearrange("p (g j) -> p g j", j=K), ALONG, ADD)
+                nc.gpsimd.tensor_tensor(lanes[:, 3 * B :, 0:2], half[:, 0], half[:, 1], ADD)
 
         turned = sbuf([P, 3 * P], F32, "turned", "late_bf")
-        w_bf = sbuf([P, M * 4], BF16, "w_bf", "pairs384")
         for i, bank in enumerate(banks):
             nc.scalar.activation(
                 turned[:, i * P : (i + 1) * P].bitcast(BF16).rearrange("g (p t) -> g p t", t=2),
@@ -126,8 +122,8 @@ def tile_attend_bag_kernel(tc, xT, w, offs, out):
             back = psum.tile([P, B], F32, name="back", tag=f"back{i}")
             nc.tensor.transpose(back[:], turned[:, i * P : (i + 1) * P], ident[:])
             nc.scalar.copy(words[:, i * B : (i + 1) * B, 0], back[:])
+        w_bf = sbuf([P, M * 4], BF16, "w_bf", f"early_half{3 * B}")
         nc.vector.tensor_copy(w_bf[:].rearrange("p (m t) -> p m t", t=4), w_raw[:].rearrange("p t m -> p m t"))
-        nc.vector.tensor_tensor(lanes[:, 3 * B :, 0:2], last_half[:, 0], last_half[:, 1], ADD)
         w_codes = sbuf([P, M], U32, "w_codes")
         w_scales = sbuf([P, M], U8, "w_scales")
         nc.vector.quantize_mx(w_codes[:].bitcast(FP8X4), w_scales[:], w_bf[:])

@@ -85,8 +85,8 @@ def tile_attend_bag_kernel(tc, xT, w, offs, out):
         order = (3, 0, 1, 2)
         singles = {}
         for i in order:
-            singles[i] = sbuf([P, B * K], BF16, f"single{i}", f"early_half{i * B}")
-            nc.scalar.activation(singles[i][:], late_bf[:].indirect(listed(i * B, B)), COPY)
+            singles[i] = sbuf([P, B * K, 2], BF16, f"single{i}", f"early_half{i * B}")
+            nc.scalar.activation(singles[i][:, :, 1], late_bf[:].indirect(listed(i * B, B)), COPY)
         gots = []
         for g0 in range(0, G, B):
             gots.append(sbuf([P, B * K], U32, f"pairs{g0}"))
@@ -94,7 +94,7 @@ def tile_attend_bag_kernel(tc, xT, w, offs, out):
         with nc.allow_low_precision(reason="the sum is float32 inside the instruction and is rounded once"):
             for i in order:
                 nc.vector.tensor_reduce(
-                    lanes[:, i * B : (i + 1) * B, 3], singles[i][:].rearrange("p (g j) -> p g j", j=K), ALONG, ADD
+                    lanes[:, i * B : (i + 1) * B, 3], singles[i][:, :, 1].rearrange("p (g j) -> p g j", j=K), ALONG, ADD
                 )
         banks = []
         for i in range(4):

@@ -15,10 +15,13 @@ U16 = mybir.dt.uint16
 U8 = mybir.dt.uint8
 FP8X4 = mybir.dt.float8_e4m3fn_x4
 ADD = mybir.AluOpType.add
+MULT = mybir.AluOpType.mult
 COPY = mybir.ActivationFunctionType.Copy
 ALONG = mybir.AxisListType.X
 
-PIECES = (512, 512, 512, 256, 256)
+PAIR_PIECES = (512, 512, 512, 256, 256)
+LAST_PIECES = (512, 512, 512, 256, 256)
+SCALAR_CAST = 640
 
 
 def tile_attend_bag_kernel(tc, xT, w, offs, out):
@@ -33,26 +36,27 @@ def tile_attend_bag_kernel(tc, xT, w, offs, out):
         def sbuf(shape, dtype, name, tag=None):
             return keep.tile(shape, dtype, name=name, tag=tag or name, align_bytes=64)
 
+        def spans(pieces):
+            return [(sum(pieces[:i]), sum(pieces[: i + 1])) for i in range(len(pieces))]
+
         offsets = keep.tile([P, G * K // 16], U16, name="offsets")
-        early = sbuf([P, T], F32, "early")
+        first = sbuf([P, T], F32, "first")
+        first_bf = sbuf([P, T], BF16, "first_bf")
+        low = sbuf([P, T], F32, "low")
         pair = sbuf([P, T], F32, "pair")
-        late = sbuf([P, T], F32, "late")
-        late_bf = sbuf([P, T], BF16, "late_bf")
-        nc.sync.dma_start(offsets[:], offs)
-        nc.scalar.dma_start(early[:, :512], x_rows[:, 2, :512])
-        nc.sync.dma_start(early[:, 1024:], x_rows[:, 2, 1024:])
-        nc.scalar.dma_start(early[:, 512:1024], x_rows[:, 2, 512:1024])
-        lows = []
-        c = 0
-        for cols in PIECES:
-            low = sbuf([P, cols], F32, f"low{c}")
-            nc.sync.dma_start(low[:], x_rows[:, 0, c : c + cols])
-            nc.sync.dma_start(pair[:, c : c + cols], x_rows[:, 1, c : c + cols])
-            lows.append((low, c, cols))
-            c += cols
-        for c in (0, T // 2):
-            nc.sync.dma_start(late[:, c : c + T // 2], x_rows[:, 3, c : c + T // 2])
+        last_bf = sbuf([P, T], BF16, "last_bf")
         w_raw = sbuf([P, 4, M], F32, "w_raw")
+        nc.scalar.dma_start(first[:, : T // 2], x_rows[:, 2, : T // 2])
+        nc.sync.dma_start(first[:, T // 2 :], x_rows[:, 2, T // 2 :])
+        nc.scalar.dma_start(low[:, : T // 2], x_rows[:, 0, : T // 2])
+        nc.sync.dma_start(offsets[:], offs)
+        nc.sync.dma_start(low[:, T // 2 :], x_rows[:, 0, T // 2 :])
+        for c0, c1 in spans(PAIR_PIECES):
+            nc.sync.dma_start(pair[:, c0:c1], x_rows[:, 1, c0:c1])
+        staged = []
+        for c0, c1 in spans(LAST_PIECES):
+            staged.append(sbuf([P, c1 - c0], F32, f"staged{c0}"))
+            nc.sync.dma_start(staged[-1][:], x_rows[:, 3, c0:c1])
         nc.sync.dma_start(w_raw[:], w_rows)
 
         warm = sbuf([P, 1], F32, "warm")
@@ -62,100 +66,103 @@ def tile_attend_bag_kernel(tc, xT, w, offs, out):
         ident = keep.tile([P, P], F32, name="ident")
         make_identity(nc, ident[:])
 
-        def listed(g0, bags):
-            return offsets[:, g0 * K // 16 : (g0 + bags) * K // 16]
+        def listed(i):
+            return offsets[:, i * B * K // 16 : (i + 1) * B * K // 16]
 
-        e = sbuf([P, 4 * G], BF16, "e")
-        lanes = e[:].rearrange("p (g t) -> p g t", t=4)
-        words = e[:].bitcast(F32).rearrange("p (g h) -> p g h", h=2)
-
-        for g0 in range(0, G, B):
-            got = sbuf([P, B, K], F32, f"early{g0}")
-            nc.vector.tensor_copy(got[:].rearrange("p g j -> p (g j)"), early[:].indirect(listed(g0, B)))
-            half = sbuf([P, B, 2], F32, f"early_half{g0}")
-            nc.gpsimd.tensor_tensor(half[:], got[:, :, 0:2], got[:, :, 2:4], ADD)
-            nc.gpsimd.tensor_tensor(lanes[:, g0 : g0 + B, 2], half[:, :, 0], half[:, :, 1], ADD)
-
-        wide = pair[:].bitcast(BF16).rearrange("p (c t) -> p c t", t=2)
-        for low, c, cols in lows:
-            nc.scalar.activation(wide[:, c : c + cols, 0], low[:], COPY)
-        for c in (0, T // 2):
-            nc.scalar.activation(late_bf[:, c : c + T // 2], late[:, c : c + T // 2], COPY)
-
-        order = (3, 0, 1, 2)
         singles = {}
-        for i in order:
-            singles[i] = sbuf([P, B * K, 2], BF16, f"single{i}", f"early_half{i * B}")
-            nc.scalar.activation(singles[i][:, :, 1], late_bf[:].indirect(listed(i * B, B)), COPY)
-        gots = []
-        for g0 in range(0, G, B):
-            gots.append(sbuf([P, B * K], U32, f"pairs{g0}"))
-            nc.vector.tensor_copy(gots[-1][:], pair[:].bitcast(U32).indirect(listed(g0, B)))
-        with nc.allow_low_precision(reason="the sum is float32 inside the instruction and is rounded once"):
-            for i in order:
-                nc.vector.tensor_reduce(
-                    lanes[:, i * B : (i + 1) * B, 3], singles[i][:, :, 1].rearrange("p (g j) -> p g j", j=K), ALONG, ADD
-                )
-        banks = []
-        for i in range(4):
-            v = gots[i][:].bitcast(BF16).rearrange("p (g s j t) -> p g s j t", s=2, j=2, t=2)
-            half = sbuf([P, 2, B, 2], F32, f"half{i}", f"early_half{3 * B}" if i == 3 else None)
-            nc.gpsimd.tensor_tensor(half[:].rearrange("p j g t -> p g j t"), v[:, :, 0], v[:, :, 1], ADD)
-            if i < 3:
-                bank = psum.tile([P, 2, P], F32, name="fwd", tag=f"bank{i * B}")
-                for t in range(2):
-                    for j in range(2):
-                        nc.tensor.matmul(
-                            bank[:, t, :], lhsT=half[:, j, :, t], rhs=ident[:], is_transpose=True, start=j == 0, stop=j == 1
-                        )
-                banks.append(bank)
-            else:
-                nc.gpsimd.tensor_tensor(lanes[:, 3 * B :, 0:2], half[:, 0], half[:, 1], ADD)
+        for t in (2, 3):
+            for i in range(3):
+                singles[t, i] = sbuf([P, K, B], F32, f"single{t}_{i}")
+                nc.vector.memset(singles[t, i][:], 0.0)
 
-        turned = sbuf([P, 3 * P], F32, "turned", "late_bf")
-        for i, bank in enumerate(banks):
+        banks = [psum.tile([P, 4, P], F32, name="fwd", tag=f"fwd{i}") for i in range(3)]
+
+        def add_turned(into, terms):
+            for j, term in enumerate(terms):
+                nc.tensor.matmul(into, lhsT=term, rhs=ident[:], is_transpose=True, start=j == 0, stop=j == len(terms) - 1)
+
+        def single_on_scalar(t, i, window):
+            high = singles[t, i][:].bitcast(BF16).rearrange("p j (g s) -> p g j s", s=2)[:, :, :, 1]
+            nc.scalar.activation(high, window[:].indirect(listed(i)), COPY)
+            add_turned(banks[i][:, t, :], [singles[t, i][:, j, :] for j in range(K)])
+
+        e = [sbuf([P, 4 * B], BF16, f"e{i}") for i in range(4)]
+        lanes = e[3][:].rearrange("p (g t) -> p g t", t=4)
+
+        def reduce_into(lane, terms):
+            with nc.allow_low_precision(reason="the sum is float32 inside the instruction and is rounded once"):
+                nc.vector.tensor_reduce(lane, terms, ALONG, ADD)
+
+        nc.vector.tensor_copy(first_bf[:, SCALAR_CAST:], first[:, SCALAR_CAST:])
+        nc.scalar.activation(first_bf[:, :SCALAR_CAST], first[:, :SCALAR_CAST], COPY)
+        got_first = sbuf([P, B * K], F32, "got_first")
+        nc.vector.tensor_copy(got_first[:], first[:].indirect(listed(3)))
+        reduce_into(lanes[:, :, 2], got_first[:].rearrange("p (g j) -> p g j", j=K))
+        for i in range(3):
+            single_on_scalar(2, i, first_bf)
+
+        halves = pair[:].bitcast(BF16).rearrange("p (c t) -> p c t", t=2)
+        for c0, c1 in spans(PAIR_PIECES):
+            nc.vector.tensor_copy(halves[:, c0:c1, 0], low[:, c0:c1])
+        for piece, (c0, c1) in zip(staged, spans(LAST_PIECES)):
+            nc.scalar.activation(last_bf[:, c0:c1], piece[:], COPY)
+
+        late = sbuf([P, 2 * B * K], U32, "late", "staged1792")
+        got = [sbuf([P, B * K], U32, f"got{i}")[:] for i in range(2)] + [late[:, : B * K], late[:, B * K :]]
+        for i in range(3):
+            nc.vector.tensor_copy(got[i], pair[:].bitcast(U32).indirect(listed(i)))
+            half = sbuf([P, 2, B, 2], F32, f"half{i}")
+            v = got[i].bitcast(BF16).rearrange("p (g s j t) -> p g s j t", s=2, j=2, t=2)
+            nc.gpsimd.tensor_tensor(half[:].rearrange("p j g t -> p g j t"), v[:, :, 0], v[:, :, 1], ADD)
+            for t in range(2):
+                add_turned(banks[i][:, t, :], [half[:, j, :, t] for j in range(2)])
+            single_on_scalar(3, i, last_bf)
+        got_last = sbuf([P, B * K], BF16, "got_last")
+        nc.vector.tensor_copy(got_last[:], last_bf[:].indirect(listed(3)))
+        nc.vector.tensor_copy(got[3], pair[:].bitcast(U32).indirect(listed(3)))
+        reduce_into(lanes[:, :, 3], got_last[:].rearrange("p (g j) -> p g j", j=K))
+        reduce_into(lanes[:, :, 0:2], got[3].bitcast(BF16).rearrange("p (g j t) -> p g t j", j=K, t=2))
+
+        w_bf = sbuf([P, M * 4], BF16, "w_bf")
+        nc.gpsimd.tensor_scalar(
+            w_bf[:].rearrange("p (m t) -> p m t", t=4), w_raw[:].rearrange("p t m -> p m t"), 1.0, 0.0, MULT, ADD
+        )
+        turned = []
+        for i in range(3):
+            turned.append(sbuf([P, 2, P], F32, f"turned{i}"))
             nc.scalar.activation(
-                turned[:, i * P : (i + 1) * P].bitcast(BF16).rearrange("g (p t) -> g p t", t=2),
-                bank[:].rearrange("g t p -> g p t"),
+                turned[i][:].bitcast(BF16).rearrange("g h (p s) -> g h p s", s=2),
+                banks[i][:].rearrange("g (h s) p -> g h p s", s=2),
                 COPY,
             )
-            back = psum.tile([P, B], F32, name="back", tag=f"back{i}")
-            nc.tensor.transpose(back[:], turned[:, i * P : (i + 1) * P], ident[:])
-            nc.scalar.copy(words[:, i * B : (i + 1) * B, 0], back[:])
-        w_bf = sbuf([P, M * 4], BF16, "w_bf", f"early_half{3 * B}")
-        nc.vector.tensor_copy(w_bf[:].rearrange("p (m t) -> p m t", t=4), w_raw[:].rearrange("p t m -> p m t"))
+        for i in range(3):
+            back = psum.tile([P, 2, B], F32, name="back", tag=f"back{i}")
+            for h in range(2):
+                nc.tensor.transpose(back[:, h, :], turned[i][:, h, :], ident[:])
+            nc.scalar.copy(e[i][:].bitcast(F32).rearrange("p (g h) -> p g h", h=2), back[:].rearrange("p h g -> p g h"))
+
         w_codes = sbuf([P, M], U32, "w_codes")
         w_scales = sbuf([P, M], U8, "w_scales")
         nc.vector.quantize_mx(w_codes[:].bitcast(FP8X4), w_scales[:], w_bf[:])
-
-        def multiply(acc, m, codes, scales):
-            cols = slice(m * P, (m + 1) * P)
-            nc.tensor.matmul_mx(
-                acc,
-                lhsT=w_codes[:, cols].bitcast(FP8X4),
-                lhsT_scale=w_scales[:, cols],
-                rhs=codes[:].bitcast(FP8X4),
-                rhs_scale=scales[:],
-                start=True,
-                stop=True,
-            )
-
-        for i, tags in ((3, ("back2",)), (0, ("bank0",)), (1, ("bank128",)), (2, ("acc0", "acc1"))):
-            g = slice(i * B, (i + 1) * B)
+        for i, tag in ((3, "fwd0"), (0, "fwd1"), (1, "fwd2"), (2, "back0")):
             codes = sbuf([P, B], U32, f"codes{i}")
             scales = sbuf([P, B], U8, f"scales{i}")
-            nc.vector.quantize_mx(codes[:].bitcast(FP8X4), scales[:], e[:, 4 * i * B : 4 * (i + 1) * B])
-            if len(tags) == 1:
-                acc = psum.tile([P, 2, B], F32, name="acc", tag=tags[0])
-                res = sbuf([P, 2, B], F32, f"res{i}")
-                for m in range(2):
-                    multiply(acc[:, m, :], m, codes, scales)
-                nc.scalar.activation(res[:], acc[:], COPY)
-                nc.sync.dma_start(out_rows[:, :, g], res[:])
+            nc.vector.quantize_mx(codes[:].bitcast(FP8X4), scales[:], e[i][:])
+            acc = psum.tile([P, 2, B], F32, name="acc", tag=tag)
+            for m in range(2):
+                cols = slice(m * P, (m + 1) * P)
+                nc.tensor.matmul_mx(
+                    acc[:, m, :],
+                    lhsT=w_codes[:, cols].bitcast(FP8X4),
+                    lhsT_scale=w_scales[:, cols],
+                    rhs=codes[:].bitcast(FP8X4),
+                    rhs_scale=scales[:],
+                    start=True,
+                    stop=True,
+                )
+            res = sbuf([P, 2, B], F32, f"res{i}")
+            if i == 2:
+                nc.vector.tensor_copy(res[:], acc[:])
             else:
-                for m in range(2):
-                    acc = psum.tile([P, B], F32, name="acc", tag=tags[m])
-                    res = sbuf([P, B], F32, f"res{i}_{m}")
-                    multiply(acc[:], m, codes, scales)
-                    nc.vector.tensor_copy(res[:], acc[:])
-                    (nc.sync if m else nc.scalar).dma_start(out[m * P : (m + 1) * P, g], res[:])
+                nc.scalar.activation(res[:], acc[:], COPY)
+            nc.sync.dma_start(out_rows[:, :, i * B : (i + 1) * B], res[:])

@@ -144,25 +144,34 @@ def tile_attend_bag_kernel(tc, xT, w, offs, out):
         w_codes = sbuf([P, M], U32, "w_codes")
         w_scales = sbuf([P, M], U8, "w_scales")
         nc.vector.quantize_mx(w_codes[:].bitcast(FP8X4), w_scales[:], w_bf[:])
-        for i, tag in ((3, "fwd0"), (0, "fwd1"), (1, "fwd2"), (2, "back0")):
+
+        def quantise(i):
             codes = sbuf([P, B], U32, f"codes{i}")
             scales = sbuf([P, B], U8, f"scales{i}")
             nc.vector.quantize_mx(codes[:].bitcast(FP8X4), scales[:], e[i][:])
-            acc = psum.tile([P, 2, B], F32, name="acc", tag=tag)
-            for m in range(2):
-                cols = slice(m * P, (m + 1) * P)
-                nc.tensor.matmul_mx(
-                    acc[:, m, :],
-                    lhsT=w_codes[:, cols].bitcast(FP8X4),
-                    lhsT_scale=w_scales[:, cols],
-                    rhs=codes[:].bitcast(FP8X4),
-                    rhs_scale=scales[:],
-                    start=True,
-                    stop=True,
-                )
-            res = sbuf([P, 2, B], F32, f"res{i}")
-            if i == 2:
-                nc.vector.tensor_copy(res[:], acc[:])
-            else:
-                nc.scalar.activation(res[:], acc[:], COPY)
-            nc.sync.dma_start(out_rows[:, :, i * B : (i + 1) * B], res[:])
+            return codes, scales
+
+        def multiply(acc, m, codes, scales):
+            cols = slice(m * P, (m + 1) * P)
+            nc.tensor.matmul_mx(
+                acc,
+                lhsT=w_codes[:, cols].bitcast(FP8X4),
+                lhsT_scale=w_scales[:, cols],
+                rhs=codes[:].bitcast(FP8X4),
+                rhs_scale=scales[:],
+                start=True,
+                stop=True,
+            )
+
+        for i, parts in ((3, ((0, 2, "fwd2", nc.scalar, nc.sync),)), (0, ((0, 2, "fwd0", nc.scalar, nc.sync),)), (1, ((0, 2, "fwd1", nc.scalar, nc.sync),)), (2, ((0, 2, "back0", nc.vector, nc.sync),))):
+            quantised = quantise(i)
+            for m0, m1, tag, engine, queue in parts:
+                acc = psum.tile([P, m1 - m0, B], F32, name="acc", tag=tag)
+                for m in range(m0, m1):
+                    multiply(acc[:, m - m0, :], m, *quantised)
+                res = sbuf([P, m1 - m0, B], F32, f"res{i}_{m0}")
+                if engine is nc.scalar:
+                    nc.scalar.activation(res[:], acc[:], COPY)
+                else:
+                    nc.vector.tensor_copy(res[:], acc[:])
+                queue.dma_start(out_rows[:, m0:m1, i * B : (i + 1) * B], res[:])

@@ -20,8 +20,9 @@ COPY = mybir.ActivationFunctionType.Copy
 ALONG = mybir.AxisListType.X
 
 PAIR_PIECES = (512, 512, 512, 256, 256)
-LAST_PIECES = (512, 512, 512, 256, 256)
+LAST_PIECES = (512, 512, 512, 512)
 SCALAR_CAST = 640
+SCALAR_MERGE = 160
 
 
 def tile_attend_bag_kernel(tc, xT, w, offs, out):
@@ -103,19 +104,24 @@ def tile_attend_bag_kernel(tc, xT, w, offs, out):
 
         halves = pair[:].bitcast(BF16).rearrange("p (c t) -> p c t", t=2)
         for c0, c1 in spans(PAIR_PIECES):
+            c1 = min(c1, T - SCALAR_MERGE)
             nc.vector.tensor_copy(halves[:, c0:c1, 0], low[:, c0:c1])
+        nc.scalar.activation(halves[:, T - SCALAR_MERGE :, 0], low[:, T - SCALAR_MERGE :], COPY)
         for piece, (c0, c1) in zip(staged, spans(LAST_PIECES)):
             nc.scalar.activation(last_bf[:, c0:c1], piece[:], COPY)
 
-        late = sbuf([P, 2 * B * K], U32, "late", "staged1792")
+        late = sbuf([P, 2 * B * K], U32, "late", "staged1024")
         got = [sbuf([P, B * K], U32, f"got{i}")[:] for i in range(2)] + [late[:, : B * K], late[:, B * K :]]
         for i in range(3):
             nc.vector.tensor_copy(got[i], pair[:].bitcast(U32).indirect(listed(i)))
             half = sbuf([P, 2, B, 2], F32, f"half{i}")
             v = got[i].bitcast(BF16).rearrange("p (g s j t) -> p g s j t", s=2, j=2, t=2)
             nc.gpsimd.tensor_tensor(half[:].rearrange("p j g t -> p g j t"), v[:, :, 0], v[:, :, 1], ADD)
-            for t in range(2):
-                add_turned(banks[i][:, t, :], [half[:, j, :, t] for j in range(2)])
+            if i < 2:
+                for t in range(2):
+                    add_turned(banks[i][:, t, :], [half[:, j, :, t] for j in range(2)])
+            else:
+                nc.gpsimd.tensor_tensor(e[i][:].rearrange("p (g t) -> p g t", t=4)[:, :, 0:2], half[:, 0], half[:, 1], ADD)
             single_on_scalar(3, i, last_bf)
         got_last = sbuf([P, B * K], BF16, "got_last")
         nc.vector.tensor_copy(got_last[:], last_bf[:].indirect(listed(3)))
@@ -130,16 +136,21 @@ def tile_attend_bag_kernel(tc, xT, w, offs, out):
         turned = []
         for i in range(3):
             turned.append(sbuf([P, 2, P], F32, f"turned{i}"))
+            h0 = 0 if i < 2 else 1
             nc.scalar.activation(
-                turned[i][:].bitcast(BF16).rearrange("g h (p s) -> g h p s", s=2),
-                banks[i][:].rearrange("g (h s) p -> g h p s", s=2),
+                turned[i][:, h0:].bitcast(BF16).rearrange("g h (p s) -> g h p s", s=2),
+                banks[i][:, 2 * h0 :].rearrange("g (h s) p -> g h p s", s=2),
                 COPY,
             )
         for i in range(3):
             back = psum.tile([P, 2, B], F32, name="back", tag=f"back{i}")
-            for h in range(2):
+            h0 = 0 if i < 2 else 1
+            for h in range(h0, 2):
                 nc.tensor.transpose(back[:, h, :], turned[i][:, h, :], ident[:])
-            nc.scalar.copy(e[i][:].bitcast(F32).rearrange("p (g h) -> p g h", h=2), back[:].rearrange("p h g -> p g h"))
+            nc.scalar.copy(
+                e[i][:].bitcast(F32).rearrange("p (g h) -> p g h", h=2)[:, :, h0:],
+                back[:, h0:].rearrange("p h g -> p g h"),
+            )
 
         w_codes = sbuf([P, M], U32, "w_codes")
         w_scales = sbuf([P, M], U8, "w_scales")
@@ -163,15 +174,19 @@ def tile_attend_bag_kernel(tc, xT, w, offs, out):
                 stop=True,
             )
 
-        for i, parts in ((3, ((0, 2, "fwd2", nc.scalar, nc.sync),)), (0, ((0, 2, "fwd0", nc.scalar, nc.sync),)), (1, ((0, 2, "fwd1", nc.scalar, nc.sync),)), (2, ((0, 2, "back0", nc.vector, nc.sync),))):
+        for i, tag in ((3, "fwd2"), (0, "fwd0"), (1, "fwd1")):
             quantised = quantise(i)
-            for m0, m1, tag, engine, queue in parts:
-                acc = psum.tile([P, m1 - m0, B], F32, name="acc", tag=tag)
-                for m in range(m0, m1):
-                    multiply(acc[:, m - m0, :], m, *quantised)
-                res = sbuf([P, m1 - m0, B], F32, f"res{i}_{m0}")
-                if engine is nc.scalar:
-                    nc.scalar.activation(res[:], acc[:], COPY)
-                else:
-                    nc.vector.tensor_copy(res[:], acc[:])
-                queue.dma_start(out_rows[:, m0:m1, i * B : (i + 1) * B], res[:])
+            acc = psum.tile([P, 2, B], F32, name="acc", tag=tag)
+            for m in range(2):
+                multiply(acc[:, m, :], m, *quantised)
+            res = sbuf([P, 2, B], F32, f"res{i}")
+            nc.scalar.activation(res[:], acc[:], COPY)
+            nc.sync.dma_start(out_rows[:, :, i * B : (i + 1) * B], res[:])
+        quantised = quantise(2)
+        res = sbuf([P, 2, B], F32, "res2")
+        accs = [psum.tile([P, B], F32, name="acc", tag=f"back{m}") for m in range(2)]
+        for m in range(2):
+            multiply(accs[m][:], m, *quantised)
+        nc.scalar.activation(res[:, 0, :], accs[0][:], COPY)
+        nc.vector.tensor_copy(res[:, 1, :], accs[1][:])
+        nc.sync.dma_start(out_rows[:, :, 2 * B : 3 * B], res[:])

@@ -35,7 +35,7 @@ def tile_attend_bag_kernel(tc, xT, w, offs, out):
         psum = ctx.enter_context(tc.psum_pool(name="psum", bufs=1))
 
         def sbuf(shape, dtype, name, tag=None):
-            return keep.tile(shape, dtype, name=name, tag=tag or name, align_bytes=64)
+            return keep.tile(shape, dtype, name=name, tag=tag or name, align_bytes=256)
 
         def spans(pieces):
             return [(sum(pieces[:i]), sum(pieces[: i + 1])) for i in range(len(pieces))]

@@ -22,7 +22,6 @@ ALONG = mybir.AxisListType.X
 PAIR_PIECES = (512, 512, 512, 256, 256)
 LAST_PIECES = (512, 512, 512, 512)
 SCALAR_CAST = 640
-SCALAR_MERGE = 160
 
 
 def tile_attend_bag_kernel(tc, xT, w, offs, out):
@@ -94,7 +93,8 @@ def tile_attend_bag_kernel(tc, xT, w, offs, out):
             with nc.allow_low_precision(reason="the sum is float32 inside the instruction and is rounded once"):
                 nc.vector.tensor_reduce(lane, terms, ALONG, ADD)
 
-        nc.vector.tensor_copy(first_bf[:, SCALAR_CAST:], first[:, SCALAR_CAST:])
+        nc.vector.tensor_copy(first_bf[:, T // 2 :], first[:, T // 2 :])
+        nc.vector.tensor_copy(first_bf[:, SCALAR_CAST : T // 2], first[:, SCALAR_CAST : T // 2])
         nc.scalar.activation(first_bf[:, :SCALAR_CAST], first[:, :SCALAR_CAST], COPY)
         got_first = sbuf([P, B * K], F32, "got_first")
         nc.vector.tensor_copy(got_first[:], first[:].indirect(listed(3)))
@@ -104,9 +104,7 @@ def tile_attend_bag_kernel(tc, xT, w, offs, out):
 
         halves = pair[:].bitcast(BF16).rearrange("p (c t) -> p c t", t=2)
         for c0, c1 in spans(PAIR_PIECES):
-            c1 = min(c1, T - SCALAR_MERGE)
             nc.vector.tensor_copy(halves[:, c0:c1, 0], low[:, c0:c1])
-        nc.scalar.activation(halves[:, T - SCALAR_MERGE :, 0], low[:, T - SCALAR_MERGE :], COPY)
         for piece, (c0, c1) in zip(staged, spans(LAST_PIECES)):
             nc.scalar.activation(last_bf[:, c0:c1], piece[:], COPY)
 

@@ -19,7 +19,7 @@ MULT = mybir.AluOpType.mult
 COPY = mybir.ActivationFunctionType.Copy
 ALONG = mybir.AxisListType.X
 
-PAIR_PIECES = (512, 512, 512, 256, 256)
+PAIR_PIECES = (512, 512, 512, 512)
 LAST_PIECES = (512, 512, 512, 512)
 SCALAR_CAST = 640
 

@@ -59,10 +59,6 @@ def tile_attend_bag_kernel(tc, xT, w, offs, out):
             nc.sync.dma_start(staged[-1][:], x_rows[:, 3, c0:c1])
         nc.sync.dma_start(w_raw[:], w_rows)
 
-        warm = sbuf([P, 1], F32, "warm")
-        warmed = sbuf([P, 1], F32, "warmed")
-        nc.vector.memset(warm[:], 0.0)
-        nc.scalar.activation(warmed[:], warm[:], COPY)
         ident = keep.tile([P, P], F32, name="ident")
         make_identity(nc, ident[:])
 

@@ -19,8 +19,8 @@ MULT = mybir.AluOpType.mult
 COPY = mybir.ActivationFunctionType.Copy
 ALONG = mybir.AxisListType.X
 
-PAIR_PIECES = (512, 512, 512, 512)
-LAST_PIECES = (512, 512, 512, 512)
+PAIR_PIECES = (512, 512, 512, 256, 256)
+LAST_PIECES = (512, 512, 512, 256, 256)
 SCALAR_CAST = 640
 
 
@@ -48,8 +48,8 @@ def tile_attend_bag_kernel(tc, xT, w, offs, out):
         w_raw = sbuf([P, 4, M], F32, "w_raw")
         nc.scalar.dma_start(first[:, : T // 2], x_rows[:, 2, : T // 2])
         nc.sync.dma_start(first[:, T // 2 :], x_rows[:, 2, T // 2 :])
-        nc.scalar.dma_start(low[:, : T // 2], x_rows[:, 0, : T // 2])
         nc.sync.dma_start(offsets[:], offs)
+        nc.scalar.dma_start(low[:, : T // 2], x_rows[:, 0, : T // 2])
         nc.sync.dma_start(low[:, T // 2 :], x_rows[:, 0, T // 2 :])
         for c0, c1 in spans(PAIR_PIECES):
             nc.sync.dma_start(pair[:, c0:c1], x_rows[:, 1, c0:c1])
@@ -82,8 +82,8 @@ def tile_attend_bag_kernel(tc, xT, w, offs, out):
             nc.scalar.activation(high, window[:].indirect(listed(i)), COPY)
             add_turned(banks[i][:, t, :], [singles[t, i][:, j, :] for j in range(K)])
 
-        e = [sbuf([P, 4 * B], BF16, f"e{i}") for i in range(4)]
-        lanes = e[3][:].rearrange("p (g t) -> p g t", t=4)
+        e = {i: sbuf([P, 4 * B], BF16, f"e{i}")[:] for i in (0, 1, 3)}
+        lanes = e[3].rearrange("p (g t) -> p g t", t=4)
 
         def reduce_into(lane, terms):
             with nc.allow_low_precision(reason="the sum is float32 inside the instruction and is rounded once"):
@@ -104,8 +104,8 @@ def tile_attend_bag_kernel(tc, xT, w, offs, out):
         for piece, (c0, c1) in zip(staged, spans(LAST_PIECES)):
             nc.scalar.activation(last_bf[:, c0:c1], piece[:], COPY)
 
-        late = sbuf([P, 2 * B * K], U32, "late", "staged1024")
-        got = [sbuf([P, B * K], U32, f"got{i}")[:] for i in range(2)] + [late[:, : B * K], late[:, B * K :]]
+        tags = ("got0", "got1", "staged1024", "staged1792")
+        got = [sbuf([P, B * K], U32, f"got{i}", tags[i])[:] for i in range(4)]
         for i in range(3):
             nc.vector.tensor_copy(got[i], pair[:].bitcast(U32).indirect(listed(i)))
             half = sbuf([P, 2, B, 2], F32, f"half{i}")
@@ -114,8 +114,6 @@ def tile_attend_bag_kernel(tc, xT, w, offs, out):
             if i < 2:
                 for t in range(2):
                     add_turned(banks[i][:, t, :], [half[:, j, :, t] for j in range(2)])
-            else:
-                nc.gpsimd.tensor_tensor(e[i][:].rearrange("p (g t) -> p g t", t=4)[:, :, 0:2], half[:, 0], half[:, 1], ADD)
             single_on_scalar(3, i, last_bf)
         got_last = sbuf([P, B * K], BF16, "got_last")
         nc.vector.tensor_copy(got_last[:], last_bf[:].indirect(listed(3)))
@@ -127,6 +125,8 @@ def tile_attend_bag_kernel(tc, xT, w, offs, out):
         nc.gpsimd.tensor_scalar(
             w_bf[:].rearrange("p (m t) -> p m t", t=4), w_raw[:].rearrange("p t m -> p m t"), 1.0, 0.0, MULT, ADD
         )
+        e[2] = sbuf([P, 4 * B], BF16, "e2", "single3_1")[:]
+        nc.gpsimd.tensor_tensor(e[2].rearrange("p (g t) -> p g t", t=4)[:, :, 0:2], half[:, 0], half[:, 1], ADD)
         turned = []
         for i in range(3):
             turned.append(sbuf([P, 2, P], F32, f"turned{i}"))
@@ -142,7 +142,7 @@ def tile_attend_bag_kernel(tc, xT, w, offs, out):
             for h in range(h0, 2):
                 nc.tensor.transpose(back[:, h, :], turned[i][:, h, :], ident[:])
             nc.scalar.copy(
-                e[i][:].bitcast(F32).rearrange("p (g h) -> p g h", h=2)[:, :, h0:],
+                e[i].bitcast(F32).rearrange("p (g h) -> p g h", h=2)[:, :, h0:],
                 back[:, h0:].rearrange("p h g -> p g h"),
             )
 
@@ -151,9 +151,9 @@ def tile_attend_bag_kernel(tc, xT, w, offs, out):
         nc.vector.quantize_mx(w_codes[:].bitcast(FP8X4), w_scales[:], w_bf[:])
 
         def quantise(i):
-            codes = sbuf([P, B], U32, f"codes{i}")
+            codes = sbuf([P, B], U32, f"codes{i}")[:]
             scales = sbuf([P, B], U8, f"scales{i}")
-            nc.vector.quantize_mx(codes[:].bitcast(FP8X4), scales[:], e[i][:])
+            nc.vector.quantize_mx(codes.bitcast(FP8X4), scales[:], e[i])
             return codes, scales
 
         def multiply(acc, m, codes, scales):
@@ -162,7 +162,7 @@ def tile_attend_bag_kernel(tc, xT, w, offs, out):
                 acc,
                 lhsT=w_codes[:, cols].bitcast(FP8X4),
                 lhsT_scale=w_scales[:, cols],
-                rhs=codes[:].bitcast(FP8X4),
+                rhs=codes.bitcast(FP8X4),
                 rhs_scale=scales[:],
                 start=True,
                 stop=True,

@@ -168,7 +168,24 @@ def tile_attend_bag_kernel(tc, xT, w, offs, out):
                 stop=True,
             )
 
-        for i, tag in ((3, "fwd2"), (0, "fwd0"), (1, "fwd1")):
+        def in_halves(i, tags, engines, stores):
+            quantised = quantise(i)
+            res = sbuf([P, 2, B], F32, f"res{i}")
+            accs = [psum.tile([P, B], F32, name="acc", tag=tag) for tag in tags]
+            for m in range(2):
+                multiply(accs[m][:], m, *quantised)
+            for m in range(2):
+                engines[m](res[:, m, :], accs[m][:])
+                if stores == 2:
+                    nc.sync.dma_start(out_rows[:, m, i * B : (i + 1) * B], res[:, m, :])
+            if stores == 1:
+                nc.sync.dma_start(out_rows[:, :, i * B : (i + 1) * B], res[:])
+
+        def on_scalar(into, acc):
+            nc.scalar.activation(into, acc, COPY)
+
+        in_halves(3, ("fwd2", "back0"), (on_scalar, on_scalar), 2)
+        for i, tag in ((0, "fwd0"), (1, "fwd1")):
             quantised = quantise(i)
             acc = psum.tile([P, 2, B], F32, name="acc", tag=tag)
             for m in range(2):
@@ -176,11 +193,4 @@ def tile_attend_bag_kernel(tc, xT, w, offs, out):
             res = sbuf([P, 2, B], F32, f"res{i}")
             nc.scalar.activation(res[:], acc[:], COPY)
             nc.sync.dma_start(out_rows[:, :, i * B : (i + 1) * B], res[:])
-        quantised = quantise(2)
-        res = sbuf([P, 2, B], F32, "res2")
-        accs = [psum.tile([P, B], F32, name="acc", tag=f"back{m}") for m in range(2)]
-        for m in range(2):
-            multiply(accs[m][:], m, *quantised)
-        nc.scalar.activation(res[:, 0, :], accs[0][:], COPY)
-        nc.vector.tensor_copy(res[:, 1, :], accs[1][:])
-        nc.sync.dma_start(out_rows[:, :, 2 * B : 3 * B], res[:])
+        in_halves(2, ("back1", "back2"), (on_scalar, nc.vector.tensor_copy), 2)

@@ -168,29 +168,20 @@ def tile_attend_bag_kernel(tc, xT, w, offs, out):
                 stop=True,
             )
 
-        def in_halves(i, tags, engines, stores):
-            quantised = quantise(i)
+        def in_halves(i, tags, engines, quantised):
             res = sbuf([P, 2, B], F32, f"res{i}")
             accs = [psum.tile([P, B], F32, name="acc", tag=tag) for tag in tags]
             for m in range(2):
                 multiply(accs[m][:], m, *quantised)
             for m in range(2):
                 engines[m](res[:, m, :], accs[m][:])
-                if stores == 2:
-                    nc.sync.dma_start(out_rows[:, m, i * B : (i + 1) * B], res[:, m, :])
-            if stores == 1:
-                nc.sync.dma_start(out_rows[:, :, i * B : (i + 1) * B], res[:])
+                nc.sync.dma_start(out_rows[:, m, i * B : (i + 1) * B], res[:, m, :])
 
         def on_scalar(into, acc):
             nc.scalar.activation(into, acc, COPY)
 
-        in_halves(3, ("fwd2", "back0"), (on_scalar, on_scalar), 2)
-        for i, tag in ((0, "fwd0"), (1, "fwd1")):
-            quantised = quantise(i)
-            acc = psum.tile([P, 2, B], F32, name="acc", tag=tag)
-            for m in range(2):
-                multiply(acc[:, m, :], m, *quantised)
-            res = sbuf([P, 2, B], F32, f"res{i}")
-            nc.scalar.activation(res[:], acc[:], COPY)
-            nc.sync.dma_start(out_rows[:, :, i * B : (i + 1) * B], res[:])
-        in_halves(2, ("back1", "back2"), (on_scalar, nc.vector.tensor_copy), 2)
+        in_halves(3, ("fwd2", "back0"), (on_scalar, on_scalar), quantise(3))
+        ready = {i: quantise(i) for i in range(3)}
+        in_halves(0, ("fwd0", "spare0"), (nc.vector.tensor_copy, on_scalar), ready[0])
+        in_halves(1, ("fwd1", "spare1"), (nc.vector.tensor_copy, on_scalar), ready[1])
+        in_halves(2, ("back1", "back2"), (on_scalar, nc.vector.tensor_copy), ready[2])

@@ -57,7 +57,8 @@ def tile_attend_bag_kernel(tc, xT, w, offs, out):
         for c0, c1 in spans(LAST_PIECES):
             staged.append(sbuf([P, c1 - c0], F32, f"staged{c0}"))
             nc.sync.dma_start(staged[-1][:], x_rows[:, 3, c0:c1])
-        nc.sync.dma_start(w_raw[:], w_rows)
+        for t in range(0, 4, 2):
+            nc.sync.dma_start(w_raw[:, t : t + 2], w_rows[:, t : t + 2])
 
         ident = keep.tile([P, P], F32, name="ident")
         make_identity(nc, ident[:])
@@ -113,7 +114,8 @@ def tile_attend_bag_kernel(tc, xT, w, offs, out):
             nc.gpsimd.tensor_tensor(half[:].rearrange("p j g t -> p g j t"), v[:, :, 0], v[:, :, 1], ADD)
             if i < 2:
                 for t in range(2):
-                    add_turned(banks[i][:, t, :], [half[:, j, :, t] for j in range(2)])
+                    add_turned(banks[2 * i][:, t, :], [half[:, j, :, t] for j in range(2)])
+        for i in (0, 2, 1):
             single_on_scalar(3, i, last_bf)
         got_last = sbuf([P, B * K], BF16, "got_last")
         nc.vector.tensor_copy(got_last[:], last_bf[:].indirect(listed(3)))
@@ -125,22 +127,22 @@ def tile_attend_bag_kernel(tc, xT, w, offs, out):
         nc.gpsimd.tensor_scalar(
             w_bf[:].rearrange("p (m t) -> p m t", t=4), w_raw[:].rearrange("p t m -> p m t"), 1.0, 0.0, MULT, ADD
         )
-        e[2] = sbuf([P, 4 * B], BF16, "e2", "single3_1")[:]
+        e[2] = sbuf([P, 4 * B], BF16, "e2", "single3_2")[:]
         nc.gpsimd.tensor_tensor(e[2].rearrange("p (g t) -> p g t", t=4)[:, :, 0:2], half[:, 0], half[:, 1], ADD)
-        turned = []
-        for i in range(3):
-            turned.append(sbuf([P, 2, P], F32, f"turned{i}"))
-            h0 = 0 if i < 2 else 1
+        turned = {}
+        for i in (0, 2, 1):
+            turned[i] = sbuf([P, 2, P], F32, f"turned{i}")
+            h0 = 1 if i == 1 else 0
             nc.scalar.activation(
                 turned[i][:, h0:].bitcast(BF16).rearrange("g h (p s) -> g h p s", s=2),
                 banks[i][:, 2 * h0 :].rearrange("g (h s) p -> g h p s", s=2),
                 COPY,
             )
-        for i in range(3):
+        for i in (0, 2, 1):
             back = psum.tile([P, 2, B], F32, name="back", tag=f"back{i}")
             h0 = 0 if i < 2 else 1
             for h in range(h0, 2):
-                nc.tensor.transpose(back[:, h, :], turned[i][:, h, :], ident[:])
+                nc.tensor.transpose(back[:, h, :], turned[i if h else 2 * i][:, h, :], ident[:])
             nc.scalar.copy(
                 e[i].bitcast(F32).rearrange("p (g h) -> p g h", h=2)[:, :, h0:],
                 back[:, h0:].rearrange("p h g -> p g h"),
@@ -168,20 +170,23 @@ def tile_attend_bag_kernel(tc, xT, w, offs, out):
                 stop=True,
             )
 
-        def in_halves(i, tags, engines, quantised):
+        def in_halves(i, tags, engines, quantised, stores=1):
             res = sbuf([P, 2, B], F32, f"res{i}")
             accs = [psum.tile([P, B], F32, name="acc", tag=tag) for tag in tags]
             for m in range(2):
                 multiply(accs[m][:], m, *quantised)
             for m in range(2):
                 engines[m](res[:, m, :], accs[m][:])
-                nc.sync.dma_start(out_rows[:, m, i * B : (i + 1) * B], res[:, m, :])
+                if stores == 2:
+                    nc.sync.dma_start(out_rows[:, m, i * B : (i + 1) * B], res[:, m, :])
+            if stores == 1:
+                nc.sync.dma_start(out_rows[:, :, i * B : (i + 1) * B], res[:])
 
         def on_scalar(into, acc):
             nc.scalar.activation(into, acc, COPY)
 
-        in_halves(3, ("fwd2", "back0"), (on_scalar, on_scalar), quantise(3))
-        ready = {i: quantise(i) for i in range(3)}
+        in_halves(3, ("fwd1", "back0"), (on_scalar, on_scalar), quantise(3), 2)
+        ready = {i: quantise(i) for i in (0, 2, 1)}
         in_halves(0, ("fwd0", "spare0"), (nc.vector.tensor_copy, on_scalar), ready[0])
-        in_halves(1, ("fwd1", "spare1"), (nc.vector.tensor_copy, on_scalar), ready[1])
-        in_halves(2, ("back1", "back2"), (on_scalar, nc.vector.tensor_copy), ready[2])
+        in_halves(2, ("fwd2", "spare1"), (nc.vector.tensor_copy, on_scalar), ready[2])
+        in_halves(1, ("back2", "back1"), (on_scalar, nc.vector.tensor_copy), ready[1])

@@ -19,9 +19,11 @@ MULT = mybir.AluOpType.mult
 COPY = mybir.ActivationFunctionType.Copy
 ALONG = mybir.AxisListType.X
 
-PAIR_PIECES = (512, 512, 512, 256, 256)
+PAIR_PIECES = (1024, 512, 256, 256)
+PAIR_LOADS = ((1, 0, 1024), (0, 1024, 1536), (1, 1024, 1536), (0, 1536, 2048), (1, 1536, 1792), (1, 1792, 2048))
 LAST_PIECES = (512, 512, 512, 256, 256)
 SCALAR_CAST = 640
+VECTOR_CAST = 128
 
 
 def tile_attend_bag_kernel(tc, xT, w, offs, out):
@@ -50,9 +52,8 @@ def tile_attend_bag_kernel(tc, xT, w, offs, out):
         nc.sync.dma_start(first[:, T // 2 :], x_rows[:, 2, T // 2 :])
         nc.sync.dma_start(offsets[:], offs)
         nc.scalar.dma_start(low[:, : T // 2], x_rows[:, 0, : T // 2])
-        nc.sync.dma_start(low[:, T // 2 :], x_rows[:, 0, T // 2 :])
-        for c0, c1 in spans(PAIR_PIECES):
-            nc.sync.dma_start(pair[:, c0:c1], x_rows[:, 1, c0:c1])
+        for plane, c0, c1 in PAIR_LOADS:
+            nc.sync.dma_start((low, pair)[plane][:, c0:c1], x_rows[:, plane, c0:c1])
         staged = []
         for c0, c1 in spans(LAST_PIECES):
             staged.append(sbuf([P, c1 - c0], F32, f"staged{c0}"))
@@ -102,10 +103,13 @@ def tile_attend_bag_kernel(tc, xT, w, offs, out):
         halves = pair[:].bitcast(BF16).rearrange("p (c t) -> p c t", t=2)
         for c0, c1 in spans(PAIR_PIECES):
             nc.vector.tensor_copy(halves[:, c0:c1, 0], low[:, c0:c1])
-        for piece, (c0, c1) in zip(staged, spans(LAST_PIECES)):
-            nc.scalar.activation(last_bf[:, c0:c1], piece[:], COPY)
+        for k, (piece, (c0, c1)) in enumerate(zip(staged, spans(LAST_PIECES))):
+            mine = c1 - c0 - (VECTOR_CAST if k == 2 else 0)
+            nc.scalar.activation(last_bf[:, c0 : c0 + mine], piece[:, :mine], COPY)
+            if k == 2:
+                nc.vector.tensor_copy(last_bf[:, c0 + mine : c1], piece[:, mine:])
 
-        tags = ("got0", "got1", "staged1024", "staged1792")
+        tags = ("got0", "staged512", "staged1024", "staged1792")
         got = [sbuf([P, B * K], U32, f"got{i}", tags[i])[:] for i in range(4)]
         for i in range(3):
             nc.vector.tensor_copy(got[i], pair[:].bitcast(U32).indirect(listed(i)))

@@ -20,7 +20,7 @@ COPY = mybir.ActivationFunctionType.Copy
 ALONG = mybir.AxisListType.X
 
 PAIR_PIECES = (1024, 512, 256, 256)
-PAIR_LOADS = ((1, 0, 1024), (0, 1024, 1536), (1, 1024, 1536), (0, 1536, 2048), (1, 1536, 1792), (1, 1792, 2048))
+PAIR_LOADS = ((1, 0, 512), (1, 512, 1024), (0, 1024, 1536), (1, 1024, 1536), (0, 1536, 2048), (1, 1536, 1792), (1, 1792, 2048))
 LAST_PIECES = (512, 512, 512, 256, 256)
 SCALAR_CAST = 640
 VECTOR_CAST = 128
@@ -49,7 +49,8 @@ def tile_attend_bag_kernel(tc, xT, w, offs, out):
         last_bf = sbuf([P, T], BF16, "last_bf")
         w_raw = sbuf([P, 4, M], F32, "w_raw")
         nc.scalar.dma_start(first[:, : T // 2], x_rows[:, 2, : T // 2])
-        nc.sync.dma_start(first[:, T // 2 :], x_rows[:, 2, T // 2 :])
+        for c0 in (T // 2, 3 * T // 4):
+            nc.sync.dma_start(first[:, c0 : c0 + T // 4], x_rows[:, 2, c0 : c0 + T // 4])
         nc.sync.dma_start(offsets[:], offs)
         nc.scalar.dma_start(low[:, : T // 2], x_rows[:, 0, : T // 2])
         for plane, c0, c1 in PAIR_LOADS:
@@ -91,7 +92,8 @@ def tile_attend_bag_kernel(tc, xT, w, offs, out):
             with nc.allow_low_precision(reason="the sum is float32 inside the instruction and is rounded once"):
                 nc.vector.tensor_reduce(lane, terms, ALONG, ADD)
 
-        nc.vector.tensor_copy(first_bf[:, T // 2 :], first[:, T // 2 :])
+        for c0 in (T // 2, 3 * T // 4):
+            nc.vector.tensor_copy(first_bf[:, c0 : c0 + T // 4], first[:, c0 : c0 + T // 4])
         nc.vector.tensor_copy(first_bf[:, SCALAR_CAST : T // 2], first[:, SCALAR_CAST : T // 2])
         nc.scalar.activation(first_bf[:, :SCALAR_CAST], first[:, :SCALAR_CAST], COPY)
         got_first = sbuf([P, B * K], F32, "got_first")

@@ -23,7 +23,7 @@ PAIR_PIECES = (1024, 512, 256, 256)
 PAIR_LOADS = ((1, 0, 512), (1, 512, 1024), (0, 1024, 1536), (1, 1024, 1536), (0, 1536, 2048), (1, 1536, 1792), (1, 1792, 2048))
 LAST_PIECES = (512, 512, 512, 256, 256)
 SCALAR_CAST = 640
-VECTOR_CAST = 128
+VECTOR_CAST = 192
 
 
 def tile_attend_bag_kernel(tc, xT, w, offs, out):
@@ -65,13 +65,14 @@ def tile_attend_bag_kernel(tc, xT, w, offs, out):
         ident = keep.tile([P, P], F32, name="ident")
         make_identity(nc, ident[:])
 
-        def listed(i):
-            return offsets[:, i * B * K // 16 : (i + 1) * B * K // 16]
+        def listed(i, chunks=1):
+            return offsets[:, i * B * K // 16 : (i + chunks) * B * K // 16]
 
+        runs = {2: ((0, 1), (1, 1), (2, 1)), 3: ((0, 2), (2, 1))}
         singles = {}
         for t in (2, 3):
-            for i in range(3):
-                singles[t, i] = sbuf([P, K, B], F32, f"single{t}_{i}")
+            for i, chunks in runs[t]:
+                singles[t, i] = sbuf([P, chunks, K, B], F32, f"single{t}_{i}")
                 nc.vector.memset(singles[t, i][:], 0.0)
 
         banks = [psum.tile([P, 4, P], F32, name="fwd", tag=f"fwd{i}") for i in range(3)]
@@ -80,12 +81,14 @@ def tile_attend_bag_kernel(tc, xT, w, offs, out):
             for j, term in enumerate(terms):
                 nc.tensor.matmul(into, lhsT=term, rhs=ident[:], is_transpose=True, start=j == 0, stop=j == len(terms) - 1)
 
-        def single_on_scalar(t, i, window):
-            high = singles[t, i][:].bitcast(BF16).rearrange("p j (g s) -> p g j s", s=2)[:, :, :, 1]
-            nc.scalar.activation(high, window[:].indirect(listed(i)), COPY)
-            add_turned(banks[i][:, t, :], [singles[t, i][:, j, :] for j in range(K)])
+        def singles_on_scalar(t, window):
+            for i, chunks in runs[t]:
+                high = singles[t, i][:].bitcast(BF16).rearrange("p c j (g s) -> p c g j s", s=2)[:, :, :, :, 1]
+                nc.scalar.activation(high, window[:].indirect(listed(i, chunks)), COPY)
+                for c in range(chunks):
+                    add_turned(banks[i + c][:, t, :], [singles[t, i][:, c, j, :] for j in range(K)])
 
-        e = {i: sbuf([P, 4 * B], BF16, f"e{i}")[:] for i in (0, 1, 3)}
+        e = {i: sbuf([P, 4 * B], BF16, f"e{i}")[:] for i in (0, 2, 3)}
         lanes = e[3].rearrange("p (g t) -> p g t", t=4)
 
         def reduce_into(lane, terms):
@@ -99,30 +102,29 @@ def tile_attend_bag_kernel(tc, xT, w, offs, out):
         got_first = sbuf([P, B * K], F32, "got_first")
         nc.vector.tensor_copy(got_first[:], first[:].indirect(listed(3)))
         reduce_into(lanes[:, :, 2], got_first[:].rearrange("p (g j) -> p g j", j=K))
-        for i in range(3):
-            single_on_scalar(2, i, first_bf)
+        singles_on_scalar(2, first_bf)
 
         halves = pair[:].bitcast(BF16).rearrange("p (c t) -> p c t", t=2)
+        low_high = low[:].bitcast(BF16).rearrange("p (c t) -> p c t", t=2)
         for c0, c1 in spans(PAIR_PIECES):
-            nc.vector.tensor_copy(halves[:, c0:c1, 0], low[:, c0:c1])
+            nc.vector.tensor_copy(halves[:, c0:c1, 0], low_high[:, c0:c1, 1])
         for k, (piece, (c0, c1)) in enumerate(zip(staged, spans(LAST_PIECES))):
             mine = c1 - c0 - (VECTOR_CAST if k == 2 else 0)
             nc.scalar.activation(last_bf[:, c0 : c0 + mine], piece[:, :mine], COPY)
             if k == 2:
                 nc.vector.tensor_copy(last_bf[:, c0 + mine : c1], piece[:, mine:])
 
-        tags = ("got0", "staged512", "staged1024", "staged1792")
+        tags = ("got0", "staged1024", "staged512", "staged1792")
         got = [sbuf([P, B * K], U32, f"got{i}", tags[i])[:] for i in range(4)]
-        for i in range(3):
+        for i in (0, 2, 1):
             nc.vector.tensor_copy(got[i], pair[:].bitcast(U32).indirect(listed(i)))
             half = sbuf([P, 2, B, 2], F32, f"half{i}")
             v = got[i].bitcast(BF16).rearrange("p (g s j t) -> p g s j t", s=2, j=2, t=2)
             nc.gpsimd.tensor_tensor(half[:].rearrange("p j g t -> p g j t"), v[:, :, 0], v[:, :, 1], ADD)
-            if i < 2:
+            if i != 1:
                 for t in range(2):
-                    add_turned(banks[2 * i][:, t, :], [half[:, j, :, t] for j in range(2)])
-        for i in (0, 2, 1):
-            single_on_scalar(3, i, last_bf)
+                    add_turned(banks[i // 2][:, t, :], [half[:, j, :, t] for j in range(2)])
+        singles_on_scalar(3, last_bf)
         got_last = sbuf([P, B * K], BF16, "got_last")
         nc.vector.tensor_copy(got_last[:], last_bf[:].indirect(listed(3)))
         nc.vector.tensor_copy(got[3], pair[:].bitcast(U32).indirect(listed(3)))
@@ -133,22 +135,22 @@ def tile_attend_bag_kernel(tc, xT, w, offs, out):
         nc.gpsimd.tensor_scalar(
             w_bf[:].rearrange("p (m t) -> p m t", t=4), w_raw[:].rearrange("p t m -> p m t"), 1.0, 0.0, MULT, ADD
         )
-        e[2] = sbuf([P, 4 * B], BF16, "e2", "single3_2")[:]
-        nc.gpsimd.tensor_tensor(e[2].rearrange("p (g t) -> p g t", t=4)[:, :, 0:2], half[:, 0], half[:, 1], ADD)
+        e[1] = sbuf([P, 4 * B], BF16, "e1", "single3_0")[:]
+        nc.gpsimd.tensor_tensor(e[1].rearrange("p (g t) -> p g t", t=4)[:, :, 0:2], half[:, 0], half[:, 1], ADD)
         turned = {}
-        for i in (0, 2, 1):
+        for i in range(3):
             turned[i] = sbuf([P, 2, P], F32, f"turned{i}")
-            h0 = 1 if i == 1 else 0
+            h0 = 1 if i == 2 else 0
             nc.scalar.activation(
                 turned[i][:, h0:].bitcast(BF16).rearrange("g h (p s) -> g h p s", s=2),
                 banks[i][:, 2 * h0 :].rearrange("g (h s) p -> g h p s", s=2),
                 COPY,
             )
-        for i in (0, 2, 1):
+        for i in range(3):
             back = psum.tile([P, 2, B], F32, name="back", tag=f"back{i}")
-            h0 = 0 if i < 2 else 1
+            h0 = 1 if i == 1 else 0
             for h in range(h0, 2):
-                nc.tensor.transpose(back[:, h, :], turned[i if h else 2 * i][:, h, :], ident[:])
+                nc.tensor.transpose(back[:, h, :], turned[i if h else i // 2][:, h, :], ident[:])
             nc.scalar.copy(
                 e[i].bitcast(F32).rearrange("p (g h) -> p g h", h=2)[:, :, h0:],
                 back[:, h0:].rearrange("p h g -> p g h"),
@@ -191,8 +193,8 @@ def tile_attend_bag_kernel(tc, xT, w, offs, out):
         def on_scalar(into, acc):
             nc.scalar.activation(into, acc, COPY)
 
-        in_halves(3, ("fwd1", "back0"), (on_scalar, on_scalar), quantise(3), 2)
-        ready = {i: quantise(i) for i in (0, 2, 1)}
+        in_halves(3, ("fwd2", "back0"), (on_scalar, on_scalar), quantise(3), 2)
+        ready = {i: quantise(i) for i in range(3)}
         in_halves(0, ("fwd0", "spare0"), (nc.vector.tensor_copy, on_scalar), ready[0])
-        in_halves(2, ("fwd2", "spare1"), (nc.vector.tensor_copy, on_scalar), ready[2])
-        in_halves(1, ("back2", "back1"), (on_scalar, nc.vector.tensor_copy), ready[1])
+        in_halves(1, ("fwd1", "spare1"), (nc.vector.tensor_copy, on_scalar), ready[1])
+        in_halves(2, ("back1", "back2"), (on_scalar, nc.vector.tensor_copy), ready[2])

@@ -133,7 +133,12 @@ def tile_attend_bag_kernel(tc, xT, w, offs, out):
 
         w_bf = sbuf([P, M * 4], BF16, "w_bf")
         nc.gpsimd.tensor_scalar(
-            w_bf[:].rearrange("p (m t) -> p m t", t=4), w_raw[:].rearrange("p t m -> p m t"), 1.0, 0.0, MULT, ADD
+            w_bf[:].rearrange("p (c i t) -> p c t i", i=4, t=4),
+            w_raw[:].rearrange("p t (c i) -> p c t i", i=4),
+            1.0,
+            0.0,
+            MULT,
+            ADD,
         )
         e[1] = sbuf([P, 4 * B], BF16, "e1", "single3_0")[:]
         nc.gpsimd.tensor_tensor(e[1].rearrange("p (g t) -> p g t", t=4)[:, :, 0:2], half[:, 0], half[:, 1], ADD)

@@ -20,10 +20,9 @@ COPY = mybir.ActivationFunctionType.Copy
 ALONG = mybir.AxisListType.X
 
 PAIR_PIECES = (1024, 512, 256, 256)
-PAIR_LOADS = ((1, 0, 512), (1, 512, 1024), (0, 1024, 1536), (1, 1024, 1536), (0, 1536, 2048), (1, 1536, 1792), (1, 1792, 2048))
-LAST_PIECES = (512, 512, 512, 256, 256)
+PAIR_LOADS = ((1, 0, 1024), (0, 1024, 1536), (1, 1024, 1536), (0, 1536, 2048), (1, 1536, 1792), (1, 1792, 2048))
+LAST_PIECES = (256,) * 8
 SCALAR_CAST = 640
-VECTOR_CAST = 192
 
 
 def tile_attend_bag_kernel(tc, xT, w, offs, out):
@@ -49,8 +48,7 @@ def tile_attend_bag_kernel(tc, xT, w, offs, out):
         last_bf = sbuf([P, T], BF16, "last_bf")
         w_raw = sbuf([P, 4, M], F32, "w_raw")
         nc.scalar.dma_start(first[:, : T // 2], x_rows[:, 2, : T // 2])
-        for c0 in (T // 2, 3 * T // 4):
-            nc.sync.dma_start(first[:, c0 : c0 + T // 4], x_rows[:, 2, c0 : c0 + T // 4])
+        nc.sync.dma_start(first[:, T // 2 :], x_rows[:, 2, T // 2 :])
         nc.sync.dma_start(offsets[:], offs)
         nc.scalar.dma_start(low[:, : T // 2], x_rows[:, 0, : T // 2])
         for plane, c0, c1 in PAIR_LOADS:
@@ -59,8 +57,7 @@ def tile_attend_bag_kernel(tc, xT, w, offs, out):
         for c0, c1 in spans(LAST_PIECES):
             staged.append(sbuf([P, c1 - c0], F32, f"staged{c0}"))
             nc.sync.dma_start(staged[-1][:], x_rows[:, 3, c0:c1])
-        for t in range(0, 4, 2):
-            nc.sync.dma_start(w_raw[:, t : t + 2], w_rows[:, t : t + 2])
+        nc.sync.dma_start(w_raw[:], w_rows)
 
         ident = keep.tile([P, P], F32, name="ident")
         make_identity(nc, ident[:])
@@ -95,8 +92,7 @@ def tile_attend_bag_kernel(tc, xT, w, offs, out):
             with nc.allow_low_precision(reason="the sum is float32 inside the instruction and is rounded once"):
                 nc.vector.tensor_reduce(lane, terms, ALONG, ADD)
 
-        for c0 in (T // 2, 3 * T // 4):
-            nc.vector.tensor_copy(first_bf[:, c0 : c0 + T // 4], first[:, c0 : c0 + T // 4])
+        nc.vector.tensor_copy(first_bf[:, T // 2 :], first[:, T // 2 :])
         nc.vector.tensor_copy(first_bf[:, SCALAR_CAST : T // 2], first[:, SCALAR_CAST : T // 2])
         nc.scalar.activation(first_bf[:, :SCALAR_CAST], first[:, :SCALAR_CAST], COPY)
         got_first = sbuf([P, B * K], F32, "got_first")
@@ -108,13 +104,10 @@ def tile_attend_bag_kernel(tc, xT, w, offs, out):
         low_high = low[:].bitcast(BF16).rearrange("p (c t) -> p c t", t=2)
         for c0, c1 in spans(PAIR_PIECES):
             nc.vector.tensor_copy(halves[:, c0:c1, 0], low_high[:, c0:c1, 1])
-        for k, (piece, (c0, c1)) in enumerate(zip(staged, spans(LAST_PIECES))):
-            mine = c1 - c0 - (VECTOR_CAST if k == 2 else 0)
-            nc.scalar.activation(last_bf[:, c0 : c0 + mine], piece[:, :mine], COPY)
-            if k == 2:
-                nc.vector.tensor_copy(last_bf[:, c0 + mine : c1], piece[:, mine:])
+        for piece, (c0, c1) in zip(staged, spans(LAST_PIECES)):
+            nc.scalar.activation(last_bf[:, c0:c1], piece[:], COPY)
 
-        tags = ("got0", "staged1024", "staged512", "staged1792")
+        tags = ("got0", "staged1024", "got2", "staged1792")
         got = [sbuf([P, B * K], U32, f"got{i}", tags[i])[:] for i in range(4)]
         for i in (0, 2, 1):
             nc.vector.tensor_copy(got[i], pair[:].bitcast(U32).indirect(listed(i)))

@@ -96,14 +96,21 @@ def tile_attend_bag_kernel(tc, xT, w, offs, out):
         nc.vector.tensor_copy(first_bf[:, SCALAR_CAST : T // 2], first[:, SCALAR_CAST : T // 2])
         nc.scalar.activation(first_bf[:, :SCALAR_CAST], first[:, :SCALAR_CAST], COPY)
         got_first = sbuf([P, B * K], F32, "got_first")
-        nc.vector.tensor_copy(got_first[:], first[:].indirect(listed(3)))
-        reduce_into(lanes[:, :, 2], got_first[:].rearrange("p (g j) -> p g j", j=K))
+        H = B // 2
+        for c in range(2):
+            cols = slice(c * H * K // 16, (c + 1) * H * K // 16)
+            nc.vector.tensor_copy(got_first[:, c * H * K : (c + 1) * H * K], first[:].indirect(listed(3)[:, cols]))
+        reduce_into(lanes[:, :H, 2], got_first[:, : H * K].rearrange("p (g j) -> p g j", j=K))
         singles_on_scalar(2, first_bf)
 
         halves = pair[:].bitcast(BF16).rearrange("p (c t) -> p c t", t=2)
         low_high = low[:].bitcast(BF16).rearrange("p (c t) -> p c t", t=2)
         for c0, c1 in spans(PAIR_PIECES):
             nc.vector.tensor_copy(halves[:, c0:c1, 0], low_high[:, c0:c1, 1])
+        half_first = sbuf([P, H, 2], F32, "half_first", "low")
+        v = got_first[:, H * K :].rearrange("p (g s j) -> p g s j", s=2, j=2)
+        nc.gpsimd.tensor_tensor(half_first[:], v[:, :, 0], v[:, :, 1], ADD)
+        nc.gpsimd.tensor_tensor(lanes[:, H:, 2], half_first[:, :, 0], half_first[:, :, 1], ADD)
         for piece, (c0, c1) in zip(staged, spans(LAST_PIECES)):
             nc.scalar.activation(last_bf[:, c0:c1], piece[:], COPY)
 
@@ -118,7 +125,7 @@ def tile_attend_bag_kernel(tc, xT, w, offs, out):
                 for t in range(2):
                     add_turned(banks[i // 2][:, t, :], [half[:, j, :, t] for j in range(2)])
         singles_on_scalar(3, last_bf)
-        got_last = sbuf([P, B * K], BF16, "got_last")
+        got_last = sbuf([P, B * K], BF16, "got_last", "low")
         nc.vector.tensor_copy(got_last[:], last_bf[:].indirect(listed(3)))
         nc.vector.tensor_copy(got[3], pair[:].bitcast(U32).indirect(listed(3)))
         reduce_into(lanes[:, :, 3], got_last[:].rearrange("p (g j) -> p g j", j=K))

@@ -145,10 +145,10 @@ def tile_attend_bag_kernel(tc, xT, w, offs, out):
         turned = {}
         for i in range(3):
             turned[i] = sbuf([P, 2, P], F32, f"turned{i}")
-            h0 = 1 if i == 2 else 0
+        for i, h0, h1 in ((0, 0, 2), (1, 1, 2), (1, 0, 1), (2, 1, 2)):
             nc.scalar.activation(
-                turned[i][:, h0:].bitcast(BF16).rearrange("g h (p s) -> g h p s", s=2),
-                banks[i][:, 2 * h0 :].rearrange("g (h s) p -> g h p s", s=2),
+                turned[i][:, h0:h1].bitcast(BF16).rearrange("g h (p s) -> g h p s", s=2),
+                banks[i][:, 2 * h0 : 2 * h1].rearrange("g (h s) p -> g h p s", s=2),
                 COPY,
             )
         for i in range(3):

@@ -161,9 +161,11 @@ def tile_attend_bag_kernel(tc, xT, w, offs, out):
                 back[:, h0:].rearrange("p h g -> p g h"),
             )
 
-        w_codes = sbuf([P, M], U32, "w_codes")
-        w_scales = sbuf([P, M], U8, "w_scales")
-        nc.vector.quantize_mx(w_codes[:].bitcast(FP8X4), w_scales[:], w_bf[:])
+        w_codes = [sbuf([P, P], U32, f"w_codes{m}") for m in range(2)]
+        w_scales = [sbuf([P, P], U8, f"w_scales{m}") for m in range(2)]
+
+        def quantise_w(m):
+            nc.vector.quantize_mx(w_codes[m][:].bitcast(FP8X4), w_scales[m][:], w_bf[:, m * 4 * P : (m + 1) * 4 * P])
 
         def quantise(i):
             codes = sbuf([P, B], U32, f"codes{i}")[:]
@@ -172,11 +174,10 @@ def tile_attend_bag_kernel(tc, xT, w, offs, out):
             return codes, scales
 
         def multiply(acc, m, codes, scales):
-            cols = slice(m * P, (m + 1) * P)
             nc.tensor.matmul_mx(
                 acc,
-                lhsT=w_codes[:, cols].bitcast(FP8X4),
-                lhsT_scale=w_scales[:, cols],
+                lhsT=w_codes[m][:].bitcast(FP8X4),
+                lhsT_scale=w_scales[m][:],
                 rhs=codes.bitcast(FP8X4),
                 rhs_scale=scales[:],
                 start=True,
@@ -198,7 +199,10 @@ def tile_attend_bag_kernel(tc, xT, w, offs, out):
         def on_scalar(into, acc):
             nc.scalar.activation(into, acc, COPY)
 
-        in_halves(3, ("fwd2", "back0"), (on_scalar, on_scalar), quantise(3), 2)
+        quantise_w(0)
+        last_codes = quantise(3)
+        quantise_w(1)
+        in_halves(3, ("fwd2", "back0"), (on_scalar, on_scalar), last_codes, 2)
         ready = {i: quantise(i) for i in range(3)}
         in_halves(0, ("fwd0", "spare0"), (nc.vector.tensor_copy, on_scalar), ready[0])
         in_halves(1, ("fwd1", "spare1"), (nc.vector.tensor_copy, on_scalar), ready[1])

@@ -22,6 +22,7 @@ ALONG = mybir.AxisListType.X
 PAIR_PIECES = (1024, 512, 256, 256)
 PAIR_LOADS = ((1, 0, 1024), (0, 1024, 1536), (1, 1024, 1536), (0, 1536, 2048), (1, 1536, 1792), (1, 1792, 2048))
 LAST_PIECES = (256,) * 8
+VECTOR_CAST = 128
 SCALAR_CAST = 640
 
 
@@ -111,8 +112,10 @@ def tile_attend_bag_kernel(tc, xT, w, offs, out):
         v = got_first[:, H * K :].rearrange("p (g s j) -> p g s j", s=2, j=2)
         nc.gpsimd.tensor_tensor(half_first[:], v[:, :, 0], v[:, :, 1], ADD)
         nc.gpsimd.tensor_tensor(lanes[:, H:, 2], half_first[:, :, 0], half_first[:, :, 1], ADD)
+        nc.vector.tensor_copy(last_bf[:, :VECTOR_CAST], staged[0][:, :VECTOR_CAST])
         for piece, (c0, c1) in zip(staged, spans(LAST_PIECES)):
-            nc.scalar.activation(last_bf[:, c0:c1], piece[:], COPY)
+            skip = max(VECTOR_CAST - c0, 0)
+            nc.scalar.activation(last_bf[:, c0 + skip : c1], piece[:, skip:], COPY)
 
         tags = ("got0", "staged1024", "got2", "staged1792")
         got = [sbuf([P, B * K], U32, f"got{i}", tags[i])[:] for i in range(4)]

@@ -97,21 +97,14 @@ def tile_attend_bag_kernel(tc, xT, w, offs, out):
         nc.vector.tensor_copy(first_bf[:, SCALAR_CAST : T // 2], first[:, SCALAR_CAST : T // 2])
         nc.scalar.activation(first_bf[:, :SCALAR_CAST], first[:, :SCALAR_CAST], COPY)
         got_first = sbuf([P, B * K], F32, "got_first")
-        H = B // 2
-        for c in range(2):
-            cols = slice(c * H * K // 16, (c + 1) * H * K // 16)
-            nc.vector.tensor_copy(got_first[:, c * H * K : (c + 1) * H * K], first[:].indirect(listed(3)[:, cols]))
-        reduce_into(lanes[:, :H, 2], got_first[:, : H * K].rearrange("p (g j) -> p g j", j=K))
+        nc.vector.tensor_copy(got_first[:], first[:].indirect(listed(3)))
+        reduce_into(lanes[:, :, 2], got_first[:].rearrange("p (g j) -> p g j", j=K))
         singles_on_scalar(2, first_bf)
 
         halves = pair[:].bitcast(BF16).rearrange("p (c t) -> p c t", t=2)
         low_high = low[:].bitcast(BF16).rearrange("p (c t) -> p c t", t=2)
         for c0, c1 in spans(PAIR_PIECES):
             nc.vector.tensor_copy(halves[:, c0:c1, 0], low_high[:, c0:c1, 1])
-        half_first = sbuf([P, H, 2], F32, "half_first", "low")
-        v = got_first[:, H * K :].rearrange("p (g s j) -> p g s j", s=2, j=2)
-        nc.gpsimd.tensor_tensor(half_first[:], v[:, :, 0], v[:, :, 1], ADD)
-        nc.gpsimd.tensor_tensor(lanes[:, H:, 2], half_first[:, :, 0], half_first[:, :, 1], ADD)
         nc.vector.tensor_copy(last_bf[:, :VECTOR_CAST], staged[0][:, :VECTOR_CAST])
         for piece, (c0, c1) in zip(staged, spans(LAST_PIECES)):
             skip = max(VECTOR_CAST - c0, 0)
@@ -128,7 +121,7 @@ def tile_attend_bag_kernel(tc, xT, w, offs, out):
                 for t in range(2):
                     add_turned(banks[i // 2][:, t, :], [half[:, j, :, t] for j in range(2)])
         singles_on_scalar(3, last_bf)
-        got_last = sbuf([P, B * K], BF16, "got_last", "low")
+        got_last = sbuf([P, B * K], BF16, "got_last")
         nc.vector.tensor_copy(got_last[:], last_bf[:].indirect(listed(3)))
         nc.vector.tensor_copy(got[3], pair[:].bitcast(U32).indirect(listed(3)))
         reduce_into(lanes[:, :, 3], got_last[:].rearrange("p (g j) -> p g j", j=K))

@@ -66,7 +66,7 @@ def tile_attend_bag_kernel(tc, xT, w, offs, out):
         def listed(i, chunks=1):
             return offsets[:, i * B * K // 16 : (i + chunks) * B * K // 16]
 
-        runs = {2: ((0, 1), (1, 1), (2, 1)), 3: ((0, 2), (2, 1))}
+        runs = {2: ((0, 2), (2, 1)), 3: ((0, 2), (2, 1))}
         singles = {}
         for t in (2, 3):
             for i, chunks in runs[t]:

@@ -19,17 +19,16 @@ MULT = mybir.AluOpType.mult
 COPY = mybir.ActivationFunctionType.Copy
 ALONG = mybir.AxisListType.X
 
-PAIR_PIECES = (1024, 512, 256, 256)
+FULL, MIXED, LATE, PLAIN = 0, 1, 2, 3
 PAIR_LOADS = ((1, 0, 1024), (0, 1024, 1536), (1, 1024, 1536), (0, 1536, 2048), (1, 1536, 1792), (1, 1792, 2048))
-LAST_PIECES = (256,) * 8
-VECTOR_CAST = 128
+PIECE = 256
 SCALAR_CAST = 640
+VECTOR_CAST = 128
 
 
 def tile_attend_bag_kernel(tc, xT, w, offs, out):
     nc = tc.nc
     x_rows = xT.rearrange("(p t) c -> p t c", t=4)
-    w_rows = w.rearrange("(p t) m -> p t m", t=4)
     out_rows = out.rearrange("(m p) g -> p m g", m=2)
     with ExitStack() as ctx:
         keep = ctx.enter_context(tc.tile_pool(name="keep", bufs=1))
@@ -37,9 +36,6 @@ def tile_attend_bag_kernel(tc, xT, w, offs, out):
 
         def sbuf(shape, dtype, name, tag=None):
             return keep.tile(shape, dtype, name=name, tag=tag or name, align_bytes=256)
-
-        def spans(pieces):
-            return [(sum(pieces[:i]), sum(pieces[: i + 1])) for i in range(len(pieces))]
 
         offsets = keep.tile([P, G * K // 16], U16, name="offsets")
         first = sbuf([P, T], F32, "first")
@@ -54,40 +50,42 @@ def tile_attend_bag_kernel(tc, xT, w, offs, out):
         nc.scalar.dma_start(low[:, : T // 2], x_rows[:, 0, : T // 2])
         for plane, c0, c1 in PAIR_LOADS:
             nc.sync.dma_start((low, pair)[plane][:, c0:c1], x_rows[:, plane, c0:c1])
-        staged = []
-        for c0, c1 in spans(LAST_PIECES):
-            staged.append(sbuf([P, c1 - c0], F32, f"staged{c0}"))
-            nc.sync.dma_start(staged[-1][:], x_rows[:, 3, c0:c1])
-        nc.sync.dma_start(w_raw[:], w_rows)
+        staged = {}
+        for c0 in range(0, T, PIECE):
+            staged[c0] = sbuf([P, PIECE], F32, f"staged{c0}")
+            nc.sync.dma_start(staged[c0][:], x_rows[:, 3, c0 : c0 + PIECE])
+        nc.sync.dma_start(w_raw[:], w.rearrange("(p t) m -> p t m", t=4))
 
         ident = keep.tile([P, P], F32, name="ident")
         make_identity(nc, ident[:])
 
-        def listed(i, chunks=1):
-            return offsets[:, i * B * K // 16 : (i + chunks) * B * K // 16]
+        def listed(g0, g1):
+            return offsets[:, g0 * K // 16 : g1 * K // 16]
 
-        runs = {2: ((0, 2), (2, 1)), 3: ((0, 2), (2, 1))}
-        singles = {}
+        runs = ((FULL, 2), (LATE, 1))
+        padded = {}
         for t in (2, 3):
-            for i, chunks in runs[t]:
-                singles[t, i] = sbuf([P, chunks, K, B], F32, f"single{t}_{i}")
-                nc.vector.memset(singles[t, i][:], 0.0)
+            for i, chunks in runs:
+                padded[t, i] = sbuf([P, chunks, K, B], F32, f"single{t}_{i}")
+                nc.vector.memset(padded[t, i][:], 0.0)
 
-        banks = [psum.tile([P, 4, P], F32, name="fwd", tag=f"fwd{i}") for i in range(3)]
+        banks = {i: psum.tile([P, 4, P], F32, name="fwd", tag=f"fwd{i}") for i in (FULL, MIXED, LATE)}
+        pair_bank = {FULL: FULL, LATE: MIXED}
 
         def add_turned(into, terms):
             for j, term in enumerate(terms):
                 nc.tensor.matmul(into, lhsT=term, rhs=ident[:], is_transpose=True, start=j == 0, stop=j == len(terms) - 1)
 
         def singles_on_scalar(t, window):
-            for i, chunks in runs[t]:
-                high = singles[t, i][:].bitcast(BF16).rearrange("p c j (g s) -> p c g j s", s=2)[:, :, :, :, 1]
-                nc.scalar.activation(high, window[:].indirect(listed(i, chunks)), COPY)
+            for i, chunks in runs:
+                high = padded[t, i][:].bitcast(BF16).rearrange("p c j (g s) -> p c g j s", s=2)[:, :, :, :, 1]
+                nc.scalar.activation(high, window[:].indirect(listed(i * B, (i + chunks) * B)), COPY)
                 for c in range(chunks):
-                    add_turned(banks[i + c][:, t, :], [singles[t, i][:, c, j, :] for j in range(K)])
+                    add_turned(banks[i + c][:, t, :], [padded[t, i][:, c, j, :] for j in range(K)])
 
-        e = {i: sbuf([P, 4 * B], BF16, f"e{i}")[:] for i in (0, 2, 3)}
-        lanes = e[3].rearrange("p (g t) -> p g t", t=4)
+        e = {i: sbuf([P, 4 * B], BF16, f"e{i}")[:] for i in (FULL, LATE, PLAIN)}
+        lanes = e[PLAIN].rearrange("p (g t) -> p g t", t=4)
+        plain = listed(PLAIN * B, G)
 
         def reduce_into(lane, terms):
             with nc.allow_low_precision(reason="the sum is float32 inside the instruction and is rounded once"):
@@ -97,35 +95,40 @@ def tile_attend_bag_kernel(tc, xT, w, offs, out):
         nc.vector.tensor_copy(first_bf[:, SCALAR_CAST : T // 2], first[:, SCALAR_CAST : T // 2])
         nc.scalar.activation(first_bf[:, :SCALAR_CAST], first[:, :SCALAR_CAST], COPY)
         got_first = sbuf([P, B * K], F32, "got_first")
-        nc.vector.tensor_copy(got_first[:], first[:].indirect(listed(3)))
+        nc.vector.tensor_copy(got_first[:], first[:].indirect(plain))
         reduce_into(lanes[:, :, 2], got_first[:].rearrange("p (g j) -> p g j", j=K))
         singles_on_scalar(2, first_bf)
 
-        halves = pair[:].bitcast(BF16).rearrange("p (c t) -> p c t", t=2)
-        low_high = low[:].bitcast(BF16).rearrange("p (c t) -> p c t", t=2)
-        for c0, c1 in spans(PAIR_PIECES):
-            nc.vector.tensor_copy(halves[:, c0:c1, 0], low_high[:, c0:c1, 1])
+        pair_halves = pair[:].bitcast(BF16).rearrange("p (c s) -> p c s", s=2)
+        low_halves = low[:].bitcast(BF16).rearrange("p (c s) -> p c s", s=2)
+        for plane, c0, c1 in PAIR_LOADS:
+            if plane == 1:
+                nc.vector.tensor_copy(pair_halves[:, c0:c1, 0], low_halves[:, c0:c1, 1])
         nc.vector.tensor_copy(last_bf[:, :VECTOR_CAST], staged[0][:, :VECTOR_CAST])
-        for piece, (c0, c1) in zip(staged, spans(LAST_PIECES)):
-            skip = max(VECTOR_CAST - c0, 0)
-            nc.scalar.activation(last_bf[:, c0 + skip : c1], piece[:, skip:], COPY)
+        for c0, piece in staged.items():
+            done = 0 if c0 else VECTOR_CAST
+            nc.scalar.activation(last_bf[:, c0 + done : c0 + PIECE], piece[:, done:], COPY)
 
-        tags = ("got0", "staged1024", "got2", "staged1792")
-        got = [sbuf([P, B * K], U32, f"got{i}", tags[i])[:] for i in range(4)]
-        for i in (0, 2, 1):
-            nc.vector.tensor_copy(got[i], pair[:].bitcast(U32).indirect(listed(i)))
-            half = sbuf([P, 2, B, 2], F32, f"half{i}")
-            v = got[i].bitcast(BF16).rearrange("p (g s j t) -> p g s j t", s=2, j=2, t=2)
-            nc.gpsimd.tensor_tensor(half[:].rearrange("p j g t -> p g j t"), v[:, :, 0], v[:, :, 1], ADD)
-            if i != 1:
+        def gather_pair(name, g0, g1, tag=None):
+            got = sbuf([P, (g1 - g0) * K], U32, name, tag)[:]
+            nc.vector.tensor_copy(got, pair[:].bitcast(U32).indirect(listed(g0, g1)))
+            return got.bitcast(BF16)
+
+        for i in (FULL, LATE, MIXED):
+            bags = B
+            got = gather_pair(f"got{i}", i * B, i * B + bags, f"staged{T // 2}" if i == MIXED else None)
+            terms = got.rearrange("p (g s j t) -> p g s j t", s=2, j=2, t=2)
+            half = sbuf([P, 2, bags, 2], F32, f"half{i}")
+            nc.gpsimd.tensor_tensor(half[:].rearrange("p j g t -> p g j t"), terms[:, :, 0], terms[:, :, 1], ADD)
+            if i in pair_bank:
                 for t in range(2):
-                    add_turned(banks[i // 2][:, t, :], [half[:, j, :, t] for j in range(2)])
+                    add_turned(banks[pair_bank[i]][:, t, :], [half[:, j, :, t] for j in range(2)])
         singles_on_scalar(3, last_bf)
         got_last = sbuf([P, B * K], BF16, "got_last")
-        nc.vector.tensor_copy(got_last[:], last_bf[:].indirect(listed(3)))
-        nc.vector.tensor_copy(got[3], pair[:].bitcast(U32).indirect(listed(3)))
+        nc.vector.tensor_copy(got_last[:], last_bf[:].indirect(plain))
+        got = gather_pair("got_plain", PLAIN * B, G, f"staged{T - PIECE}")
         reduce_into(lanes[:, :, 3], got_last[:].rearrange("p (g j) -> p g j", j=K))
-        reduce_into(lanes[:, :, 0:2], got[3].bitcast(BF16).rearrange("p (g j t) -> p g t j", j=K, t=2))
+        reduce_into(lanes[:, :, 0:2], got.rearrange("p (g j t) -> p g t j", j=K, t=2))
 
         w_bf = sbuf([P, M * 4], BF16, "w_bf")
         nc.gpsimd.tensor_scalar(
@@ -136,70 +139,63 @@ def tile_attend_bag_kernel(tc, xT, w, offs, out):
             MULT,
             ADD,
         )
-        e[1] = sbuf([P, 4 * B], BF16, "e1", "single3_0")[:]
-        nc.gpsimd.tensor_tensor(e[1].rearrange("p (g t) -> p g t", t=4)[:, :, 0:2], half[:, 0], half[:, 1], ADD)
-        turned = {}
-        for i in range(3):
-            turned[i] = sbuf([P, 2, P], F32, f"turned{i}")
-        for i, h0, h1 in ((0, 0, 2), (1, 1, 2), (1, 0, 1), (2, 1, 2)):
+        e[MIXED] = sbuf([P, 4 * B], BF16, f"e{MIXED}", f"single3_{FULL}")[:]
+        nc.gpsimd.tensor_tensor(e[MIXED].rearrange("p (g t) -> p g t", t=4)[:, :, 0:2], half[:, 0], half[:, 1], ADD)
+
+        turned = {i: sbuf([P, 2, P], F32, f"turned{i}") for i in banks}
+        for i, h0, h1 in ((FULL, 0, 2), (MIXED, 1, 2), (MIXED, 0, 1), (LATE, 1, 2)):
             nc.scalar.activation(
                 turned[i][:, h0:h1].bitcast(BF16).rearrange("g h (p s) -> g h p s", s=2),
                 banks[i][:, 2 * h0 : 2 * h1].rearrange("g (h s) p -> g h p s", s=2),
                 COPY,
             )
-        for i in range(3):
+        for i in banks:
             back = psum.tile([P, 2, B], F32, name="back", tag=f"back{i}")
-            h0 = 1 if i == 1 else 0
+            h0 = 0 if i in pair_bank else 1
             for h in range(h0, 2):
-                nc.tensor.transpose(back[:, h, :], turned[i if h else i // 2][:, h, :], ident[:])
+                nc.tensor.transpose(back[:, h, :], turned[i if h else pair_bank[i]][:, h, :], ident[:])
             nc.scalar.copy(
                 e[i].bitcast(F32).rearrange("p (g h) -> p g h", h=2)[:, :, h0:],
                 back[:, h0:].rearrange("p h g -> p g h"),
             )
 
-        w_codes = [sbuf([P, P], U32, f"w_codes{m}") for m in range(2)]
-        w_scales = [sbuf([P, P], U8, f"w_scales{m}") for m in range(2)]
-
-        def quantise_w(m):
-            nc.vector.quantize_mx(w_codes[m][:].bitcast(FP8X4), w_scales[m][:], w_bf[:, m * 4 * P : (m + 1) * 4 * P])
-
-        def quantise(i):
-            codes = sbuf([P, B], U32, f"codes{i}")[:]
-            scales = sbuf([P, B], U8, f"scales{i}")
-            nc.vector.quantize_mx(codes.bitcast(FP8X4), scales[:], e[i])
+        def quantise(name, values):
+            codes = sbuf([P, P], U32, f"{name}_codes")[:].bitcast(FP8X4)
+            scales = sbuf([P, P], U8, f"{name}_scales")[:]
+            nc.vector.quantize_mx(codes, scales, values)
             return codes, scales
-
-        def multiply(acc, m, codes, scales):
-            nc.tensor.matmul_mx(
-                acc,
-                lhsT=w_codes[m][:].bitcast(FP8X4),
-                lhsT_scale=w_scales[m][:],
-                rhs=codes.bitcast(FP8X4),
-                rhs_scale=scales[:],
-                start=True,
-                stop=True,
-            )
-
-        def in_halves(i, tags, engines, quantised, stores=1):
-            res = sbuf([P, 2, B], F32, f"res{i}")
-            accs = [psum.tile([P, B], F32, name="acc", tag=tag) for tag in tags]
-            for m in range(2):
-                multiply(accs[m][:], m, *quantised)
-            for m in range(2):
-                engines[m](res[:, m, :], accs[m][:])
-                if stores == 2:
-                    nc.sync.dma_start(out_rows[:, m, i * B : (i + 1) * B], res[:, m, :])
-            if stores == 1:
-                nc.sync.dma_start(out_rows[:, :, i * B : (i + 1) * B], res[:])
 
         def on_scalar(into, acc):
             nc.scalar.activation(into, acc, COPY)
 
-        quantise_w(0)
-        last_codes = quantise(3)
-        quantise_w(1)
-        in_halves(3, ("fwd2", "back0"), (on_scalar, on_scalar), last_codes, 2)
-        ready = {i: quantise(i) for i in range(3)}
-        in_halves(0, ("fwd0", "spare0"), (nc.vector.tensor_copy, on_scalar), ready[0])
-        in_halves(1, ("fwd1", "spare1"), (nc.vector.tensor_copy, on_scalar), ready[1])
-        in_halves(2, ("back1", "back2"), (on_scalar, nc.vector.tensor_copy), ready[2])
+        def product(i, tags, engines, stores):
+            res = sbuf([P, 2, B], F32, f"res{i}")
+            accs = [psum.tile([P, B], F32, name="acc", tag=tag) for tag in tags]
+            for m in range(2):
+                nc.tensor.matmul_mx(
+                    accs[m][:],
+                    lhsT=w_mx[m][0],
+                    lhsT_scale=w_mx[m][1],
+                    rhs=e_mx[i][0],
+                    rhs_scale=e_mx[i][1],
+                    start=True,
+                    stop=True,
+                )
+            rows = out_rows[:, :, i * B : (i + 1) * B]
+            for m in range(2):
+                engines[m](res[:, m, :], accs[m][:])
+                if stores == 2:
+                    nc.sync.dma_start(rows[:, m, :], res[:, m, :])
+            if stores == 1:
+                nc.sync.dma_start(rows, res[:])
+
+        on_vector = nc.vector.tensor_copy
+        w_mx = [quantise("w0", w_bf[:, : 4 * P])]
+        e_mx = {PLAIN: quantise(f"e{PLAIN}", e[PLAIN])}
+        w_mx.append(quantise("w1", w_bf[:, 4 * P :]))
+        product(PLAIN, (f"fwd{LATE}", f"back{FULL}"), (on_scalar, on_scalar), 2)
+        for i in banks:
+            e_mx[i] = quantise(f"e{i}", e[i])
+        product(FULL, (f"fwd{FULL}", "spare0"), (on_vector, on_scalar), 1)
+        product(MIXED, (f"fwd{MIXED}", "spare1"), (on_vector, on_scalar), 1)
+        product(LATE, (f"back{MIXED}", f"back{LATE}"), (on_scalar, on_vector), 1)

@@ -37,7 +37,7 @@ def tile_attend_bag_kernel(tc, xT, w, offs, out):
         def sbuf(shape, dtype, name, tag=None):
             return keep.tile(shape, dtype, name=name, tag=tag or name, align_bytes=256)
 
-        offsets = keep.tile([P, G * K // 16], U16, name="offsets")
+        offsets = sbuf([P, G * K // 16], U16, "offsets")
         first = sbuf([P, T], F32, "first")
         first_bf = sbuf([P, T], BF16, "first_bf")
         low = sbuf([P, T], F32, "low")
@@ -56,7 +56,7 @@ def tile_attend_bag_kernel(tc, xT, w, offs, out):
             nc.sync.dma_start(staged[c0][:], x_rows[:, 3, c0 : c0 + PIECE])
         nc.sync.dma_start(w_raw[:], w.rearrange("(p t) m -> p t m", t=4))
 
-        ident = keep.tile([P, P], F32, name="ident")
+        ident = sbuf([P, P], F32, "ident")
         make_identity(nc, ident[:])
 
         def listed(g0, g1):

@@ -23,7 +23,6 @@ FULL, MIXED, LATE, PLAIN = 0, 1, 2, 3
 PAIR_LOADS = ((1, 0, 1024), (0, 1024, 1536), (1, 1024, 1536), (0, 1536, 2048), (1, 1536, 1792), (1, 1792, 2048))
 PIECE = 256
 SCALAR_CAST = 640
-VECTOR_CAST = 128
 
 
 def tile_attend_bag_kernel(tc, xT, w, offs, out):
@@ -104,10 +103,8 @@ def tile_attend_bag_kernel(tc, xT, w, offs, out):
         for plane, c0, c1 in PAIR_LOADS:
             if plane == 1:
                 nc.vector.tensor_copy(pair_halves[:, c0:c1, 0], low_halves[:, c0:c1, 1])
-        nc.vector.tensor_copy(last_bf[:, :VECTOR_CAST], staged[0][:, :VECTOR_CAST])
         for c0, piece in staged.items():
-            done = 0 if c0 else VECTOR_CAST
-            nc.scalar.activation(last_bf[:, c0 + done : c0 + PIECE], piece[:, done:], COPY)
+            nc.scalar.activation(last_bf[:, c0 : c0 + PIECE], piece[:], COPY)
 
         def gather_pair(name, g0, g1, tag=None):
             got = sbuf([P, (g1 - g0) * K], U32, name, tag)[:]

@@ -195,4 +195,4 @@ def tile_attend_bag_kernel(tc, xT, w, offs, out):
             e_mx[i] = quantise(f"e{i}", e[i])
         product(FULL, (f"fwd{FULL}", "spare0"), (on_vector, on_scalar), 1)
         product(MIXED, (f"fwd{MIXED}", "spare1"), (on_vector, on_scalar), 1)
-        product(LATE, (f"back{MIXED}", f"back{LATE}"), (on_scalar, on_vector), 1)
+        product(LATE, (f"back{MIXED}", f"back{LATE}"), (on_vector, on_scalar), 1)

@@ -140,7 +140,7 @@ def tile_attend_bag_kernel(tc, xT, w, offs, out):
         nc.gpsimd.tensor_tensor(e[MIXED].rearrange("p (g t) -> p g t", t=4)[:, :, 0:2], half[:, 0], half[:, 1], ADD)
 
         turned = {i: sbuf([P, 2, P], F32, f"turned{i}") for i in banks}
-        for i, h0, h1 in ((FULL, 0, 2), (MIXED, 1, 2), (MIXED, 0, 1), (LATE, 1, 2)):
+        for i, h0, h1 in ((FULL, 0, 2), (MIXED, 0, 2), (LATE, 1, 2)):
             nc.scalar.activation(
                 turned[i][:, h0:h1].bitcast(BF16).rearrange("g h (p s) -> g h p s", s=2),
                 banks[i][:, 2 * h0 : 2 * h1].rearrange("g (h s) p -> g h p s", s=2),

@@ -78,9 +78,10 @@ def tile_attend_bag_kernel(tc, xT, w, offs, out):
         def singles_on_scalar(t, window):
             for i, chunks in runs:
                 high = padded[t, i][:].bitcast(BF16).rearrange("p c j (g s) -> p c g j s", s=2)[:, :, :, :, 1]
-                nc.scalar.activation(high, window[:].indirect(listed(i * B, (i + chunks) * B)), COPY)
-                for c in range(chunks):
-                    add_turned(banks[i + c][:, t, :], [padded[t, i][:, c, j, :] for j in range(K)])
+                for c0, c1 in ((0, chunks),) if t == 2 else [(c, c + 1) for c in range(chunks)]:
+                    nc.scalar.activation(high[:, c0:c1], window[:].indirect(listed((i + c0) * B, (i + c1) * B)), COPY)
+                    for c in range(c0, c1):
+                        add_turned(banks[i + c][:, t, :], [padded[t, i][:, c, j, :] for j in range(K)])
 
         e = {i: sbuf([P, 4 * B], BF16, f"e{i}")[:] for i in (FULL, LATE, PLAIN)}
         lanes = e[PLAIN].rearrange("p (g t) -> p g t", t=4)
@@ -140,7 +141,7 @@ def tile_attend_bag_kernel(tc, xT, w, offs, out):
         nc.gpsimd.tensor_tensor(e[MIXED].rearrange("p (g t) -> p g t", t=4)[:, :, 0:2], half[:, 0], half[:, 1], ADD)
 
         turned = {i: sbuf([P, 2, P], F32, f"turned{i}") for i in banks}
-        for i, h0, h1 in ((FULL, 0, 2), (MIXED, 0, 2), (LATE, 1, 2)):
+        for i, h0, h1 in ((FULL, 0, 2), (MIXED, 1, 2), (MIXED, 0, 1), (LATE, 1, 2)):
             nc.scalar.activation(
                 turned[i][:, h0:h1].bitcast(BF16).rearrange("g h (p s) -> g h p s", s=2),
                 banks[i][:, 2 * h0 : 2 * h1].rearrange("g (h s) p -> g h p s", s=2),
@@ -156,8 +157,8 @@ def tile_attend_bag_kernel(tc, xT, w, offs, out):
                 back[:, h0:].rearrange("p h g -> p g h"),
             )
 
-        def quantise(name, values):
-            codes = sbuf([P, P], U32, f"{name}_codes")[:].bitcast(FP8X4)
+        def quantise(name, values, tag=None):
+            codes = sbuf([P, P], U32, f"{name}_codes", tag)[:].bitcast(FP8X4)
             scales = sbuf([P, P], U8, f"{name}_scales")[:]
             nc.vector.quantize_mx(codes, scales, values)
             return codes, scales
@@ -189,7 +190,7 @@ def tile_attend_bag_kernel(tc, xT, w, offs, out):
         on_vector = nc.vector.tensor_copy
         w_mx = [quantise("w0", w_bf[:, : 4 * P])]
         e_mx = {PLAIN: quantise(f"e{PLAIN}", e[PLAIN])}
-        w_mx.append(quantise("w1", w_bf[:, 4 * P :]))
+        w_mx.append(quantise("w1", w_bf[:, 4 * P :], f"staged{T - PIECE}"))
         product(PLAIN, (f"fwd{LATE}", f"back{FULL}"), (on_scalar, on_scalar), 2)
         for i in banks:
             e_mx[i] = quantise(f"e{i}", e[i])

@@ -19,10 +19,7 @@ MULT = mybir.AluOpType.mult
 COPY = mybir.ActivationFunctionType.Copy
 ALONG = mybir.AxisListType.X
 
-FULL, MIXED, LATE, PLAIN = 0, 1, 2, 3
-PAIR_LOADS = ((1, 0, 1024), (0, 1024, 1536), (1, 1024, 1536), (0, 1536, 2048), (1, 1536, 1792), (1, 1792, 2048))
-PIECE = 256
-SCALAR_CAST = 640
+EARLY, LATE, SUMMED, REDUCED = 0, 1, 2, 3
 
 
 def tile_attend_bag_kernel(tc, xT, w, offs, out):
@@ -37,125 +34,72 @@ def tile_attend_bag_kernel(tc, xT, w, offs, out):
             return keep.tile(shape, dtype, name=name, tag=tag or name, align_bytes=256)
 
         offsets = sbuf([P, G * K // 16], U16, "offsets")
-        first = sbuf([P, T], F32, "first")
-        first_bf = sbuf([P, T], BF16, "first_bf")
-        low = sbuf([P, T], F32, "low")
-        pair = sbuf([P, T], F32, "pair")
-        last_bf = sbuf([P, T], BF16, "last_bf")
+        planes = [sbuf([P, T], F32, f"plane{t}") for t in range(4)]
         w_raw = sbuf([P, 4, M], F32, "w_raw")
-        nc.scalar.dma_start(first[:, : T // 2], x_rows[:, 2, : T // 2])
-        nc.sync.dma_start(first[:, T // 2 :], x_rows[:, 2, T // 2 :])
+        H = T // 2
+        nc.scalar.dma_start(planes[0][:, :H], x_rows[:, 0, :H])
+        nc.sync.dma_start(planes[0][:, H:], x_rows[:, 0, H:])
         nc.sync.dma_start(offsets[:], offs)
-        nc.scalar.dma_start(low[:, : T // 2], x_rows[:, 0, : T // 2])
-        for plane, c0, c1 in PAIR_LOADS:
-            nc.sync.dma_start((low, pair)[plane][:, c0:c1], x_rows[:, plane, c0:c1])
-        staged = {}
-        for c0 in range(0, T, PIECE):
-            staged[c0] = sbuf([P, PIECE], F32, f"staged{c0}")
-            nc.sync.dma_start(staged[c0][:], x_rows[:, 3, c0 : c0 + PIECE])
+        nc.scalar.dma_start(planes[1][:, :H], x_rows[:, 1, :H])
+        nc.sync.dma_start(planes[1][:, H:], x_rows[:, 1, H:])
+        for t in (2, 3):
+            nc.sync.dma_start(planes[t][:], x_rows[:, t, :])
         nc.sync.dma_start(w_raw[:], w.rearrange("(p t) m -> p t m", t=4))
 
         ident = sbuf([P, P], F32, "ident")
         make_identity(nc, ident[:])
 
-        def listed(g0, g1):
-            return offsets[:, g0 * K // 16 : g1 * K // 16]
+        warm = sbuf([P, 16], F32, "warm")
+        nc.vector.memset(warm[:, :8], 0.0)
+        nc.scalar.activation(warm[:, 8:], warm[:, :8], COPY)
 
-        runs = ((FULL, 2), (LATE, 1))
-        padded = {}
-        for t in (2, 3):
-            for i, chunks in runs:
-                padded[t, i] = sbuf([P, chunks, K, B], F32, f"single{t}_{i}")
-                nc.vector.memset(padded[t, i][:], 0.0)
+        def listed(i):
+            return offsets[:, i * B * K // 16 : (i + 1) * B * K // 16]
 
-        banks = {i: psum.tile([P, 4, P], F32, name="fwd", tag=f"fwd{i}") for i in (FULL, MIXED, LATE)}
-        pair_bank = {FULL: FULL, LATE: MIXED}
+        early_bank = psum.tile([P, 4, P], F32, name="fwd", tag="bank0")
+        late_banks = [psum.tile([P, 2, P], F32, name="fwd", tag=f"bank{1 + h}") for h in range(2)]
+        e = {i: sbuf([P, 4 * B], BF16, f"e{i}")[:] for i in range(4)}
+        lanes = {i: e[i].rearrange("p (g t) -> p g t", t=4) for i in range(4)}
+        halves = {i: sbuf([P, 4, B, 2], F32, f"halves{i}") for i in (SUMMED, REDUCED)}
 
-        def add_turned(into, terms):
-            for j, term in enumerate(terms):
-                nc.tensor.matmul(into, lhsT=term, rhs=ident[:], is_transpose=True, start=j == 0, stop=j == len(terms) - 1)
+        def gather_and_turn(t, i):
+            dealt = sbuf([P, K, B], F32, f"dealt{t}_{i}")
+            nc.vector.tensor_copy(dealt[:].rearrange("p j g -> p g j"), planes[t][:].indirect(listed(i)))
+            into = early_bank[:, t, :] if i == EARLY else late_banks[t // 2][:, t % 2, :]
+            for j in range(K):
+                nc.tensor.matmul(into, lhsT=dealt[:, j, :], rhs=ident[:], is_transpose=True, start=j == 0, stop=j == K - 1)
 
-        def singles_on_scalar(t, window):
-            for i, chunks in runs:
-                high = padded[t, i][:].bitcast(BF16).rearrange("p c j (g s) -> p c g j s", s=2)[:, :, :, :, 1]
-                for c0, c1 in ((0, chunks),) if t == 2 else [(c, c + 1) for c in range(chunks)]:
-                    nc.scalar.activation(high[:, c0:c1], window[:].indirect(listed((i + c0) * B, (i + c1) * B)), COPY)
-                    for c in range(c0, c1):
-                        add_turned(banks[i + c][:, t, :], [padded[t, i][:, c, j, :] for j in range(K)])
+        def gather_listed(t, i):
+            got = sbuf([P, B * K], BF16, f"got{t}_{i}")
+            nc.scalar.activation(got[:], planes[t][:].indirect(listed(i)), COPY)
+            return got[:]
 
-        e = {i: sbuf([P, 4 * B], BF16, f"e{i}")[:] for i in (FULL, LATE, PLAIN)}
-        lanes = e[PLAIN].rearrange("p (g t) -> p g t", t=4)
-        plain = listed(PLAIN * B, G)
+        def halve(t, i):
+            terms = gather_listed(t, i).rearrange("p (g s j) -> p g s j", s=2, j=2)
+            nc.gpsimd.tensor_tensor(halves[i][:, t], terms[:, :, 0], terms[:, :, 1], ADD)
+
+        def finish(i, t0):
+            both = halves[i][:, t0 : t0 + 2].rearrange("p t g j -> p g t j")
+            nc.gpsimd.tensor_tensor(lanes[i][:, :, t0 : t0 + 2], both[:, :, :, 0], both[:, :, :, 1], ADD)
 
         def reduce_into(lane, terms):
             with nc.allow_low_precision(reason="the sum is float32 inside the instruction and is rounded once"):
                 nc.vector.tensor_reduce(lane, terms, ALONG, ADD)
 
-        nc.vector.tensor_copy(first_bf[:, T // 2 :], first[:, T // 2 :])
-        nc.vector.tensor_copy(first_bf[:, SCALAR_CAST : T // 2], first[:, SCALAR_CAST : T // 2])
-        nc.scalar.activation(first_bf[:, :SCALAR_CAST], first[:, :SCALAR_CAST], COPY)
-        got_first = sbuf([P, B * K], F32, "got_first")
-        nc.vector.tensor_copy(got_first[:], first[:].indirect(plain))
-        reduce_into(lanes[:, :, 2], got_first[:].rearrange("p (g j) -> p g j", j=K))
-        singles_on_scalar(2, first_bf)
-
-        pair_halves = pair[:].bitcast(BF16).rearrange("p (c s) -> p c s", s=2)
-        low_halves = low[:].bitcast(BF16).rearrange("p (c s) -> p c s", s=2)
-        for plane, c0, c1 in PAIR_LOADS:
-            if plane == 1:
-                nc.vector.tensor_copy(pair_halves[:, c0:c1, 0], low_halves[:, c0:c1, 1])
-        for c0, piece in staged.items():
-            nc.scalar.activation(last_bf[:, c0 : c0 + PIECE], piece[:], COPY)
-
-        def gather_pair(name, g0, g1, tag=None):
-            got = sbuf([P, (g1 - g0) * K], U32, name, tag)[:]
-            nc.vector.tensor_copy(got, pair[:].bitcast(U32).indirect(listed(g0, g1)))
-            return got.bitcast(BF16)
-
-        for i in (FULL, LATE, MIXED):
-            bags = B
-            got = gather_pair(f"got{i}", i * B, i * B + bags, f"staged{T // 2}" if i == MIXED else None)
-            terms = got.rearrange("p (g s j t) -> p g s j t", s=2, j=2, t=2)
-            half = sbuf([P, 2, bags, 2], F32, f"half{i}")
-            nc.gpsimd.tensor_tensor(half[:].rearrange("p j g t -> p g j t"), terms[:, :, 0], terms[:, :, 1], ADD)
-            if i in pair_bank:
-                for t in range(2):
-                    add_turned(banks[pair_bank[i]][:, t, :], [half[:, j, :, t] for j in range(2)])
-        singles_on_scalar(3, last_bf)
-        got_last = sbuf([P, B * K], BF16, "got_last")
-        nc.vector.tensor_copy(got_last[:], last_bf[:].indirect(plain))
-        got = gather_pair("got_plain", PLAIN * B, G, f"staged{T - PIECE}")
-        reduce_into(lanes[:, :, 3], got_last[:].rearrange("p (g j) -> p g j", j=K))
-        reduce_into(lanes[:, :, 0:2], got.rearrange("p (g j t) -> p g t j", j=K, t=2))
-
-        w_bf = sbuf([P, M * 4], BF16, "w_bf")
-        nc.gpsimd.tensor_scalar(
-            w_bf[:].rearrange("p (c i t) -> p c t i", i=4, t=4),
-            w_raw[:].rearrange("p t (c i) -> p c t i", i=4),
-            1.0,
-            0.0,
-            MULT,
-            ADD,
-        )
-        e[MIXED] = sbuf([P, 4 * B], BF16, f"e{MIXED}", f"single3_{FULL}")[:]
-        nc.gpsimd.tensor_tensor(e[MIXED].rearrange("p (g t) -> p g t", t=4)[:, :, 0:2], half[:, 0], half[:, 1], ADD)
-
-        turned = {i: sbuf([P, 2, P], F32, f"turned{i}") for i in banks}
-        for i, h0, h1 in ((FULL, 0, 2), (MIXED, 1, 2), (MIXED, 0, 1), (LATE, 1, 2)):
-            nc.scalar.activation(
-                turned[i][:, h0:h1].bitcast(BF16).rearrange("g h (p s) -> g h p s", s=2),
-                banks[i][:, 2 * h0 : 2 * h1].rearrange("g (h s) p -> g h p s", s=2),
-                COPY,
-            )
-        for i in banks:
-            back = psum.tile([P, 2, B], F32, name="back", tag=f"back{i}")
-            h0 = 0 if i in pair_bank else 1
-            for h in range(h0, 2):
-                nc.tensor.transpose(back[:, h, :], turned[i if h else pair_bank[i]][:, h, :], ident[:])
-            nc.scalar.copy(
-                e[i].bitcast(F32).rearrange("p (g h) -> p g h", h=2)[:, :, h0:],
-                back[:, h0:].rearrange("p h g -> p g h"),
-            )
+        for t in range(3):
+            for i in (EARLY, LATE):
+                gather_and_turn(t, i)
+                halve(t, i + 2)
+            if t == 1:
+                for i in (SUMMED, REDUCED):
+                    finish(i, 0)
+        gather_and_turn(3, EARLY)
+        halve(3, SUMMED)
+        finish(SUMMED, 2)
+        gather_and_turn(3, LATE)
+        got = gather_listed(3, REDUCED)
+        reduce_into(lanes[REDUCED][:, :, 2], halves[REDUCED][:, 2])
+        reduce_into(lanes[REDUCED][:, :, 3], got.rearrange("p (g j) -> p g j", j=K))
 
         def quantise(name, values, tag=None):
             codes = sbuf([P, P], U32, f"{name}_codes", tag)[:].bitcast(FP8X4)
@@ -166,34 +110,37 @@ def tile_attend_bag_kernel(tc, xT, w, offs, out):
         def on_scalar(into, acc):
             nc.scalar.activation(into, acc, COPY)
 
-        def product(i, tags, engines, stores):
+        on_vector = nc.vector.tensor_copy
+        turned = {i: sbuf([P, 2, P], F32, f"turned{i}", "got3_2" if i == LATE else None) for i in (EARLY, LATE)}
+        for into, sums in ((turned[EARLY][:], early_bank), (turned[LATE][:, :1], late_banks[0]), (turned[LATE][:, 1:], late_banks[1])):
+            on_scalar(
+                into.bitcast(BF16).rearrange("g h (p s) -> g h p s", s=2),
+                sums[:].rearrange("g (h s) p -> g h p s", s=2),
+            )
+        for i in (EARLY, LATE):
+            back = psum.tile([P, 2, B], F32, name="back", tag=f"bank{i}")
+            for h in range(2):
+                nc.tensor.transpose(back[:, h, :], turned[i][:, h, :], ident[:])
+            nc.scalar.copy(e[i].bitcast(F32).rearrange("p (g h) -> p g h", h=2), back[:].rearrange("p h g -> p g h"))
+
+        w_tile = sbuf([P, 2, 4 * P], BF16, "w_bf", f"halves{SUMMED}")
+        w_bf = [w_tile[:, m] for m in range(2)]
+        for m in range(2):
+            nc.vector.tensor_copy(
+                w_bf[m].rearrange("p (c i t) -> p c t i", i=4, t=4),
+                w_raw[:, :, m * P : (m + 1) * P].rearrange("p t (c i) -> p c t i", i=4),
+            )
+        e_mx = {REDUCED: quantise(f"e{REDUCED}", e[REDUCED], "w_raw")}
+        w_mx = [quantise(f"w{m}", w_bf[m]) for m in range(2)]
+        for i in (SUMMED, EARLY, LATE):
+            e_mx[i] = quantise(f"e{i}", e[i], None)
+        for n, i in enumerate((REDUCED, SUMMED, EARLY, LATE)):
             res = sbuf([P, 2, B], F32, f"res{i}")
-            accs = [psum.tile([P, B], F32, name="acc", tag=tag) for tag in tags]
+            accs = [psum.tile([P, B], F32, name="acc", tag=f"bank{(3 + 2 * n + m) % 8}") for m in range(2)]
             for m in range(2):
                 nc.tensor.matmul_mx(
-                    accs[m][:],
-                    lhsT=w_mx[m][0],
-                    lhsT_scale=w_mx[m][1],
-                    rhs=e_mx[i][0],
-                    rhs_scale=e_mx[i][1],
-                    start=True,
-                    stop=True,
+                    accs[m][:], lhsT=w_mx[m][0], lhsT_scale=w_mx[m][1], rhs=e_mx[i][0], rhs_scale=e_mx[i][1], start=True, stop=True
                 )
-            rows = out_rows[:, :, i * B : (i + 1) * B]
-            for m in range(2):
-                engines[m](res[:, m, :], accs[m][:])
-                if stores == 2:
-                    nc.sync.dma_start(rows[:, m, :], res[:, m, :])
-            if stores == 1:
-                nc.sync.dma_start(rows, res[:])
-
-        on_vector = nc.vector.tensor_copy
-        w_mx = [quantise("w0", w_bf[:, : 4 * P])]
-        e_mx = {PLAIN: quantise(f"e{PLAIN}", e[PLAIN])}
-        w_mx.append(quantise("w1", w_bf[:, 4 * P :], f"staged{T - PIECE}"))
-        product(PLAIN, (f"fwd{LATE}", f"back{FULL}"), (on_scalar, on_scalar), 2)
-        for i in banks:
-            e_mx[i] = quantise(f"e{i}", e[i])
-        product(FULL, (f"fwd{FULL}", "spare0"), (on_vector, on_scalar), 1)
-        product(MIXED, (f"fwd{MIXED}", "spare1"), (on_vector, on_scalar), 1)
-        product(LATE, (f"back{MIXED}", f"back{LATE}"), (on_vector, on_scalar), 1)
+            on_vector(res[:, 0, :], accs[0][:])
+            on_scalar(res[:, 1, :], accs[1][:])
+            nc.sync.dma_start(out_rows[:, :, i * B : (i + 1) * B], res[:])

@@ -28,10 +28,14 @@ def tile_attend_bag_kernel(tc, xT, w, offs, out):
     out_rows = out.rearrange("(m p) g -> p m g", m=2)
     with ExitStack() as ctx:
         keep = ctx.enter_context(tc.tile_pool(name="keep", bufs=1))
+        reused = ctx.enter_context(tc.tile_pool(name="reused", bufs=1))
         psum = ctx.enter_context(tc.psum_pool(name="psum", bufs=1))
 
         def sbuf(shape, dtype, name, tag=None):
             return keep.tile(shape, dtype, name=name, tag=tag or name, align_bytes=256)
+
+        def laid(shape, dtype, name, offset):
+            return reused.tile(shape, dtype, name=name, offset=offset, align_bytes=256)
 
         offsets = sbuf([P, G * K // 16], U16, "offsets")
         planes = [sbuf([P, T], F32, f"plane{t}") for t in range(4)]
@@ -53,53 +57,67 @@ def tile_attend_bag_kernel(tc, xT, w, offs, out):
         nc.vector.memset(warm[:, :8], 0.0)
         nc.scalar.activation(warm[:, 8:], warm[:, :8], COPY)
 
-        def listed(i):
-            return offsets[:, i * B * K // 16 : (i + 1) * B * K // 16]
+        def listed(i0, i1):
+            return offsets[:, i0 * B * K // 16 : i1 * B * K // 16]
 
         early_bank = psum.tile([P, 4, P], F32, name="fwd", tag="bank0")
         late_banks = [psum.tile([P, 2, P], F32, name="fwd", tag=f"bank{1 + h}") for h in range(2)]
-        e = {i: sbuf([P, 4 * B], BF16, f"e{i}")[:] for i in range(4)}
-        lanes = {i: e[i].rearrange("p (g t) -> p g t", t=4) for i in range(4)}
-        halves = {i: sbuf([P, 4, B, 2], F32, f"halves{i}") for i in (SUMMED, REDUCED)}
+        e_turned = {i: sbuf([P, 4 * B], BF16, f"e{i}")[:] for i in (EARLY, LATE)}
+        e_placed = sbuf([P, 2, 4 * B], BF16, "e_placed")
+        e = {EARLY: e_turned[EARLY], LATE: e_turned[LATE], SUMMED: e_placed[:, 0], REDUCED: e_placed[:, 1]}
+        lanes = e_placed[:].rearrange("p c (g t) -> p (c g) t", t=4)
+        first_halves = laid([P, 2, 2 * B, 2], F32, "first_halves", 0)
+        last_halves = laid([P, 3 * B, 2], F32, "last_halves", 0)
 
-        def gather_and_turn(t, i):
-            dealt = sbuf([P, K, B], F32, f"dealt{t}_{i}")
-            nc.vector.tensor_copy(dealt[:].rearrange("p j g -> p g j"), planes[t][:].indirect(listed(i)))
-            into = early_bank[:, t, :] if i == EARLY else late_banks[t // 2][:, t % 2, :]
-            for j in range(K):
-                nc.tensor.matmul(into, lhsT=dealt[:, j, :], rhs=ident[:], is_transpose=True, start=j == 0, stop=j == K - 1)
+        def gather_and_turn(t, i0, i1):
+            dealt = sbuf([P, i1 - i0, K, B], F32, f"dealt{t}_{i0}")
+            nc.vector.tensor_copy(dealt[:].rearrange("p c j g -> p c g j"), planes[t][:].indirect(listed(i0, i1)))
+            for i in range(i0, i1):
+                into = early_bank[:, t, :] if i == EARLY else late_banks[t // 2][:, t % 2, :]
+                for j in range(K):
+                    nc.tensor.matmul(
+                        into, lhsT=dealt[:, i - i0, j, :], rhs=ident[:], is_transpose=True, start=j == 0, stop=j == K - 1
+                    )
 
-        def gather_listed(t, i):
-            got = sbuf([P, B * K], BF16, f"got{t}_{i}")
-            nc.scalar.activation(got[:], planes[t][:].indirect(listed(i)), COPY)
-            return got[:]
+        got = {}
 
-        def halve(t, i):
-            terms = gather_listed(t, i).rearrange("p (g s j) -> p g s j", s=2, j=2)
-            nc.gpsimd.tensor_tensor(halves[i][:, t], terms[:, :, 0], terms[:, :, 1], ADD)
+        def gather_listed(t, i0, i1, into=None):
+            got[t, i0] = (into or sbuf([P, (i1 - i0) * B * K], BF16, f"got{t}_{i0}"))[:]
+            nc.scalar.activation(got[t, i0], planes[t][:].indirect(listed(i0, i1)), COPY)
 
-        def finish(i, t0):
-            both = halves[i][:, t0 : t0 + 2].rearrange("p t g j -> p g t j")
-            nc.gpsimd.tensor_tensor(lanes[i][:, :, t0 : t0 + 2], both[:, :, :, 0], both[:, :, :, 1], ADD)
+        def halve(t, i0, i1):
+            bags = slice((i0 - SUMMED) * B, (i1 - SUMMED) * B)
+            into = first_halves[:, t, bags] if t < 2 else last_halves[:, bags] if t == 2 else last_halves[:, 2 * B :]
+            terms = got[t, i0].rearrange("p (g s j) -> p g s j", s=2, j=2)
+            nc.gpsimd.tensor_tensor(into, terms[:, :, 0], terms[:, :, 1], ADD)
+
+        def finish(into, both):
+            both = both.rearrange("p t g j -> p g t j")
+            nc.gpsimd.tensor_tensor(into, both[:, :, :, 0], both[:, :, :, 1], ADD)
 
         def reduce_into(lane, terms):
             with nc.allow_low_precision(reason="the sum is float32 inside the instruction and is rounded once"):
                 nc.vector.tensor_reduce(lane, terms, ALONG, ADD)
 
-        for t in range(3):
-            for i in (EARLY, LATE):
-                gather_and_turn(t, i)
-                halve(t, i + 2)
-            if t == 1:
-                for i in (SUMMED, REDUCED):
-                    finish(i, 0)
-        gather_and_turn(3, EARLY)
-        halve(3, SUMMED)
-        finish(SUMMED, 2)
-        gather_and_turn(3, LATE)
-        got = gather_listed(3, REDUCED)
-        reduce_into(lanes[REDUCED][:, :, 2], halves[REDUCED][:, 2])
-        reduce_into(lanes[REDUCED][:, :, 3], got.rearrange("p (g j) -> p g j", j=K))
+        gather_and_turn(0, 0, 2)
+        gather_listed(0, 2, 4)
+        halve(0, 2, 4)
+        gather_and_turn(1, 0, 2)
+        for i in (SUMMED, REDUCED):
+            gather_listed(1, i, i + 1)
+            halve(1, i, i + 1)
+        finish(lanes[:, :, 0:2], first_halves[:])
+        gather_and_turn(2, 0, 2)
+        gather_listed(2, 2, 4)
+        halve(2, 2, 4)
+        gather_and_turn(3, EARLY, EARLY + 1)
+        gather_listed(3, SUMMED, SUMMED + 1)
+        halve(3, SUMMED, SUMMED + 1)
+        finish(lanes[:, :B, 2:4], last_halves[:].rearrange("p (t g) j -> p t g j", g=B)[:, 0:3:2])
+        gather_and_turn(3, LATE, LATE + 1)
+        gather_listed(3, REDUCED, REDUCED + 1, laid([P, B * K], BF16, "got_last", 3 * B * 8))
+        reduce_into(lanes[:, B:, 2], last_halves[:, B : 2 * B])
+        reduce_into(lanes[:, B:, 3], got[3, REDUCED].rearrange("p (g j) -> p g j", j=K))
 
         def quantise(name, values, tag=None):
             codes = sbuf([P, P], U32, f"{name}_codes", tag)[:].bitcast(FP8X4)
@@ -111,7 +129,7 @@ def tile_attend_bag_kernel(tc, xT, w, offs, out):
             nc.scalar.activation(into, acc, COPY)
 
         on_vector = nc.vector.tensor_copy
-        turned = {i: sbuf([P, 2, P], F32, f"turned{i}", "got3_2" if i == LATE else None) for i in (EARLY, LATE)}
+        turned = {i: sbuf([P, 2, P], F32, f"turned{i}", "dealt3_0" if i == LATE else None) for i in (EARLY, LATE)}
         for into, sums in ((turned[EARLY][:], early_bank), (turned[LATE][:, :1], late_banks[0]), (turned[LATE][:, 1:], late_banks[1])):
             on_scalar(
                 into.bitcast(BF16).rearrange("g h (p s) -> g h p s", s=2),
@@ -123,24 +141,36 @@ def tile_attend_bag_kernel(tc, xT, w, offs, out):
                 nc.tensor.transpose(back[:, h, :], turned[i][:, h, :], ident[:])
             nc.scalar.copy(e[i].bitcast(F32).rearrange("p (g h) -> p g h", h=2), back[:].rearrange("p h g -> p g h"))
 
-        w_tile = sbuf([P, 2, 4 * P], BF16, "w_bf", f"halves{SUMMED}")
+        w_tile = sbuf([P, 2, 4 * P], BF16, "w_bf", f"got3_{SUMMED}")
         w_bf = [w_tile[:, m] for m in range(2)]
         for m in range(2):
             nc.vector.tensor_copy(
                 w_bf[m].rearrange("p (c i t) -> p c t i", i=4, t=4),
                 w_raw[:, :, m * P : (m + 1) * P].rearrange("p t (c i) -> p c t i", i=4),
             )
-        e_mx = {REDUCED: quantise(f"e{REDUCED}", e[REDUCED], "w_raw")}
         w_mx = [quantise(f"w{m}", w_bf[m]) for m in range(2)]
-        for i in (SUMMED, EARLY, LATE):
-            e_mx[i] = quantise(f"e{i}", e[i], None)
-        for n, i in enumerate((REDUCED, SUMMED, EARLY, LATE)):
-            res = sbuf([P, 2, B], F32, f"res{i}")
-            accs = [psum.tile([P, B], F32, name="acc", tag=f"bank{(3 + 2 * n + m) % 8}") for m in range(2)]
+        e_mx = {i: quantise(f"e{i}", e[i], "w_raw" if i == REDUCED else None) for i in (SUMMED, REDUCED, EARLY, LATE)}
+
+        def product(i, tags, engines, stores, tag=None):
+            res = sbuf([P, 2, B], F32, f"res{i}", tag)
+            accs = [psum.tile([P, 2 // len(tags), B], F32, name="acc", tag=tag) for tag in tags]
             for m in range(2):
                 nc.tensor.matmul_mx(
-                    accs[m][:], lhsT=w_mx[m][0], lhsT_scale=w_mx[m][1], rhs=e_mx[i][0], rhs_scale=e_mx[i][1], start=True, stop=True
+                    accs[m * len(tags) // 2][:, m % (2 // len(tags))],
+                    lhsT=w_mx[m][0],
+                    lhsT_scale=w_mx[m][1],
+                    rhs=e_mx[i][0],
+                    rhs_scale=e_mx[i][1],
+                    start=True,
+                    stop=True,
                 )
-            on_vector(res[:, 0, :], accs[0][:])
-            on_scalar(res[:, 1, :], accs[1][:])
-            nc.sync.dma_start(out_rows[:, :, i * B : (i + 1) * B], res[:])
+            for n, engine in enumerate(engines):
+                engine(res[:, n : n + 2 // len(tags)], accs[n][:])
+            for n in range(stores):
+                rows = slice(2 * n // stores, 2 * (n + 1) // stores)
+                nc.sync.dma_start(out_rows[:, rows, i * B : (i + 1) * B], res[:, rows])
+
+        product(SUMMED, ("bank2",), (on_scalar,), 1)
+        product(REDUCED, ("bank0",), (on_scalar,), 1)
+        product(EARLY, ("bank3", "bank4"), (on_vector, on_scalar), 1)
+        product(LATE, ("bank5", "bank6"), (on_vector, on_scalar), 1)

@@ -19,7 +19,8 @@ MULT = mybir.AluOpType.mult
 COPY = mybir.ActivationFunctionType.Copy
 ALONG = mybir.AxisListType.X
 
-EARLY, LATE, SUMMED, REDUCED = 0, 1, 2, 3
+EARLY, LATE = 0, 1
+PLACED = (2, 3)
 
 
 def tile_attend_bag_kernel(tc, xT, w, offs, out):
@@ -39,7 +40,7 @@ def tile_attend_bag_kernel(tc, xT, w, offs, out):
 
         offsets = sbuf([P, G * K // 16], U16, "offsets")
         planes = [sbuf([P, T], F32, f"plane{t}") for t in range(4)]
-        w_raw = sbuf([P, 4, M], F32, "w_raw")
+        w_raw = laid([P, 4, M], F32, "w_raw", 4096)
         H = T // 2
         nc.scalar.dma_start(planes[0][:, :H], x_rows[:, 0, :H])
         nc.sync.dma_start(planes[0][:, H:], x_rows[:, 0, H:])
@@ -62,12 +63,10 @@ def tile_attend_bag_kernel(tc, xT, w, offs, out):
 
         early_bank = psum.tile([P, 4, P], F32, name="fwd", tag="bank0")
         late_banks = [psum.tile([P, 2, P], F32, name="fwd", tag=f"bank{1 + h}") for h in range(2)]
-        e_turned = {i: sbuf([P, 4 * B], BF16, f"e{i}")[:] for i in (EARLY, LATE)}
         e_placed = sbuf([P, 2, 4 * B], BF16, "e_placed")
-        e = {EARLY: e_turned[EARLY], LATE: e_turned[LATE], SUMMED: e_placed[:, 0], REDUCED: e_placed[:, 1]}
-        lanes = e_placed[:].rearrange("p c (g t) -> p (c g) t", t=4)
-        first_halves = laid([P, 2, 2 * B, 2], F32, "first_halves", 0)
-        last_halves = laid([P, 3 * B, 2], F32, "last_halves", 0)
+        e = {i: sbuf([P, 4 * B], BF16, f"e{i}")[:] for i in (EARLY, LATE)}
+        e.update({i: e_placed[:, i - 2] for i in PLACED})
+        lanes = e_placed[:].rearrange("p c (g t) -> p c g t", t=4)
 
         def gather_and_turn(t, i0, i1):
             dealt = sbuf([P, i1 - i0, K, B], F32, f"dealt{t}_{i0}")
@@ -79,48 +78,49 @@ def tile_attend_bag_kernel(tc, xT, w, offs, out):
                         into, lhsT=dealt[:, i - i0, j, :], rhs=ident[:], is_transpose=True, start=j == 0, stop=j == K - 1
                     )
 
-        got = {}
-
         def gather_listed(t, i0, i1, into=None):
-            got[t, i0] = (into or sbuf([P, (i1 - i0) * B * K], BF16, f"got{t}_{i0}"))[:]
-            nc.scalar.activation(got[t, i0], planes[t][:].indirect(listed(i0, i1)), COPY)
+            got = (into or sbuf([P, (i1 - i0) * B * K], BF16, f"got{t}_{i0}"))[:]
+            nc.scalar.activation(got, planes[t][:].indirect(listed(i0, i1)), COPY)
+            return got
 
-        def halve(t, i0, i1):
-            bags = slice((i0 - SUMMED) * B, (i1 - SUMMED) * B)
-            into = first_halves[:, t, bags] if t < 2 else last_halves[:, bags] if t == 2 else last_halves[:, 2 * B :]
-            terms = got[t, i0].rearrange("p (g s j) -> p g s j", s=2, j=2)
+        def halve(into, got):
+            terms = got.rearrange("p (g s j) -> p g s j", s=2, j=2)
             nc.gpsimd.tensor_tensor(into, terms[:, :, 0], terms[:, :, 1], ADD)
-
-        def finish(into, both):
-            both = both.rearrange("p t g j -> p g t j")
-            nc.gpsimd.tensor_tensor(into, both[:, :, :, 0], both[:, :, :, 1], ADD)
 
         def reduce_into(lane, terms):
             with nc.allow_low_precision(reason="the sum is float32 inside the instruction and is rounded once"):
                 nc.vector.tensor_reduce(lane, terms, ALONG, ADD)
 
-        gather_and_turn(0, 0, 2)
-        gather_listed(0, 2, 4)
-        halve(0, 2, 4)
-        gather_and_turn(1, 0, 2)
-        for i in (SUMMED, REDUCED):
-            gather_listed(1, i, i + 1)
-            halve(1, i, i + 1)
-        finish(lanes[:, :, 0:2], first_halves[:])
-        gather_and_turn(2, 0, 2)
-        gather_listed(2, 2, 4)
-        halve(2, 2, 4)
-        gather_and_turn(3, EARLY, EARLY + 1)
-        gather_listed(3, SUMMED, SUMMED + 1)
-        halve(3, SUMMED, SUMMED + 1)
-        finish(lanes[:, :B, 2:4], last_halves[:].rearrange("p (t g) j -> p t g j", g=B)[:, 0:3:2])
-        gather_and_turn(3, LATE, LATE + 1)
-        gather_listed(3, REDUCED, REDUCED + 1, laid([P, B * K], BF16, "got_last", 3 * B * 8))
-        reduce_into(lanes[:, B:, 2], last_halves[:, B : 2 * B])
-        reduce_into(lanes[:, B:, 3], got[3, REDUCED].rearrange("p (g j) -> p g j", j=K))
+        first_halves = {i: laid([P, 2, B, 2], F32, f"first_halves{i}", (i - 2) * 2048) for i in PLACED}
+        for t in range(2):
+            gather_and_turn(t, EARLY, LATE + 1)
+            for i in PLACED:
+                halve(first_halves[i][:, t], gather_listed(t, i, i + 1))
+        for i in PLACED:
+            both = first_halves[i][:].rearrange("p t g j -> p g t j")
+            nc.gpsimd.tensor_tensor(lanes[:, i - 2, :, 0:2], both[:, :, :, 0], both[:, :, :, 1], ADD)
+        gather_and_turn(2, EARLY, LATE + 1)
+        third_halves = laid([P, 2, B, 2], F32, "third_halves", 1024)
+        halve(third_halves[:].rearrange("p c g j -> p (c g) j"), gather_listed(2, 2, 4))
+        w_tile = sbuf([P, M * 4], BF16, "w_bf", "got2_2")
+        nc.gpsimd.tensor_scalar(
+            w_tile[:].rearrange("p (c i t) -> p c t i", i=4, t=4),
+            w_raw[:].rearrange("p t (c i) -> p c t i", i=4),
+            1.0,
+            0.0,
+            MULT,
+            ADD,
+        )
+        last = {}
+        for i in (EARLY, LATE):
+            gather_and_turn(3, i, i + 1)
+            last[i + 2] = gather_listed(3, i + 2, i + 3, laid([P, B * K], BF16, f"got_last{i + 2}", i * 3072))
+        for i in PLACED:
+            reduce_into(lanes[:, i - 2, :, 3], last[i].rearrange("p (g j) -> p g j", j=K))
+        reduce_into(lanes[:, :, :, 2], third_halves[:])
 
-        def quantise(name, values, tag=None):
-            codes = sbuf([P, P], U32, f"{name}_codes", tag)[:].bitcast(FP8X4)
+        def quantise(name, values, codes=None):
+            codes = (codes or sbuf([P, P], U32, f"{name}_codes"))[:].bitcast(FP8X4)
             scales = sbuf([P, P], U8, f"{name}_scales")[:]
             nc.vector.quantize_mx(codes, scales, values)
             return codes, scales
@@ -141,18 +141,12 @@ def tile_attend_bag_kernel(tc, xT, w, offs, out):
                 nc.tensor.transpose(back[:, h, :], turned[i][:, h, :], ident[:])
             nc.scalar.copy(e[i].bitcast(F32).rearrange("p (g h) -> p g h", h=2), back[:].rearrange("p h g -> p g h"))
 
-        w_tile = sbuf([P, 2, 4 * P], BF16, "w_bf", f"got3_{SUMMED}")
-        w_bf = [w_tile[:, m] for m in range(2)]
-        for m in range(2):
-            nc.vector.tensor_copy(
-                w_bf[m].rearrange("p (c i t) -> p c t i", i=4, t=4),
-                w_raw[:, :, m * P : (m + 1) * P].rearrange("p t (c i) -> p c t i", i=4),
-            )
-        w_mx = [quantise(f"w{m}", w_bf[m]) for m in range(2)]
-        e_mx = {i: quantise(f"e{i}", e[i], "w_raw" if i == REDUCED else None) for i in (SUMMED, REDUCED, EARLY, LATE)}
+        w_mx = [quantise(f"w{m}", w_tile[:, m * 4 * P : (m + 1) * 4 * P]) for m in range(2)]
+        e_mx = {i: quantise(f"e{i}", e[i], laid([P, P], U32, f"e{i}_codes", 4096 + (i - 2) * 512)) for i in PLACED}
+        e_mx.update({i: quantise(f"e{i}", e[i]) for i in (EARLY, LATE)})
 
-        def product(i, tags, engines, stores, tag=None):
-            res = sbuf([P, 2, B], F32, f"res{i}", tag)
+        def product(i, tags, engines, stores):
+            res = sbuf([P, 2, B], F32, f"res{i}")
             accs = [psum.tile([P, 2 // len(tags), B], F32, name="acc", tag=tag) for tag in tags]
             for m in range(2):
                 nc.tensor.matmul_mx(
@@ -170,7 +164,7 @@ def tile_attend_bag_kernel(tc, xT, w, offs, out):
                 rows = slice(2 * n // stores, 2 * (n + 1) // stores)
                 nc.sync.dma_start(out_rows[:, rows, i * B : (i + 1) * B], res[:, rows])
 
-        product(SUMMED, ("bank2",), (on_scalar,), 1)
-        product(REDUCED, ("bank0",), (on_scalar,), 1)
+        product(2, ("bank2",), (on_scalar,), 1)
+        product(3, ("bank0",), (on_scalar,), 1)
         product(EARLY, ("bank3", "bank4"), (on_vector, on_scalar), 1)
         product(LATE, ("bank5", "bank6"), (on_vector, on_scalar), 1)

@@ -21,6 +21,7 @@ ALONG = mybir.AxisListType.X
 
 EARLY, LATE = 0, 1
 PLACED = (2, 3)
+SHARE = 16
 
 
 def tile_attend_bag_kernel(tc, xT, w, offs, out):
@@ -42,21 +43,24 @@ def tile_attend_bag_kernel(tc, xT, w, offs, out):
         planes = [sbuf([P, T], F32, f"plane{t}") for t in range(4)]
         w_raw = laid([P, 4, M], F32, "w_raw", 4096)
         H = T // 2
-        nc.scalar.dma_start(planes[0][:, :H], x_rows[:, 0, :H])
-        nc.sync.dma_start(planes[0][:, H:], x_rows[:, 0, H:])
+        Q = T // 4
+        nc.scalar.dma_start(planes[0][:, :Q], x_rows[:, 0, :Q])
         nc.sync.dma_start(offsets[:], offs)
-        nc.scalar.dma_start(planes[1][:, :H], x_rows[:, 1, :H])
-        nc.sync.dma_start(planes[1][:, H:], x_rows[:, 1, H:])
-        for t in (2, 3):
-            nc.sync.dma_start(planes[t][:], x_rows[:, t, :])
-        nc.sync.dma_start(w_raw[:], w.rearrange("(p t) m -> p t m", t=4))
+        nc.scalar.dma_start(planes[0][:, Q:H], x_rows[:, 0, Q:H])
+        nc.sync.dma_start(planes[0][:, H:], x_rows[:, 0, H:])
+        for t in (1, 2):
+            nc.scalar.dma_start(planes[t][:, :H], x_rows[:, t, :H])
+            nc.sync.dma_start(planes[t][:, H:], x_rows[:, t, H:])
+        nc.sync.dma_start(planes[3][:], x_rows[:, 3, :])
+        for t in (0, 2):
+            nc.sync.dma_start(w_raw[:, t : t + 2], w.rearrange("(p t) m -> p t m", t=4)[:, t : t + 2])
+
+        warm = sbuf([P, 16], F32, "warm")
+        nc.gpsimd.memset(warm[:, :8], 0.0)
+        nc.scalar.activation(warm[:, 8:], warm[:, :8], COPY)
 
         ident = sbuf([P, P], F32, "ident")
         make_identity(nc, ident[:])
-
-        warm = sbuf([P, 16], F32, "warm")
-        nc.vector.memset(warm[:, :8], 0.0)
-        nc.scalar.activation(warm[:, 8:], warm[:, :8], COPY)
 
         def listed(i0, i1):
             return offsets[:, i0 * B * K // 16 : i1 * B * K // 16]
@@ -68,18 +72,19 @@ def tile_attend_bag_kernel(tc, xT, w, offs, out):
         e.update({i: e_placed[:, i - 2] for i in PLACED})
         lanes = e_placed[:].rearrange("p c (g t) -> p c g t", t=4)
 
+        def add_turned(into, terms):
+            for j, term in enumerate(terms):
+                nc.tensor.matmul(into, lhsT=term, rhs=ident[:], is_transpose=True, start=j == 0, stop=j == K - 1)
+
         def gather_and_turn(t, i0, i1):
             dealt = sbuf([P, i1 - i0, K, B], F32, f"dealt{t}_{i0}")
             nc.vector.tensor_copy(dealt[:].rearrange("p c j g -> p c g j"), planes[t][:].indirect(listed(i0, i1)))
             for i in range(i0, i1):
                 into = early_bank[:, t, :] if i == EARLY else late_banks[t // 2][:, t % 2, :]
-                for j in range(K):
-                    nc.tensor.matmul(
-                        into, lhsT=dealt[:, i - i0, j, :], rhs=ident[:], is_transpose=True, start=j == 0, stop=j == K - 1
-                    )
+                add_turned(into, [dealt[:, i - i0, j, :] for j in range(K)])
 
         def gather_listed(t, i0, i1, into=None):
-            got = (into or sbuf([P, (i1 - i0) * B * K], BF16, f"got{t}_{i0}"))[:]
+            got = sbuf([P, (i1 - i0) * B * K], BF16, f"got{t}_{i0}")[:] if into is None else into
             nc.scalar.activation(got, planes[t][:].indirect(listed(i0, i1)), COPY)
             return got
 
@@ -87,63 +92,31 @@ def tile_attend_bag_kernel(tc, xT, w, offs, out):
             terms = got.rearrange("p (g s j) -> p g s j", s=2, j=2)
             nc.gpsimd.tensor_tensor(into, terms[:, :, 0], terms[:, :, 1], ADD)
 
+        def finish(into, both):
+            both = both.rearrange("p t (q i) j -> p q t i j", i=4)
+            into = into.rearrange("p (q i) t -> p q t i", i=4)
+            nc.gpsimd.tensor_tensor(into, both[:, :, :, :, 0], both[:, :, :, :, 1], ADD)
+
         def reduce_into(lane, terms):
             with nc.allow_low_precision(reason="the sum is float32 inside the instruction and is rounded once"):
                 nc.vector.tensor_reduce(lane, terms, ALONG, ADD)
 
-        first_halves = {i: laid([P, 2, B, 2], F32, f"first_halves{i}", (i - 2) * 2048) for i in PLACED}
-        for t in range(2):
-            gather_and_turn(t, EARLY, LATE + 1)
-            for i in PLACED:
-                halve(first_halves[i][:, t], gather_listed(t, i, i + 1))
-        for i in PLACED:
-            both = first_halves[i][:].rearrange("p t g j -> p g t j")
-            nc.gpsimd.tensor_tensor(lanes[:, i - 2, :, 0:2], both[:, :, :, 0], both[:, :, :, 1], ADD)
-        gather_and_turn(2, EARLY, LATE + 1)
-        third_halves = laid([P, 2, B, 2], F32, "third_halves", 1024)
-        halve(third_halves[:].rearrange("p c g j -> p (c g) j"), gather_listed(2, 2, 4))
-        w_tile = sbuf([P, M * 4], BF16, "w_bf", "got2_2")
-        nc.gpsimd.tensor_scalar(
-            w_tile[:].rearrange("p (c i t) -> p c t i", i=4, t=4),
-            w_raw[:].rearrange("p t (c i) -> p c t i", i=4),
-            1.0,
-            0.0,
-            MULT,
-            ADD,
-        )
-        last = {}
-        for i in (EARLY, LATE):
-            gather_and_turn(3, i, i + 1)
-            last[i + 2] = gather_listed(3, i + 2, i + 3, laid([P, B * K], BF16, f"got_last{i + 2}", i * 3072))
-        for i in PLACED:
-            reduce_into(lanes[:, i - 2, :, 3], last[i].rearrange("p (g j) -> p g j", j=K))
-        reduce_into(lanes[:, :, :, 2], third_halves[:])
+        def on_scalar(into, acc):
+            nc.scalar.activation(into, acc, COPY)
+
+        on_vector = nc.vector.tensor_copy
+
+        def round_sums(engine, into, sums):
+            engine(
+                into.bitcast(BF16).rearrange("g h (p s) -> g h p s", s=2),
+                sums.rearrange("g (h s) p -> g h p s", s=2),
+            )
 
         def quantise(name, values, codes=None):
             codes = (codes or sbuf([P, P], U32, f"{name}_codes"))[:].bitcast(FP8X4)
             scales = sbuf([P, P], U8, f"{name}_scales")[:]
             nc.vector.quantize_mx(codes, scales, values)
             return codes, scales
-
-        def on_scalar(into, acc):
-            nc.scalar.activation(into, acc, COPY)
-
-        on_vector = nc.vector.tensor_copy
-        turned = {i: sbuf([P, 2, P], F32, f"turned{i}", "dealt3_0" if i == LATE else None) for i in (EARLY, LATE)}
-        for into, sums in ((turned[EARLY][:], early_bank), (turned[LATE][:, :1], late_banks[0]), (turned[LATE][:, 1:], late_banks[1])):
-            on_scalar(
-                into.bitcast(BF16).rearrange("g h (p s) -> g h p s", s=2),
-                sums[:].rearrange("g (h s) p -> g h p s", s=2),
-            )
-        for i in (EARLY, LATE):
-            back = psum.tile([P, 2, B], F32, name="back", tag=f"bank{i}")
-            for h in range(2):
-                nc.tensor.transpose(back[:, h, :], turned[i][:, h, :], ident[:])
-            nc.scalar.copy(e[i].bitcast(F32).rearrange("p (g h) -> p g h", h=2), back[:].rearrange("p h g -> p g h"))
-
-        w_mx = [quantise(f"w{m}", w_tile[:, m * 4 * P : (m + 1) * 4 * P]) for m in range(2)]
-        e_mx = {i: quantise(f"e{i}", e[i], laid([P, P], U32, f"e{i}_codes", 4096 + (i - 2) * 512)) for i in PLACED}
-        e_mx.update({i: quantise(f"e{i}", e[i]) for i in (EARLY, LATE)})
 
         def product(i, tags, engines, stores):
             res = sbuf([P, 2, B], F32, f"res{i}")
@@ -164,7 +137,64 @@ def tile_attend_bag_kernel(tc, xT, w, offs, out):
                 rows = slice(2 * n // stores, 2 * (n + 1) // stores)
                 nc.sync.dma_start(out_rows[:, rows, i * B : (i + 1) * B], res[:, rows])
 
+        def cast_w(into):
+            nc.gpsimd.tensor_scalar(
+                into.rearrange("p (c i t) -> p c t i", i=4, t=4),
+                w_raw[:].rearrange("p t (c i) -> p c t i", i=4),
+                1.0,
+                0.0,
+                MULT,
+                ADD,
+            )
+
+        def turn_back(i, h0, h1):
+            for h in range(h0, h1):
+                nc.tensor.transpose(back[i][:, h, :], turned[i][:, h, :], ident[:])
+
+        def copy_back(i, engine=nc.scalar.copy):
+            engine(e[i].bitcast(F32).rearrange("p (g h) -> p g h", h=2), back[i][:].rearrange("p h g -> p g h"))
+
+        first_halves = {i: laid([P, 2, B, 2], F32, f"first_halves{i}", (i - 2) * 2048) for i in PLACED}
+        gather_and_turn(0, EARLY, LATE + 1)
+        got = gather_listed(0, 2, 4)
+        for i in PLACED:
+            halve(first_halves[i][:, 0], got[:, (i - 2) * B * K : (i - 1) * B * K])
+        gather_and_turn(1, EARLY, LATE + 1)
+        for i in PLACED:
+            halve(first_halves[i][:, 1], gather_listed(1, i, i + 1))
+        for i in PLACED:
+            finish(lanes[:, i - 2, :, 0:2], first_halves[i][:])
+        gather_and_turn(2, EARLY, LATE + 1)
+        third_halves = laid([P, 2, B, 2], F32, "third_halves", 1024)
+        halve(third_halves[:].rearrange("p c g j -> p (c g) j"), gather_listed(2, 2, 4))
+        w_bf = sbuf([P, M * 4], BF16, "w_bf", "got2_2")[:]
+        cast_w(w_bf)
+        shared = sbuf([P, B * K], F32, "shared")
+        cut = (B - SHARE) * K
+        entries = listed(EARLY, EARLY + 1)
+        nc.vector.tensor_copy(shared[:, :cut], planes[3][:].indirect(entries[:, : cut // 16]))
+        nc.scalar.activation(shared[:, cut:], planes[3][:].indirect(entries[:, cut // 16 :]), COPY)
+        add_turned(early_bank[:, 3, :], [shared[:, j::K] for j in range(K)])
+        gather_and_turn(3, LATE, LATE + 1)
+        last = {i: gather_listed(3, i, i + 1, laid([P, B * K], BF16, f"got_last{i}", (i - 2) * 3072)[:]) for i in PLACED}
+        turned = {i: sbuf([P, 2, P], F32, f"turned{i}", "shared" if i == LATE else None) for i in (EARLY, LATE)}
+        reduce_into(lanes[:, 0, :, 3], last[2].rearrange("p (g j) -> p g j", j=K))
+        reduce_into(lanes[:, :, :, 2], third_halves[:])
+        reduce_into(lanes[:, 1, :, 3], last[3].rearrange("p (g j) -> p g j", j=K))
+        round_sums(on_scalar, turned[EARLY][:], early_bank[:])
+        round_sums(on_scalar, turned[LATE][:, :1], late_banks[0][:])
+        round_sums(on_scalar, turned[LATE][:, 1:], late_banks[1][:])
+        back = {i: psum.tile([P, 2, B], F32, name="back", tag=f"bank{i}") for i in (EARLY, LATE)}
+        for i in (EARLY, LATE):
+            turn_back(i, 0, 2)
+            copy_back(i)
+        w_mx, e_mx = [], {}
+        for m, i in enumerate(PLACED):
+            w_mx.append(quantise(f"w{m}", w_bf[:, m * 4 * P : (m + 1) * 4 * P]))
+            e_mx[i] = quantise(f"e{i}", e[i], laid([P, P], U32, f"e{i}_codes", 4096 + m * 512))
+        for i in (EARLY, LATE):
+            e_mx[i] = quantise(f"e{i}", e[i], laid([P, P], U32, f"e{i}_codes", 5120 + i * 512))
         product(2, ("bank2",), (on_scalar,), 1)
         product(3, ("bank0",), (on_scalar,), 1)
         product(EARLY, ("bank3", "bank4"), (on_vector, on_scalar), 1)
-        product(LATE, ("bank5", "bank6"), (on_vector, on_scalar), 1)
+        product(LATE, ("bank5", "bank6"), (on_vector, on_scalar), 2)

@@ -19,9 +19,10 @@ MULT = mybir.AluOpType.mult
 COPY = mybir.ActivationFunctionType.Copy
 ALONG = mybir.AxisListType.X
 
-EARLY, LATE = 0, 1
-PLACED = (2, 3)
-SHARE = 16
+PLACED = MIXED, ADDED = 0, 1
+EARLY, LATE = 2, 3
+HELD = 64
+WALK = 4
 
 
 def tile_attend_bag_kernel(tc, xT, w, offs, out):
@@ -39,9 +40,12 @@ def tile_attend_bag_kernel(tc, xT, w, offs, out):
         def laid(shape, dtype, name, offset):
             return reused.tile(shape, dtype, name=name, offset=offset, align_bytes=256)
 
+        def bank(shape, name, n):
+            return psum.tile(shape, F32, name=name, tag=f"bank{n}")
+
         offsets = sbuf([P, G * K // 16], U16, "offsets")
         planes = [sbuf([P, T], F32, f"plane{t}") for t in range(4)]
-        w_raw = laid([P, 4, M], F32, "w_raw", 4096)
+        w_raw = laid([P, 4, M], F32, "w_raw", 0)
         H = T // 2
         Q = T // 4
         nc.scalar.dma_start(planes[0][:, :Q], x_rows[:, 0, :Q])
@@ -65,136 +69,143 @@ def tile_attend_bag_kernel(tc, xT, w, offs, out):
         def listed(i0, i1):
             return offsets[:, i0 * B * K // 16 : i1 * B * K // 16]
 
-        early_bank = psum.tile([P, 4, P], F32, name="fwd", tag="bank0")
-        late_banks = [psum.tile([P, 2, P], F32, name="fwd", tag=f"bank{1 + h}") for h in range(2)]
+        early_bank = bank([P, 4, P], "fwd", 0)
+        late_banks = [bank([P, 2, P], "fwd", 1 + h) for h in range(2)]
         e_placed = sbuf([P, 2, 4 * B], BF16, "e_placed")
-        e = {i: sbuf([P, 4 * B], BF16, f"e{i}")[:] for i in (EARLY, LATE)}
-        e.update({i: e_placed[:, i - 2] for i in PLACED})
         lanes = e_placed[:].rearrange("p c (g t) -> p c g t", t=4)
-
-        def add_turned(into, terms):
-            for j, term in enumerate(terms):
-                nc.tensor.matmul(into, lhsT=term, rhs=ident[:], is_transpose=True, start=j == 0, stop=j == K - 1)
+        shared = sbuf([P, 5 * 2 * B], F32, "shared")
+        places = [shared[:, n * 2 * B : (n + 1) * 2 * B] for n in range(3)]
+        start = 2 * B - HELD // 2
+        parts = [shared[:, start + n * 2 * B : start + (n + 1) * 2 * B] for n in range(4)]
+        e = {i: e_placed[:, i] for i in PLACED}
+        e.update({i: sbuf([P, 4 * B], BF16, f"e{i}")[:] for i in (EARLY, LATE)})
 
         def gather_and_turn(t, i0, i1):
             dealt = sbuf([P, i1 - i0, K, B], F32, f"dealt{t}_{i0}")
             nc.vector.tensor_copy(dealt[:].rearrange("p c j g -> p c g j"), planes[t][:].indirect(listed(i0, i1)))
             for i in range(i0, i1):
                 into = early_bank[:, t, :] if i == EARLY else late_banks[t // 2][:, t % 2, :]
-                add_turned(into, [dealt[:, i - i0, j, :] for j in range(K)])
+                for j in range(K):
+                    nc.tensor.matmul(
+                        into, lhsT=dealt[:, i - i0, j, :], rhs=ident[:], is_transpose=True, start=j == 0, stop=j == K - 1
+                    )
 
-        def gather_listed(t, i0, i1, into=None):
-            got = sbuf([P, (i1 - i0) * B * K], BF16, f"got{t}_{i0}")[:] if into is None else into
-            nc.scalar.activation(got, planes[t][:].indirect(listed(i0, i1)), COPY)
-            return got
+        def gather_listed(t, entries, into):
+            nc.scalar.activation(into, planes[t][:].indirect(entries), COPY)
+            return into
+
+        def fresh(t, i):
+            return gather_listed(t, listed(i, i + 1), sbuf([P, B * K], BF16, f"got{t}_{i}")[:])
 
         def halve(into, got):
             terms = got.rearrange("p (g s j) -> p g s j", s=2, j=2)
-            nc.gpsimd.tensor_tensor(into, terms[:, :, 0], terms[:, :, 1], ADD)
+            nc.gpsimd.tensor_tensor(into.rearrange("p (g j) -> p g j", j=2), terms[:, :, 0], terms[:, :, 1], ADD)
 
-        def finish(into, both):
-            both = both.rearrange("p t (q i) j -> p q t i j", i=4)
-            into = into.rearrange("p (q i) t -> p q t i", i=4)
-            nc.gpsimd.tensor_tensor(into, both[:, :, :, :, 0], both[:, :, :, :, 1], ADD)
+        def finish(into, halves):
+            both = halves.rearrange("p (t g j) -> p g t j", g=B, j=2)
+            nc.gpsimd.tensor_tensor(into, both[:, :, :, 0], both[:, :, :, 1], ADD)
 
         def reduce_into(lane, terms):
             with nc.allow_low_precision(reason="the sum is float32 inside the instruction and is rounded once"):
                 nc.vector.tensor_reduce(lane, terms, ALONG, ADD)
 
-        def on_scalar(into, acc):
-            nc.scalar.activation(into, acc, COPY)
-
-        on_vector = nc.vector.tensor_copy
-
-        def round_sums(engine, into, sums):
-            engine(
+        def round_sums(into, sums):
+            nc.scalar.copy(
                 into.bitcast(BF16).rearrange("g h (p s) -> g h p s", s=2),
                 sums.rearrange("g (h s) p -> g h p s", s=2),
             )
 
-        def quantise(name, values, codes=None):
-            codes = (codes or sbuf([P, P], U32, f"{name}_codes"))[:].bitcast(FP8X4)
-            scales = sbuf([P, P], U8, f"{name}_scales")[:]
-            nc.vector.quantize_mx(codes, scales, values)
-            return codes, scales
+        def turn_back(i, turned):
+            back = bank([P, 2, B], "back", i - EARLY)
+            for h in range(2):
+                nc.tensor.transpose(back[:, h, :], turned[:, h, :], ident[:])
+            return back
 
-        def product(i, tags, engines, stores):
-            res = sbuf([P, 2, B], F32, f"res{i}")
-            accs = [psum.tile([P, 2 // len(tags), B], F32, name="acc", tag=tag) for tag in tags]
-            for m in range(2):
-                nc.tensor.matmul_mx(
-                    accs[m * len(tags) // 2][:, m % (2 // len(tags))],
-                    lhsT=w_mx[m][0],
-                    lhsT_scale=w_mx[m][1],
-                    rhs=e_mx[i][0],
-                    rhs_scale=e_mx[i][1],
-                    start=True,
-                    stop=True,
-                )
-            for n, engine in enumerate(engines):
-                engine(res[:, n : n + 2 // len(tags)], accs[n][:])
-            for n in range(stores):
-                rows = slice(2 * n // stores, 2 * (n + 1) // stores)
-                nc.sync.dma_start(out_rows[:, rows, i * B : (i + 1) * B], res[:, rows])
+        def copy_back(i, back):
+            nc.scalar.copy(e[i].bitcast(F32).rearrange("p (g h) -> p g h", h=2), back[:].rearrange("p h g -> p g h"))
 
-        def cast_w(into):
-            nc.gpsimd.tensor_scalar(
-                into.rearrange("p (c i t) -> p c t i", i=4, t=4),
-                w_raw[:].rearrange("p t (c i) -> p c t i", i=4),
-                1.0,
-                0.0,
-                MULT,
-                ADD,
+        def operand(name, width, codes=None):
+            codes = codes or sbuf([P, width], U32, f"{name}_codes")
+            return codes[:].bitcast(FP8X4), sbuf([P, width], U8, f"{name}_scales")[:]
+
+        def quantise(into, at, values):
+            nc.vector.quantize_mx(into[0][:, at : at + B], into[1][:, at : at + B], values)
+
+        def multiply(into, m, i):
+            nc.tensor.matmul_mx(
+                into,
+                lhsT=w_mx[0][:, m * P : (m + 1) * P],
+                lhsT_scale=w_mx[1][:, m * P : (m + 1) * P],
+                rhs=e_mx[i][0],
+                rhs_scale=e_mx[i][1],
+                start=True,
+                stop=True,
             )
 
-        def turn_back(i, h0, h1):
-            for h in range(h0, h1):
-                nc.tensor.transpose(back[i][:, h, :], turned[i][:, h, :], ident[:])
-
-        def copy_back(i, engine=nc.scalar.copy):
-            engine(e[i].bitcast(F32).rearrange("p (g h) -> p g h", h=2), back[i][:].rearrange("p h g -> p g h"))
-
-        first_halves = {i: laid([P, 2, B, 2], F32, f"first_halves{i}", (i - 2) * 2048) for i in PLACED}
         gather_and_turn(0, EARLY, LATE + 1)
-        got = gather_listed(0, 2, 4)
-        for i in PLACED:
-            halve(first_halves[i][:, 0], got[:, (i - 2) * B * K : (i - 1) * B * K])
+        first_halves = sbuf([P, 2 * B], F32, "first_halves")[:]
+        halve(first_halves, fresh(0, ADDED))
+        finish(lanes[:, ADDED, :, 0:1], first_halves)
+        halve(parts[0], fresh(0, MIXED))
         gather_and_turn(1, EARLY, LATE + 1)
-        for i in PLACED:
-            halve(first_halves[i][:, 1], gather_listed(1, i, i + 1))
-        for i in PLACED:
-            finish(lanes[:, i - 2, :, 0:2], first_halves[i][:])
+        halve(parts[1], fresh(1, MIXED))
+        halve(parts[2], gather_listed(1, listed(ADDED, ADDED + 1), parts[3].bitcast(BF16)))
+        finish(lanes[:, MIXED, :, 0:2], shared[:, start : start + 4 * B])
         gather_and_turn(2, EARLY, LATE + 1)
-        third_halves = laid([P, 2, B, 2], F32, "third_halves", 1024)
-        halve(third_halves[:].rearrange("p c g j -> p (c g) j"), gather_listed(2, 2, 4))
-        w_bf = sbuf([P, M * 4], BF16, "w_bf", "got2_2")[:]
-        cast_w(w_bf)
-        shared = sbuf([P, B * K], F32, "shared")
-        cut = (B - SHARE) * K
-        entries = listed(EARLY, EARLY + 1)
-        nc.vector.tensor_copy(shared[:, :cut], planes[3][:].indirect(entries[:, : cut // 16]))
-        nc.scalar.activation(shared[:, cut:], planes[3][:].indirect(entries[:, cut // 16 :]), COPY)
-        add_turned(early_bank[:, 3, :], [shared[:, j::K] for j in range(K)])
-        gather_and_turn(3, LATE, LATE + 1)
-        last = {i: gather_listed(3, i, i + 1, laid([P, B * K], BF16, f"got_last{i}", (i - 2) * 3072)[:]) for i in PLACED}
-        turned = {i: sbuf([P, 2, P], F32, f"turned{i}", "shared" if i == LATE else None) for i in (EARLY, LATE)}
-        reduce_into(lanes[:, 0, :, 3], last[2].rearrange("p (g j) -> p g j", j=K))
-        reduce_into(lanes[:, :, :, 2], third_halves[:])
-        reduce_into(lanes[:, 1, :, 3], last[3].rearrange("p (g j) -> p g j", j=K))
-        round_sums(on_scalar, turned[EARLY][:], early_bank[:])
-        round_sums(on_scalar, turned[LATE][:, :1], late_banks[0][:])
-        round_sums(on_scalar, turned[LATE][:, 1:], late_banks[1][:])
-        back = {i: psum.tile([P, 2, B], F32, name="back", tag=f"bank{i}") for i in (EARLY, LATE)}
+        halve(parts[3], fresh(2, ADDED))
+        third_halves = places[0]
+        halve(third_halves, fresh(2, MIXED))
+        finish(lanes[:, ADDED, :, 1:3], shared[:, start + 4 * B : start + 8 * B])
+        w_bf = sbuf([P, M * 4], BF16, "w_bf", f"got2_{MIXED}")[:]
+        nc.gpsimd.tensor_scalar(
+            w_bf.rearrange("p (c i t) -> p c t i", i=WALK, t=4),
+            w_raw[:].rearrange("p t (c i) -> p c t i", i=WALK),
+            1.0,
+            0.0,
+            MULT,
+            ADD,
+        )
         for i in (EARLY, LATE):
-            turn_back(i, 0, 2)
-            copy_back(i)
-        w_mx, e_mx = [], {}
-        for m, i in enumerate(PLACED):
-            w_mx.append(quantise(f"w{m}", w_bf[:, m * 4 * P : (m + 1) * 4 * P]))
-            e_mx[i] = quantise(f"e{i}", e[i], laid([P, P], U32, f"e{i}_codes", 4096 + m * 512))
+            gather_and_turn(3, i, i + 1)
+        got = gather_listed(3, listed(MIXED, MIXED + 1), places[1].bitcast(BF16))
+        reduce_into(lanes[:, MIXED, :, 3], got.rearrange("p (g j) -> p g j", j=K))
+        reduce_into(lanes[:, MIXED, :, 2], third_halves.rearrange("p (g j) -> p g j", j=2))
+        got = places[2].bitcast(BF16)
+        cut = B * K - HELD
+        entries = listed(ADDED, ADDED + 1)
+        gather_listed(3, entries[:, : cut // 16], got[:, :cut])
+        gather_listed(3, entries[:, cut // 16 :], got[:, cut:])
+        reduce_into(lanes[:, ADDED, :, 3], got.rearrange("p (g j) -> p g j", j=K))
+        turned = {
+            EARLY: sbuf([P, 2, P], F32, "turned_early")[:],
+            LATE: sbuf([P, 2, P], F32, "turned_late", f"dealt3_{EARLY}")[:],
+        }
+        round_sums(turned[EARLY], early_bank[:])
+        for h in range(2):
+            round_sums(turned[LATE][:, h : h + 1], late_banks[h][:])
+        backs = {i: turn_back(i, turned[i]) for i in (EARLY, LATE)}
         for i in (EARLY, LATE):
-            e_mx[i] = quantise(f"e{i}", e[i], laid([P, P], U32, f"e{i}_codes", 5120 + i * 512))
-        product(2, ("bank2",), (on_scalar,), 1)
-        product(3, ("bank0",), (on_scalar,), 1)
-        product(EARLY, ("bank3", "bank4"), (on_vector, on_scalar), 1)
-        product(LATE, ("bank5", "bank6"), (on_vector, on_scalar), 2)
+            copy_back(i, backs[i])
+        w_mx = operand("w", M)
+        e_mx = {i: operand(f"e{i}", B, laid([P, B], U32, f"e{i}_codes", 512 * i)) for i in range(4)}
+        quantise(w_mx, 0, w_bf[:, : 4 * P])
+        for i in PLACED:
+            quantise(e_mx[i], 0, e[i])
+        quantise(w_mx, P, w_bf[:, 4 * P :])
+        for i in (EARLY, LATE):
+            quantise(e_mx[i], 0, e[i])
+        pair = sbuf([P, 2, 2, B], F32, "pair")
+        for m, n in enumerate((2, 0)):
+            acc = bank([P, 2, B], "acc", n)
+            for i in PLACED:
+                multiply(acc[:, i], m, i)
+            nc.scalar.copy(pair[:, m], acc[:])
+            nc.sync.dma_start(out_rows[:, m, : 2 * B], pair[:, m].rearrange("p c g -> p (c g)"))
+        for i in (EARLY, LATE):
+            res = sbuf([P, 2, B], F32, f"res{i}")
+            for m, engine in enumerate((nc.vector.tensor_copy, nc.scalar.copy)):
+                acc = bank([P, B], "acc", 2 * i + m - 1)
+                multiply(acc[:], m, i)
+                engine(res[:, m], acc[:])
+            for rows in (slice(0, 2),) if i == EARLY else (slice(0, 1), slice(1, 2)):
+                nc.sync.dma_start(out_rows[:, rows, i * B : (i + 1) * B], res[:, rows])

from contextlib import ExitStack

import concourse.mybir as mybir
from concourse.masks import make_identity

D, T, G, K, M = 512, 2048, 512, 4, 256
P = 128
B = 128
FLOPS = 2 * D * G * M

F32 = mybir.dt.float32
BF16 = mybir.dt.bfloat16
U32 = mybir.dt.uint32
U16 = mybir.dt.uint16
U8 = mybir.dt.uint8
FP8X4 = mybir.dt.float8_e4m3fn_x4
ADD = mybir.AluOpType.add
MULT = mybir.AluOpType.mult
COPY = mybir.ActivationFunctionType.Copy
ALONG = mybir.AxisListType.X

PLACED = MIXED, ADDED = 0, 1
EARLY, LATE = 2, 3
HELD = 64
WALK = 4


def tile_attend_bag_kernel(tc, xT, w, offs, out):
    nc = tc.nc
    x_rows = xT.rearrange("(p t) c -> p t c", t=4)
    out_rows = out.rearrange("(m p) g -> p m g", m=2)
    with ExitStack() as ctx:
        keep = ctx.enter_context(tc.tile_pool(name="keep", bufs=1))
        reused = ctx.enter_context(tc.tile_pool(name="reused", bufs=1))
        psum = ctx.enter_context(tc.psum_pool(name="psum", bufs=1))

        def sbuf(shape, dtype, name, tag=None):
            return keep.tile(shape, dtype, name=name, tag=tag or name, align_bytes=256)

        def laid(shape, dtype, name, offset):
            return reused.tile(shape, dtype, name=name, offset=offset, align_bytes=256)

        def bank(shape, name, n):
            return psum.tile(shape, F32, name=name, tag=f"bank{n}")

        offsets = sbuf([P, G * K // 16], U16, "offsets")
        planes = [sbuf([P, T], F32, f"plane{t}") for t in range(4)]
        w_raw = laid([P, 4, M], F32, "w_raw", 0)
        H = T // 2
        Q = T // 4
        nc.scalar.dma_start(planes[0][:, :Q], x_rows[:, 0, :Q])
        nc.sync.dma_start(offsets[:], offs)
        nc.scalar.dma_start(planes[0][:, Q:H], x_rows[:, 0, Q:H])
        nc.sync.dma_start(planes[0][:, H:], x_rows[:, 0, H:])
        for t in (1, 2):
            nc.scalar.dma_start(planes[t][:, :H], x_rows[:, t, :H])
            nc.sync.dma_start(planes[t][:, H:], x_rows[:, t, H:])
        nc.sync.dma_start(planes[3][:], x_rows[:, 3, :])
        for t in (0, 2):
            nc.sync.dma_start(w_raw[:, t : t + 2], w.rearrange("(p t) m -> p t m", t=4)[:, t : t + 2])

        warm = sbuf([P, 16], F32, "warm")
        nc.gpsimd.memset(warm[:, :8], 0.0)
        nc.scalar.activation(warm[:, 8:], warm[:, :8], COPY)

        ident = sbuf([P, P], F32, "ident")
        make_identity(nc, ident[:])

        def listed(i0, i1):
            return offsets[:, i0 * B * K // 16 : i1 * B * K // 16]

        early_bank = bank([P, 4, P], "fwd", 0)
        late_banks = [bank([P, 2, P], "fwd", 1 + h) for h in range(2)]
        e_placed = sbuf([P, 2, 4 * B], BF16, "e_placed")
        lanes = e_placed[:].rearrange("p c (g t) -> p c g t", t=4)
        shared = sbuf([P, 5 * 2 * B], F32, "shared")
        places = [shared[:, n * 2 * B : (n + 1) * 2 * B] for n in range(3)]
        start = 2 * B - HELD // 2
        parts = [shared[:, start + n * 2 * B : start + (n + 1) * 2 * B] for n in range(4)]
        e = {i: e_placed[:, i] for i in PLACED}
        e.update({i: sbuf([P, 4 * B], BF16, f"e{i}")[:] for i in (EARLY, LATE)})

        def gather_and_turn(t, i0, i1):
            dealt = sbuf([P, i1 - i0, K, B], F32, f"dealt{t}_{i0}")
            nc.vector.tensor_copy(dealt[:].rearrange("p c j g -> p c g j"), planes[t][:].indirect(listed(i0, i1)))
            for i in range(i0, i1):
                into = early_bank[:, t, :] if i == EARLY else late_banks[t // 2][:, t % 2, :]
                for j in range(K):
                    nc.tensor.matmul(
                        into, lhsT=dealt[:, i - i0, j, :], rhs=ident[:], is_transpose=True, start=j == 0, stop=j == K - 1
                    )

        def gather_listed(t, entries, into):
            nc.scalar.activation(into, planes[t][:].indirect(entries), COPY)
            return into

        def fresh(t, i):
            return gather_listed(t, listed(i, i + 1), sbuf([P, B * K], BF16, f"got{t}_{i}")[:])

        def halve(into, got):
            terms = got.rearrange("p (g s j) -> p g s j", s=2, j=2)
            nc.gpsimd.tensor_tensor(into.rearrange("p (g j) -> p g j", j=2), terms[:, :, 0], terms[:, :, 1], ADD)

        def finish(into, halves):
            both = halves.rearrange("p (t g j) -> p g t j", g=B, j=2)
            nc.gpsimd.tensor_tensor(into, both[:, :, :, 0], both[:, :, :, 1], ADD)

        def reduce_into(lane, terms):
            with nc.allow_low_precision(reason="the sum is float32 inside the instruction and is rounded once"):
                nc.vector.tensor_reduce(lane, terms, ALONG, ADD)

        def round_sums(into, sums):
            nc.scalar.copy(
                into.bitcast(BF16).rearrange("g h (p s) -> g h p s", s=2),
                sums.rearrange("g (h s) p -> g h p s", s=2),
            )

        def turn_back(i, turned):
            back = bank([P, 2, B], "back", i - EARLY)
            for h in range(2):
                nc.tensor.transpose(back[:, h, :], turned[:, h, :], ident[:])
            return back

        def copy_back(i, back):
            nc.scalar.copy(e[i].bitcast(F32).rearrange("p (g h) -> p g h", h=2), back[:].rearrange("p h g -> p g h"))

        def operand(name, width, codes=None):
            codes = codes or sbuf([P, width], U32, f"{name}_codes")
            return codes[:].bitcast(FP8X4), sbuf([P, width], U8, f"{name}_scales")[:]

        def quantise(into, at, values):
            nc.vector.quantize_mx(into[0][:, at : at + B], into[1][:, at : at + B], values)

        def multiply(into, m, i):
            nc.tensor.matmul_mx(
                into,
                lhsT=w_mx[0][:, m * P : (m + 1) * P],
                lhsT_scale=w_mx[1][:, m * P : (m + 1) * P],
                rhs=e_mx[i][0],
                rhs_scale=e_mx[i][1],
                start=True,
                stop=True,
            )

        gather_and_turn(0, EARLY, LATE + 1)
        first_halves = sbuf([P, 2 * B], F32, "first_halves")[:]
        halve(first_halves, fresh(0, ADDED))
        finish(lanes[:, ADDED, :, 0:1], first_halves)
        halve(parts[0], fresh(0, MIXED))
        gather_and_turn(1, EARLY, LATE + 1)
        halve(parts[1], fresh(1, MIXED))
        halve(parts[2], gather_listed(1, listed(ADDED, ADDED + 1), parts[3].bitcast(BF16)))
        finish(lanes[:, MIXED, :, 0:2], shared[:, start : start + 4 * B])
        gather_and_turn(2, EARLY, LATE + 1)
        halve(parts[3], fresh(2, ADDED))
        third_halves = places[0]
        halve(third_halves, fresh(2, MIXED))
        finish(lanes[:, ADDED, :, 1:3], shared[:, start + 4 * B : start + 8 * B])
        w_bf = sbuf([P, M * 4], BF16, "w_bf", f"got2_{MIXED}")[:]
        nc.gpsimd.tensor_scalar(
            w_bf.rearrange("p (c i t) -> p c t i", i=WALK, t=4),
            w_raw[:].rearrange("p t (c i) -> p c t i", i=WALK),
            1.0,
            0.0,
            MULT,
            ADD,
        )
        for i in (EARLY, LATE):
            gather_and_turn(3, i, i + 1)
        got = gather_listed(3, listed(MIXED, MIXED + 1), places[1].bitcast(BF16))
        reduce_into(lanes[:, MIXED, :, 3], got.rearrange("p (g j) -> p g j", j=K))
        reduce_into(lanes[:, MIXED, :, 2], third_halves.rearrange("p (g j) -> p g j", j=2))
        got = places[2].bitcast(BF16)
        cut = B * K - HELD
        entries = listed(ADDED, ADDED + 1)
        gather_listed(3, entries[:, : cut // 16], got[:, :cut])
        gather_listed(3, entries[:, cut // 16 :], got[:, cut:])
        reduce_into(lanes[:, ADDED, :, 3], got.rearrange("p (g j) -> p g j", j=K))
        turned = {
            EARLY: sbuf([P, 2, P], F32, "turned_early")[:],
            LATE: sbuf([P, 2, P], F32, "turned_late", f"dealt3_{EARLY}")[:],
        }
        round_sums(turned[EARLY], early_bank[:])
        for h in range(2):
            round_sums(turned[LATE][:, h : h + 1], late_banks[h][:])
        backs = {i: turn_back(i, turned[i]) for i in (EARLY, LATE)}
        for i in (EARLY, LATE):
            copy_back(i, backs[i])
        w_mx = operand("w", M)
        e_mx = {i: operand(f"e{i}", B, laid([P, B], U32, f"e{i}_codes", 512 * i)) for i in range(4)}
        quantise(w_mx, 0, w_bf[:, : 4 * P])
        for i in PLACED:
            quantise(e_mx[i], 0, e[i])
        quantise(w_mx, P, w_bf[:, 4 * P :])
        for i in (EARLY, LATE):
            quantise(e_mx[i], 0, e[i])
        pair = sbuf([P, 2, 2, B], F32, "pair")
        for m, n in enumerate((2, 0)):
            acc = bank([P, 2, B], "acc", n)
            for i in PLACED:
                multiply(acc[:, i], m, i)
            nc.scalar.copy(pair[:, m], acc[:])
            nc.sync.dma_start(out_rows[:, m, : 2 * B], pair[:, m].rearrange("p c g -> p (c g)"))
        for i in (EARLY, LATE):
            res = sbuf([P, 2, B], F32, f"res{i}")
            for m, engine in enumerate((nc.vector.tensor_copy, nc.scalar.copy)):
                acc = bank([P, B], "acc", 2 * i + m - 1)
                multiply(acc[:], m, i)
                engine(res[:, m], acc[:])
            for rows in (slice(0, 2),) if i == EARLY else (slice(0, 1), slice(1, 2)):
                nc.sync.dma_start(out_rows[:, rows, i * B : (i + 1) * B], res[:, rows])
